import numpy as np, ml_dtypes
CORES = [24,25,26,27,28,29,30,31]
N = 8
BF = ml_dtypes.bfloat16
L, C, S, F, T, RB = 256, 3072, 2560, 1536, 5, 32
R16 = np.arange(16)[:, None]
def alphabet(rng, A):
    near = rng.integers(0, 256 - A, (8, 16, 1)) + np.arange(A)
    return np.where(rng.random((8, 16, 1)) < 0.5, near, rng.integers(0, 255, (8, 16, A)))
def values(rng, al, n, skew):
    A = al.shape[-1]; ix = np.minimum((A * rng.random((N, 8, 16, n)) ** skew).astype(np.int64), A - 1)
    return np.take_along_axis(np.broadcast_to(al, (N, 8, 16, A)), ix, 3)
def base(rng, A, skew, sizes):
    al = alphabet(rng, A); m = values(rng, al, F, skew); v = values(rng, al, C, skew)
    share = 0.0625 * rng.choice(np.array(sizes), (N, 8, 1, C))
    pt = np.where(rng.random((N, 8, 16, C)) < share, v, 255)
    return rng.integers(0, C, (N, 8, 16, S)), pt, rng.integers(0, C, (N, 8, C)), rng.integers(0, S, (N, 8, C)), m
def keyed(rng):
    h = C // 2; kr = rng.permutation(16)[:8]; b0 = rng.integers(0, 230, 8)
    pt = np.full((N, 8, 16, C), 255); v = rng.integers(0, 255, (N, 8, 16, C - h)); pt[..., h:] = np.where(rng.random(v.shape) < 0.6, v, 255)
    m = rng.integers(0, 255, (N, 8, 16, F))
    for g in range(8):
        pt[:, g, kr[g], :h] = b0[g] + np.arange(h) % 16
        pt[:, g, kr[g], h:] = np.where(rng.random((N, C - h)) < 0.8, b0[g] + np.arange(h, C) % 20, 255)
        m[:, g, kr[g]] = b0[g] + np.arange(F) % 20
    cl = 16 * rng.integers(0, h // 16, (N, 8, 16, S)) + R16
    return cl, pt, rng.integers(h, C, (N, 8, C)), rng.integers(0, S, (N, 8, C)), m
def message(rng, key):
    return key + 20 * rng.integers(0, F // 20, key.shape)
def edge(rng, lo, hi, shape, share):
    return np.where(rng.random(shape) < share, np.where(rng.random(shape) < 0.5, lo, hi), rng.integers(lo, hi + 1, shape))
def boxes(n, ids):
    return np.where(R16 < n[:, :, None, :], ids, 0)
def pack(cl, pt, bo, gs, m, q, n, p, s, w):
    i4 = lambda a: np.ascontiguousarray(a).astype(np.int32)
    bf = lambda a: np.ascontiguousarray(a.reshape(N, 128, -1)).astype(np.float32).astype(BF)
    return {"cl": i4(cl.reshape(N, 128, S)), "pt": bf(pt), "bo": i4(bo), "gs": i4(gs), "m0": bf(m), "q0": i4(q.reshape(N, 128, L)), "n0": i4(n), "p0": i4(p), "s0": i4(s), "w0": i4(w)}
def setup_inputs(rng):
    cl, pt, bo, gs, m = base(rng, 3, 1, [3, 3, 4, 4, 5, 6, 16])
    n = rng.choice(np.array([0, 1, 1, 2, 2, 3, 4, 6, 10, 15, 16, 16]), (N, 8, L))
    p = np.where(rng.random(n.shape) < 0.7, 0, (rng.random(n.shape) * (n + 1)).astype(np.int64)); p = np.minimum(p, n)
    w = np.where(rng.random(n.shape) < 0.6, 0, rng.integers(0, RB + 16, n.shape))
    return pack(cl, pt, bo, gs, m, boxes(n, rng.integers(0, F, (N, 8, 16, L))), n, p, rng.integers(0, S, n.shape), w)
def setup_inputs_spread(rng):
    cl, pt, bo, gs, m = base(rng, 16, 3, [2, 2, 3, 3, 4, 6, 16])
    cl = (C * rng.random(cl.shape) ** 2).astype(np.int64); bo = (C * rng.random(bo.shape) ** 3).astype(np.int64); gs = (S * rng.random(gs.shape) ** 2).astype(np.int64)
    n = np.minimum((17 * rng.random((N, 8, L)) ** 2).astype(np.int64), 16); p = np.minimum((rng.random(n.shape) * (n + 1)).astype(np.int64), n)
    s = np.minimum((S * rng.random(n.shape) ** 4).astype(np.int64), S - 1); w = rng.integers(0, RB + 16, n.shape)
    ids = (F * rng.random((N, 8, 16, L)) ** 2).astype(np.int64)
    return pack(np.minimum(cl, C - 1), pt, np.minimum(bo, C - 1), np.minimum(gs, S - 1), m, boxes(n, np.minimum(ids, F - 1)), n, p, s, w)
def setup_inputs_ends(rng):
    cl = edge(rng, 0, C - 1, (N, 8, 16, S), 0.7); bo = edge(rng, 0, C - 1, (N, 8, C), 0.7); gs = edge(rng, 0, S - 1, (N, 8, C), 0.7); m = edge(rng, 0, 254, (N, 8, 16, F), 0.9)
    v = rng.choice(np.array([0.3, 0.5, 0.6, 0.7, 0.8]), (N, 8, 1, C)); shape = (N, 8, 16, C)
    pt = np.where(rng.random(shape) < v, 255, np.where(rng.random(shape) < 0.5, 0, 254)); pt = np.where(rng.random(shape) < 0.04, rng.integers(0, 256, shape), pt)
    rr = np.array([0, 7, 15]); e0 = rng.choice(np.array([0, 254]), (8, 3)); e1 = rng.choice(np.array([0, 254]), (8, 3)); e1[:, 0] = 254 - e0[:, 0]
    pt[..., 0] = 255; pt[..., C - 1] = 255
    for g in range(8):
        pt[:, g, rr, 0] = e0[g]; pt[:, g, rr, C - 1] = e1[g]
    m[:, 7, rr, 0] = e0[7]; m[:, 7, rr, F - 1] = e1[7]
    cl[:, 7, :, 0] = C - 1; cl[:, 7, :15, S - 1] = 0; cl[:, 7, 15, S - 1] = C - 1; gs[:, 7, C - 1] = S - 1; bo[:, 7, C - 1] = C - 1
    shape = (N, 8, L)
    n = np.where(rng.random(shape) < 0.8, rng.choice(np.array([0, 16, 16]), shape), rng.choice(np.array([1, 2, 15]), shape))
    p = np.where(rng.random(shape) < 0.8, np.where(rng.random(shape) < 0.7, 0, n), np.maximum(n - 1, 0))
    s = edge(rng, 0, S - 1, shape, 0.7)
    w = np.where(rng.random(shape) < 0.75, np.where(rng.random(shape) < 0.6, 0, RB + 15), rng.choice(np.array([RB - 2, RB - 1, RB - 1, RB]), shape))
    ids = edge(rng, 0, F - 1, (N, 8, 16, L), 0.7)
    a = np.array([0, 1, L // 2, L - 2, L - 1]); b = np.array([2, 3, L - 3])
    for z, st, x in ((a, S - 1, F - 1), (b, 0, 0)):
        s[:, 7, z] = st; n[:, 7, z] = 16; p[:, 7, z] = 15; w[:, 7, z] = RB - 1; ids[:, 7, 15, z] = x
    return pack(cl, pt, bo, gs, m, boxes(n, ids), n, p, s, w)
def setup_inputs_corners(rng):
    cl, pt, bo, gs, m = base(rng, 3, 1, [3, 3, 4, 4, 5, 6, 16])
    n = rng.choice(np.array([0, 1, 15, 16]), (N, 8, L)); p = np.choose(rng.integers(0, 3, n.shape), [0 * n, n, np.maximum(n - 1, 0)])
    w = rng.choice(np.array([0, 1, RB - 17, RB - 16, RB - 1, RB, RB + 15]), n.shape); q = boxes(n, rng.integers(0, F, (N, 8, 16, L)))
    s = np.ascontiguousarray(np.argsort(rng.random((N, 8, S)), axis=-1)[..., :L])
    for a in range(N):
        for g in range(8):
            x = np.take_along_axis(q[a, g], np.minimum(p[a, g], 15)[None, :], 0)[0]; o = rng.permutation(C); ex, ne = o[:L], o[L:2 * L]
            v = m[a, g][:, x]; r = rng.integers(0, 16, L); off = np.where(R16 == r, np.where(v < 254, v + 1, v - 1), v)
            hide = (rng.random((16, L)) < 0.5) & (R16 != r) & (rng.random(L) < 0.5)
            pt[a, g][:, ex] = v; pt[a, g][:, ne] = np.where(hide, 255, off)
            first = np.choose(rng.integers(0, 4, L), [16, 15, 0, 1])
            cl[a, g][:, s[a, g]] = np.where(R16 < first, ne, ex)
    return pack(cl, pt, bo, gs, m, q, n, p, s, w)
def setup_inputs_crowd(rng):
    cl, pt, bo, gs, m = keyed(rng); shape = (N, 8, L); a = np.arange(N)
    key = rng.integers(0, 20, (N, 8, 16, L)); key[:, :6] = 0; key[:, 2:4] = 16
    n = rng.integers(0, 17, shape); n[:, :6] = 16; p = np.zeros(shape, np.int64); w = np.zeros(shape, np.int64)
    s = rng.integers(0, S, shape); s[:, :6] = rng.integers(0, S, (N, 6, 1))
    ids = message(rng, key); same = np.array(ids[:, :6, :1, :1]); ids[:, :6] = same
    one = rng.integers(0, L, (N, 8))
    ids[a, 1, :, one[:, 1]] = 19; ids[a, 3, :, one[:, 3]] = 0
    w[:, 4] = RB; w[a, 4, one[:, 4]] = RB - 1
    p[::2, 5] = 16; p[a[::2], 5, one[::2, 5]] = 15; n[a[::2], 5, one[::2, 5]] = 15
    s[:, 6] = rng.choice(np.array([0, S - 1]), (N, L)); ids[:, 6] = rng.choice(np.array([0, 20 * (F // 20) - 20]), (N, 16, L)); gs[:, 6] = rng.choice(np.array([0, S - 1]), (N, C))
    cl[:, 6, :, 0] = 16 * rng.integers(0, C // 32, (N, 1)); cl[:, 6, :, S - 1] = 16 * rng.integers(0, C // 32, (N, 1)); cl[:, 6, 0, S - 1] += 1
    z = (rng.integers(0, N) + np.arange(2)) % N; y = np.array([0, 1, 2, 3, 4, 5, 7])
    n[z] = rng.integers(1, 17, (2, 8, L)); p[z] = 0; w[z] = 0
    ids[z[:, None], y, 0] = message(rng, rng.integers(0, 16, (2, 7, L)))
    for r in range(N):
        if r not in z: pt[r, 7, :, C // 2::4] = 0
    return pack(cl, pt, bo, gs, m, boxes(n, ids), n, p, s, w)
def setup_inputs_calm(rng):
    cl, pt, bo, gs, m = keyed(rng); shape = (N, 8, L); i = np.arange(L)
    e = ((np.arange(8) + np.arange(N)[:, None]) % 4)[:, :, None] + 0 * i
    ty = (i + rng.integers(0, 8, (N, 8, 1))) % 8; j = T - 2 - e % 2
    fj = np.where(R16 < j[:, :, None], 0, 16)
    key = np.choose(ty[:, :, None], [0, fj, fj, 0, 16, 16, 0, rng.integers(0, 20, (N, 8, 16, L))])
    n = np.choose(ty, [16, 16, 16, 16, e + 1, 16, e, rng.integers(14, 17, shape)])
    p = np.choose(ty, [0, 0, 0, 0, 0, 10 + e, 0, np.minimum((rng.random(shape) * (n + 1)).astype(np.int64), n)])
    w = np.choose(ty, [RB - (T - 1 - e), RB - 1 - j, RB - 2 - j, RB - T + e % 2, 0, 0, e, rng.integers(0, RB + 16, shape)])
    return pack(cl, pt, bo, gs, m, boxes(n, message(rng, key)), n, p, rng.integers(0, S, shape), w)
def check_inputs(d):
    bad = []
    for k, lo, hi in (("cl", 0, C - 1), ("pt", 0, 255), ("bo", 0, C - 1), ("gs", 0, S - 1), ("m0", 0, 254), ("q0", 0, F - 1), ("n0", 0, 16), ("p0", 0, 16), ("s0", 0, S - 1), ("w0", 0, RB + 15)):
        v = np.asarray(d[k]).astype(np.float64)
        if not np.all((v >= lo) & (v <= hi)): bad.append("range of " + k)
    for k in ("pt", "m0"):
        v = np.asarray(d[k]).astype(np.float64)
        if np.any(v != np.floor(v)): bad.append("whole numbers of " + k)
    if np.any(d["p0"] > d["n0"]): bad.append("p0 at most n0")
    n = d["n0"].astype(np.int64)[:, :, None, :]; q = d["q0"].astype(np.int64).reshape(N, 8, 16, L)
    if np.any(np.where(R16 >= n, q, 0) != 0): bad.append("0 in empty places of q0")
    return bad
def reference(cl, pt, bo, gs, m0, q0, n0, p0, s0, w0):
    lists_ = cl.astype(np.int64).reshape(N, 8, 16, S); tp = pt.astype(np.float32).astype(np.int64).reshape(N, 8, 16, C)
    M = np.zeros((N, 8, 16, F + T * L), np.int64); M[..., :F] = m0.astype(np.float32).astype(np.int64).reshape(N, 8, 16, F)
    q = q0.astype(np.int64).reshape(N, 8, 16, L); n = n0.astype(np.int64); p = p0.astype(np.int64); s = s0.astype(np.int64); w = w0.astype(np.int64)
    body = bo.astype(np.int64); nxt = gs.astype(np.int64)
    for t in range(T):
        rest = w >= RB; act = ~rest & (p < n)
        x = np.take_along_axis(q, np.minimum(p, 15)[:, :, None, :], 2)
        m = np.take_along_axis(M, x, 3)
        c = np.take_along_axis(lists_, s[:, :, None, :], 3)
        ok = np.ones((N, 8, 16, L), bool)
        for row in range(16):
            g = np.take_along_axis(tp[:, :, row], c.reshape(N, 8, 16 * L), 2).reshape(N, 8, 16, L)
            ok &= (g == 255) | (g == m[:, :, row][:, :, None, :])
        found = act & np.any(ok, axis=2); fail = act & ~found; k = np.argmax(ok, axis=2)
        c1 = np.take_along_axis(c, k[:, :, None, :], 2)[:, :, 0]
        b = np.take_along_axis(tp, np.take_along_axis(body, c1, 2)[:, :, None, :], 3)
        out = np.where(found[:, :, None, :], np.where(b == 255, m, b), 0)
        w = np.where(rest, 0, np.where(found, w + k + 1, np.where(fail, w + 16, w)))
        s = np.where(found, np.take_along_axis(nxt, c1, 2), s)
        up = np.concatenate([q[:, :, 1:], np.zeros((N, 8, 1, L), np.int64)], axis=2)
        q = np.where(found[:, :, None, :] & (R16 >= p[:, :, None, :]), up, q)
        n = n - found; p = np.where(found, 0, np.where(fail, p + 1, p))
        d = 1 + t % (N - 1)
        M[..., F + L * t:F + L * (t + 1)] = np.roll(out, d, axis=0)
        keep = np.roll(found, d, axis=0) & (n < 16)
        q = np.where(keep[:, :, None, :] & (R16 == n[:, :, None, :]), F + L * t + np.arange(L), q)
        n = n + keep
    return {"mn": np.ascontiguousarray(M[..., F:]).reshape(N, 128, T * L).astype(np.float32).astype(BF), "yq": q.reshape(N, 128, L).astype(np.float32),
            "ys": np.concatenate([s, p, n, w], axis=2).astype(np.float32)}

@@ -1,0 +1,588 @@
+import numpy as np
+from concourse.bass import DstId, RemoteDMATransfer
+from concourse.mybir import dt, AluOpType, AxisListType, ActivationFunctionType
+
+ALU = AluOpType
+AF = ActivationFunctionType
+H = 2
+LH = 256 // H
+CA = LH // 16
+NB = LH // 32
+STEPS = 5
+NC_, NS, NF = 3072, 2560, 1536
+M0 = 16 + NF
+GBW = 6152
+TCH = 4
+CFG = {"f": "act", "pneg": "act", "gg": "act", "bias": 2000.0, "tries": 2500, "seed": 1, "t0dve": 2, "ech": 1, "ovh": 15.0,
+       "temp": 200.0, "noise": 1500.0, "share": 0.03}
+
+SCRATCH = {
+    "CL": ("sbuf", [128, NS], "int32"),
+    "PT": ("sbuf", [128, NC_], "bfloat16"),
+    "TT": ("sbuf", [128, 16 + NC_], "bfloat16"),
+    "I1": ("sbuf", [128, 128], "bfloat16"),
+    "I13": ("sbuf", [128, 128], "bfloat16"),
+    "I31": ("sbuf", [128, 128], "bfloat16"),
+    "C5": ("sbuf", [128, LH], "bfloat16"),
+    "GB": ("sbuf", [128, GBW], "float32"),
+    "M": ("sbuf", [128, M0 + STEPS * 256], "bfloat16"),
+    "BG": ("sbuf", [128, 384], "int32"),
+    "BF": ("sbuf", [128, 384], "float32"),
+    "BD": ("dram", [16, NC_], "float32"),
+    "QI": ("sbuf", [128, 256], "int32"),
+    "SR": ("sbuf", [128, 256], "int32"),
+    "PI": ("sbuf", [128, 8], "int32"),
+    "PF": ("sbuf", [128, 16], "float32"),
+    "IU": ("sbuf", [128, 160], "float32"),
+    "BW": ("sbuf", [128, 144], "bfloat16"),
+    "I40": ("sbuf", [128, 128], "bfloat16"),
+    "IB": ("sbuf", [128, 128], "bfloat16"),
+    "IH": ("sbuf", [128, 128], "bfloat16"),
+    "IF": ("sbuf", [128, 128], "float32"),
+    "SW0": ("sbuf", [128, 160], "float32"),
+    "SW1": ("sbuf", [128, 160], "float32"),
+    "ZC": ("sbuf", [128, 3 * LH], "bfloat16"),
+    "SEG": ("sbuf", [128, LH], "float32"),
+    "RK": ("sbuf", [128, LH], "float32"),
+    "KI": ("sbuf", [128, STEPS * 256], "float32"),
+    "KEY": ("sbuf", [128, STEPS * 256], "float32"),
+    "MN": ("sbuf", [128, STEPS * 256], "bfloat16"),
+    "OUT": ("sbuf", [128, STEPS * 256], "bfloat16"),
+    "FS": ("sbuf", [128, STEPS * H * CA], "bfloat16"),
+    "FR": ("sbuf", [128, STEPS * H * CA], "bfloat16"),
+    "YQ": ("sbuf", [128, 256], "float32"),
+    "YS": ("sbuf", [128, 256], "float32"),
+}
+for _h in range(H):
+    for _n, _w, _d in (
+        ("T", 16 * LH, "bfloat16"), ("E", 16 * LH, "bfloat16"),
+        ("C16", LH, "uint16"), ("KF", LH, "float32"), ("MS", LH, "bfloat16"), ("T1", LH, "bfloat16"),
+        ("TR", LH, "float32"), ("SC", LH, "float32"), ("GG", LH, "float32"), ("GT", LH, "float32"),
+        ("Q", LH + 8, "float32"), ("XS", LH, "float32"), ("QJ", LH, "int32"), ("YT", LH, "float32"),
+        ("RH", 3 * CA, "bfloat16"), ("SB", 10 * CA, "bfloat16"), ("SF", 10 * CA, "float32"),
+        ("SI", 8 * CA, "int32"), ("SU", 4 * CA, "uint16"),
+    ):
+        SCRATCH["%s%d" % (_n, _h)] = ("sbuf", [128, _w], _d)
+    SCRATCH["A3%d" % _h] = ("sbuf", [128, NB, 32], "float32")
+    SCRATCH["B3%d" % _h] = ("sbuf", [128, NB, 32], "float32")
+    SCRATCH["PS%d" % _h] = ("psum", [128, 512], "float32")
+    SCRATCH["PM%d" % _h] = ("psum", [128, 512], "float32")
+    SCRATCH["PZ%d" % _h] = ("psum", [128, 512], "float32")
+    SCRATCH["PX%d" % _h] = ("psum", [128, 16, 32], "float32")
+
+NDMA = 40
+SEMAPHORES = (["pe", "dve", "act", "pool", "left"] + ["d%d" % i for i in range(NDMA)]
+              + ["am%d_%d" % (t, h) for t in range(STEPS) for h in range(H)]
+              + ["af%d_%d" % (t, h) for t in range(STEPS) for h in range(H)])
+
+G_ = 1.55
+CY = 0.95
+PC = 0.5
+HOP = 90.0
+BW_ = 200.0
+
+
+def plan_ops(g, T, topo, core, rank):
+    ops = []
+    N = len(T.cores)
+
+    def op(eng, calls, reads, writes, cost, banks=(), kind="c", lat=0.0, sem=None):
+        if not isinstance(calls, list):
+            calls = [calls]
+        ops.append({"eng": eng, "calls": calls, "r": list(reads), "w": list(writes), "cost": cost,
+                    "banks": list(banks), "kind": kind, "lat": lat, "sem": sem, "half": 0})
+
+    V, A, P = g.vector, g.scalar, g.tensor
+
+    def vc(n, c=1.0):
+        return max(64.0, n * c) * CY
+
+    def ts(out, in0, s1, s2, o0, o1, r, w, n, c=1.0, banks=()):
+        if o1 is None:
+            f = lambda: V.tensor_scalar(out, in0, s1, None, o0)
+        else:
+            f = lambda: V.tensor_scalar(out, in0, s1, s2, o0, o1)
+        op("dve", f, r, w, vc(n, c), banks)
+
+    def tt(out, a, b, o, r, w, n, c=2.0, banks=()):
+        op("dve", lambda: V.tensor_tensor(out, a, b, o), r, w, vc(n, c), banks)
+
+    def cp(out, a, r, w, n, c=1.0, banks=()):
+        op("dve", lambda: V.tensor_copy(out, a), r, w, vc(n, c), banks)
+
+    def ms(ap, v, w, n):
+        op("dve", lambda: V.memset(ap, v), [], w, vc(n))
+
+    def ac(out, a, func, bias, scale, r, w, n, c=1.0, banks=()):
+        op("act", lambda: A.activation(out, a, func, bias=bias, scale=scale), r, w, vc(n, c) + (60 if c > 1 else 0), banks)
+
+    def mm(lst, r, w, banks):
+        calls = []
+        cost = 0.0
+        for (o, l, rh, st, sp, n, f4) in lst:
+            calls.append(lambda o=o, l=l, rh=rh, st=st, sp=sp: P.matmul(o, l, rh, st, sp))
+            cost += max(64, n) * (4 if f4 else 1) * PC
+        op("pe", calls, r, w, cost, banks)
+
+    def io(out, pat, base, cm, w, n, flt=True):
+        if flt:
+            f = lambda: g.iota(out, pat, base, cm, allow_small_or_imprecise_dtypes=True)
+        else:
+            f = lambda: g.iota(out, pat, base, cm)
+        op("pool", f, [], w + ["pool_order"], 130 + 2 * n * CY)
+
+    loaded = [0.0]
+
+    def dma(q, out, in_, r, w, nbytes, load=False):
+        e = g.sync if q == "sp" else g.scalar
+        if load:
+            loaded[0] += nbytes
+            nbytes = loaded[0]
+        op(q, lambda: e.dma_start(out, in_), r, w, 60.0, ["loads_" + q] if load else [], kind="d", lat=1800 + nbytes / BW_)
+
+    hc = NC_ // 2
+    ms(T.SR[:], 0, ["SR"], 256)
+    for k in range(2):
+        dma("act" if k else "sp", T.PT[:, k * hc:(k + 1) * hc], T.pt[:, k * hc:(k + 1) * hc], [], ["PT%d" % k], 393216, True)
+    for x, src in enumerate((T.s0, T.p0, T.n0, T.w0)):
+        dma("act" if x % 2 else "sp", T.SR[x::16, :], src[:], ["SR"], ["SR%d" % x], 8192, True)
+    dma("sp", T.QI[:], T.q0[:], [], ["QI"], 131072, True)
+    for x, src in enumerate((T.bo, T.gs)):
+        dma("act" if x else "sp", T.BG[:, 192 * x:192 * (x + 1)], src[:], [], ["BG%d" % x], 98304, True)
+    for k in range(2):
+        dma("act" if k else "sp", T.CL[:, k * 1280:(k + 1) * 1280], T.cl[:, k * 1280:(k + 1) * 1280], [], ["CL%d" % k], 655360, True)
+    dma("act", T.M[:, 16:M0], T.m0[:], [], ["Mi"], 393216, True)
+    cp(T.BF[:], T.BG[:], ["BG0", "BG1"], ["BF"], 384)
+    for x in range(2):
+        dma("sp", T.BD[8 * x:8 * x + 8, :], T.BF[:, 192 * x:192 * (x + 1)], ["BF"], ["BD%d" % x], 98304)
+
+    PI, PF = T.PI, T.PF
+    io(PI[:, 0:1], [[0, 1]], 0, 1, ["pi"], 1, flt=False)
+    io(T.IU[:], [[1, 160]], 0, 0, ["IU"], 160)
+    io(T.RK[:], [[0, CA], [4096, 16]], 16 - 65536, 0, ["RK"], LH)
+    io(T.ZC[:, 2 * LH:3 * LH], [[0, CA], [2, 16]], -1, 0, ["ZC1"], LH)
+    io(T.ZC[:, 0:2 * LH], [[0, 2 * CA], [-2, 16]], -1, 0, ["ZC0"], 2 * LH)
+    io(T.KI[:], [[16, STEPS * 16], [0, 16]], M0, 1, ["KI"], STEPS * 256)
+    io(T.GB[:, 1028:GBW], [[0, GBW - 1028]], 0, 0, ["GBa"], GBW - 1028)
+    ms(T.GB[:, 4:1028], 0.0, ["GBb"], 1024)
+    ms(T.M[:, 0:16], -2.0 ** 64, ["Md"], 8)
+    ts(PI[:, 1:2], PI[:, 0:1], 15, None, ALU.bitwise_and, None, ["pi"], ["pb"], 1)
+    ts(PI[:, 2:3], PI[:, 0:1], 4, 1, ALU.arith_shift_right, ALU.bitwise_and, ["pi"], ["pg"], 1)
+    cp(PF[:, 0:3], PI[:, 0:3], ["pi", "pb", "pg"], ["pf"], 3)
+    tt(PF[:, 3:4], PF[:, 1:2], PF[:, 0:1], ALU.subtract, ["pf"], ["ng"], 1)
+    ts(PF[:, 4:5], PF[:, 3:4], -1.0, 15.0, ALU.mult, ALU.add, ["ng"], ["g15"], 1)
+    ts(PF[:, 5:6], PF[:, 0:1], 16.0, None, ALU.add, None, ["pf"], ["p16"], 1)
+    ts(PF[:, 6:7], PF[:, 2:3], -1.0, 1.0, ALU.mult, ALU.add, ["pf"], ["ev"], 1)
+    ts(PF[:, 7:8], PF[:, 1:2], -8192.0, float(15 * 8192 + 4 - 2 ** 21), ALU.mult, ALU.add, ["pf"], ["k0"], 1)
+    ts(PF[:, 8:9], PF[:, 2:3], float(NC_), PF[:, 7:8], ALU.mult, ALU.add, ["pf", "k0"], ["kcol"], 1)
+    ts(T.SW0[:], T.IU[:], PF[:, 5:6], PF[:, 6:7], ALU.is_equal, ALU.mult, ["IU", "p16", "ev"], ["SW0"], 160)
+    ts(T.SW1[:], T.IU[:], PF[:, 5:6], PF[:, 2:3], ALU.is_equal, ALU.mult, ["IU", "p16", "pf"], ["SW1"], 160)
+    ts(T.IB[:], T.IU[:, 0:128], PF[:, 0:1], -2.0 ** 18, ALU.is_equal, ALU.mult, ["IU", "pf"], ["IB"], 128)
+    ts(T.IH[:], T.IB[:], 0.5, None, ALU.mult, None, ["IB"], ["IH"], 64)
+    ts(T.I40[:], T.IB[:], -2.0 ** -58, None, ALU.mult, None, ["IB"], ["I40"], 64)
+    ts(T.IF[:], T.IU[:, 0:128], PF[:, 0:1], None, ALU.is_equal, None, ["IU", "pf"], ["IF"], 128)
+    ts(T.BW[:], T.IU[:, 0:144], PF[:, 4:5], 2.0 ** 17, ALU.is_equal, ALU.mult, ["IU", "g15"], ["BW"], 144)
+    ms(T.SEG[:], 1.0, ["SEG"], LH)
+    ms(T.SEG[:, 0::16], 0.0, ["SEG"], CA)
+    for t in range(STEPS):
+        ac(T.KEY[:, 256 * t:256 * (t + 1)], T.KI[:, 256 * t:256 * (t + 1)], AF.Identity, PF[:, 3:4], 1.0, ["KI", "ng"], ["KEY%d" % t], 256)
+    ms(T.TT[:, 0:16], -1.0, ["TTd"], 16)
+    ms(T.C5[:], 512.0, ["C5"], 64)
+    ts(PF[:, 9:10], PF[:, 1:2], 2.0, 4112.0, ALU.is_ge, ALU.mult, ["pf"], ["dum"], 1)
+    ts(T.GB[:, 0:4], T.IU[:, 0:4], -16.0, PF[:, 9:10], ALU.min, ALU.add, ["IU", "dum"], ["GBd"], 4)
+    ts(T.I13[:], T.IB[:], 2.0 ** -5, None, ALU.mult, None, ["IB"], ["I13"], 64)
+    ts(T.I1[:], T.IB[:], -2.0 ** -18, None, ALU.mult, None, ["IB"], ["I1"], 64)
+    ts(T.I31[:], T.IB[:], 2.0 ** -49, None, ALU.mult, None, ["IB"], ["I31"], 64)
+    ttk = []
+    for k in range(6):
+        cs = slice(512 * k, 512 * (k + 1))
+        cd = slice(16 + 512 * k, 16 + 512 * (k + 1))
+        bk = ("PS0", "PM0", "PS1", "PM1")[k % 4]
+        src = "PT%d" % (k // 3)
+        ac(T[bk][:, 0:512], T.PT[:, cs], AF.Relu, -254.0 * 2.0 ** 40, 2.0 ** 40, [src], ["V" + bk], 512, banks=[bk])
+        tt(T.TT[:, cd], T.PT[:, cs], T[bk][:, 0:512], ALU.max, [src, "V" + bk], ["TT%d" % k], 512, 1.0, [bk])
+        ttk.append("TT%d" % k)
+    gbt = ["GBb"]
+    for al in range(2):
+        for ga in range(2):
+            for x in range(2):
+                tok = "GB%d%d%d" % (al, ga, x)
+                gbt.append(tok)
+                dma("sp", T.GB[16 * al + x::32, 4 + ga * NC_:4 + (ga + 1) * NC_], T.BD[8 * x + ga:8 * x + 8:2, :],
+                    ["GBa", "GBb", "BD%d" % x], [tok], 200000)
+
+    def swap_big(h, src3, lo, r, w):
+        PX = T["PX%d" % h]
+        lst = []
+        for al in range(2):
+            SW = T.SW1 if al else T.SW0
+            for ga in range(2):
+                off = 16 - 16 * (ga - al)
+                lst.append((PX[:, lo:lo + NB, 16 * al:16 * al + 16], SW[:, off:off + 128],
+                            src3[:, :, 16 * ga:16 * ga + 16], ga == 0, ga == 1, LH // 2, True))
+        mm(lst, r + ["SW0", "SW1"], w, ["PX%d" % h])
+
+    def half(h):
+        S = str(h)
+        b = lambda n: T[n + S]
+        M, Tg, E, C16, KF, MS, T1 = T.M, b("T"), b("E"), b("C16"), b("KF"), b("MS"), b("T1")
+        TR, SC, GG, GT, Q, XS, QJ, YT = b("TR"), b("SC"), b("GG"), b("GT"), b("Q"), b("XS"), b("QJ"), b("YT")
+        RH, SB, SF, SI, SU = b("RH"), b("SB"), b("SF"), b("SI"), b("SU")
+        A3, B3, PS, PM, PZ, PX = b("A3"), b("B3"), b("PS"), b("PM"), b("PZ"), b("PX")
+        col = lambda buf, i: buf[:, i * CA:(i + 1) * CA]
+        k_ = lambda n: n + S
+        rho, n1, pneg = col(RH, 0), col(RH, 1), col(RH, 2)
+        pA, pB, n_, wz, act, p1, nr, dd, nu = [col(SB, i) for i in range(9)]
+        sA, sm = [col(SF, i) for i in range(2)]
+        ci, ix, w_, xk, xi = [col(SI, i) for i in range(5)]
+        nfb = GT[:, 2::16]
+        su, iu, bu, xu = [col(SU, i) for i in range(4)]
+        pp = [(pA, k_("pA")), (pB, k_("pB"))]
+        lanes = slice(h * LH, (h + 1) * LH)
+        bS, bM, bZ, bX = k_("PS"), k_("PM"), k_("PZ"), k_("PX")
+        s_ = sA
+
+        ms(Q[:, LH:LH + 8], -1.0e6, [k_("Qpad")], 8)
+        ms(YT[:], 0.0, [k_("YT")], LH)
+
+        cp(A3[:], T.SR[:, lanes], ["SR", "SR0", "SR1", "SR2", "SR3"], [k_("A3")], LH)
+        swap_big(h, A3, 0, [k_("A3")], [k_("X0")])
+        op("dve", [(lambda a=a: V.transpose(GT[:, 32 * a:32 * a + 32], PX[:, a, :])) for a in range(NB)],
+           [k_("X0")], [k_("GT")], NB * vc(32), [bX])
+        cp(su, GT[:, 0::16], [k_("GT")], [k_("su")], CA)
+        cp(B3[:], T.QI[:, lanes], ["QI"], [k_("B3")], LH)
+        swap_big(h, B3, NB, [k_("B3")], [k_("X1")])
+        ac(s_, GT[:, 0::16], AF.Identity, 0.0, 1.0, [k_("GT")], [k_("s")], CA)
+        ac(pA, GT[:, 1::16], AF.Identity, 0.0, 1.0, [k_("GT")], [k_("pA")], CA)
+        ac(pneg, GT[:, 1::16], AF.Identity, 0.0, -1.0, [k_("GT")], [k_("pneg")], CA)
+        ac(n_, GT[:, 2::16], AF.Identity, 0.0, 1.0, [k_("GT")], [k_("n")], CA)
+        cp(w_, GT[:, 3::16], [k_("GT")], [k_("w")], CA)
+        op("dve", [(lambda a=a: V.transpose(TR[:, 32 * a:32 * a + 32], PX[:, NB + a, :])) for a in range(NB)],
+           [k_("X1")], [k_("TR")], NB * vc(32), [bX])
+        tt(Q[:, 0:LH], TR[:], T.RK[:], ALU.add, [k_("TR"), "RK"], [k_("Q")], LH)
+
+        def lin(who, out, a, sc, bi, r, w):
+            if CFG[who] == "act":
+                ac(out, a, AF.Identity, bi, sc, r, w, CA)
+            else:
+                ts(out, a, sc, bi, ALU.mult, ALU.add, r, w, CA)
+
+        def bcast(lo, hi_, r):
+            lst = [(PZ[:, lo * LH:hi_ * LH], T.IH[:], T.ZC[:, lo * LH:hi_ * LH], True, False, (hi_ - lo) * LH, False)]
+            mm(lst, ["IH", "ZC0", "ZC1"], [k_("Z%d_" % q) for q in range(lo, hi_)], [bZ])
+            lst = [(PZ[:, lo * LH + j:hi_ * LH:16], T.IB[:], RH[:, lo * CA:hi_ * CA], False, j == 15, CA, False) for j in range(16)]
+            mm(lst, r + ["IB"], [k_("Z%d_" % q) for q in range(lo, hi_)], [bZ])
+
+        def select():
+            op("dve", lambda: V.tensor_tensor_scan(XS[:], PZ[:, 2 * LH:3 * LH], Q[:, 0:LH], 0.0, ALU.max, ALU.min),
+               [k_("Z2_"), k_("Q")], [k_("XS")], vc(LH), [bZ])
+
+        def ready(p_, pk):
+            ts(nr, w_, 32.0, None, ALU.is_lt, None, [k_("w")], [k_("nr")], CA)
+            tt(dd, n_, p_, ALU.subtract, [k_("n"), pk], [k_("dd")], CA)
+            tt(act, dd, nr, ALU.min, [k_("dd"), k_("nr")], [k_("act")], CA)
+            tt(xk, XS[:, 15::16], act, ALU.mult, [k_("XS"), k_("act")], [k_("xk")], CA)
+            ts(xi, xk, 4095, None, ALU.bitwise_and, None, [k_("xk")], [k_("xi")], CA)
+            cp(xu, xi, [k_("xi")], [k_("xu")], CA)
+            tt(p1, p_, act, ALU.add, [pk, k_("act")], [k_("p1")], CA)
+            tt(wz, w_, nr, ALU.mult, [k_("w"), k_("nr")], [k_("wz")], CA)
+
+        bcast(2, 3, [k_("pneg")])
+        select()
+        ready(*pp[0])
+
+        for t in range(STEPS):
+            yield
+            last = t == STEPS - 1
+            p_, pk = pp[t % 2]
+            pn, pnk = pp[(t + 1) % 2]
+            dst = T.cores[(rank + 1 + t % (N - 1)) % N]
+            rid, pid, _ = topo.addr(dst)
+            mask = topo.mask(core, dst)
+            neng = len(topo.engines(core, dst))
+            cp(C16[:], T.CL[:, 0:NS].indirect(su), ["CL0", "CL1", k_("su")], [k_("C16")], LH + 40, G_)
+            lc = LH // TCH
+            tk = [k_("T%d_" % c) for c in range(TCH)]
+            for c in range(TCH):
+                o_ = Tg[:, 16 * lc * c:16 * lc * (c + 1)]
+                i_ = T.TT[:, 16:16 + NC_].indirect(C16[:, lc * c:lc * (c + 1)])
+                if t == 0 and h == 0 and c >= TCH - CFG["t0dve"]:
+                    ts(o_, i_, 2.0 ** -40, None, ALU.mult, None, ttk + [k_("C16")], [tk[c]], 16 * lc + 40, G_)
+                else:
+                    ac(o_, i_, AF.Identity, 0.0, 2.0 ** -40, ttk + [k_("C16")], [tk[c]], 16 * lc, G_)
+            ts(KF[:], C16[:], PF[:, 8:9], None, ALU.add, None, [k_("C16"), "kcol"], [k_("KF")], LH)
+            wend = M0 if t == 0 else M0 + 256 * (t - 1) + LH * (h + 1)
+            rd = ["Md", "Mi", k_("xu")] + ["AM%d_%d" % (u, o) for u in range(t) for o in range(H) if u < t - 1 or o <= h]
+            ac(MS[:], M[:, 0:wend].indirect(xu), AF.Identity, 0.0, 1.0, rd, [k_("MS")], LH, G_)
+            mm([(PM[:, 0:LH], T.I40[:], MS[:], True, True, LH, False)], [k_("MS"), "I40"], [k_("PMv")], [bM])
+            mm([(PS[:, 0:LH], T.IF[:], KF[:], True, False, LH, True)], [k_("KF"), "IF"], [k_("S")], [bS])
+            ech = CFG["ech"]
+            le, per = LH // ech, 2 * ech
+            for e in range(ech):
+                tke = tk[e * TCH // ech:(e + 1) * TCH // ech]
+                lo, hi_ = e * le, (e + 1) * le
+                for c in range(4):
+                    mm([(PS[:, lo:hi_], T.BW[:, 15 - k:143 - k], Tg[:, 16 * lo + k:16 * hi_:16], False, False, le, False)
+                        for k in range(4 * c, 4 * c + 4)], tke + ["BW"], [k_("S")], [bS])
+                if e == 0:
+                    mm([(PS[:, 0:LH], T.I40[:], MS[:], False, False, LH, False)], [k_("MS"), "I40"], [k_("S")], [bS])
+                for c in range(16 // per):
+                    ks = range(per * c, per * (c + 1))
+                    et = k_("E%d_%d_" % (e, c))
+                    op("dve", [(lambda k=k, lo=lo, hi_=hi_: V.tensor_tensor(
+                        E[:, k * LH + lo:k * LH + hi_], Tg[:, 16 * lo + k:16 * hi_:16], PM[:, lo:hi_], ALU.is_equal)) for k in ks],
+                       tke + [k_("PMv")], [et], per * (vc(le) + CFG["ovh"]), [bM])
+                    mm([(PS[:, lo:hi_], T.BW[:, 15 - k:143 - k], E[:, k * LH + lo:k * LH + hi_], False,
+                         k == 15 and e == ech - 1, le, False) for k in ks], [et, "BW"], [k_("S")], [bS])
+            op("dve", lambda: V.transpose(TR[:], PS[:, 0:LH]), [k_("S")], [k_("TR")], vc(LH), [bS])
+            op("dve", lambda: V.tensor_tensor_scan(SC[:], T.SEG[:], TR[:], 0.0, ALU.mult, ALU.max),
+               [k_("TR"), "SEG"], [k_("SC")], vc(LH))
+            cp(ci, SC[:, 15::16], [k_("SC")], [k_("ci")], CA)
+            ts(ix, ci, 8191, None, ALU.bitwise_and, None, [k_("ci")], [k_("ix")], CA)
+            cp(iu, ix, [k_("ix")], [k_("iu")], CA)
+            if CFG["gg"] == "act":
+                ac(GG[:], T.GB[:, 0:GBW].indirect(iu), AF.Identity, 0.0, 1.0, ["GBa", "GBd", k_("iu")] + gbt, [k_("GG")], LH, G_)
+            else:
+                cp(GG[:], T.GB[:, 0:GBW].indirect(iu), ["GBa", "GBd", k_("iu")] + gbt, [k_("GG")], LH + 40, G_)
+            op("dve", lambda: V.transpose(GT[:], GG[:]), [k_("GG")], [k_("GT")], vc(LH))
+            lst = []
+            for al in range(2):
+                SW = T.SW1 if al else T.SW0
+                for ga in range(2):
+                    off = 16 - 16 * (ga - al)
+                    lst.append((PX[:, 0, al:CA:2], SW[:, off:off + 128], SC[:, 15 + 16 * ga::32], False, al + ga == 2, NB, True))
+            so = PX[:, 0, 0:CA]
+            mm([(so, T.I13[:], wz, True, False, CA, False), (so, T.IH[:], act, False, False, CA, False)],
+               [k_("wz"), k_("act"), "I13", "IH"], [k_("X0")], [bX])
+            mm(lst, [k_("SC"), "SW0", "SW1"], [k_("X0")], [bX])
+            ts(w_, so, -2.0 ** -13, 0.375, ALU.mult, ALU.add, [k_("X0")], [k_("w")], CA, banks=[bX])
+            fc = slice((t * H + h) * CA, (t * H + h + 1) * CA)
+            f_, a_ = T.FS[:, fc], T.FR[:, fc]
+            ft = k_("f%d_" % t)
+            lin("f", f_, nfb, -2.0 ** -12, 1.0, [k_("GT")], [ft])
+            op("pool", lambda f_=f_, a_=a_, t=t, pid=pid, rid=rid, mask=mask: g.remote_dma(
+                a_, f_, T.sem["af%d_%d" % (t, h)], T.sem.left, pid, rid, mask),
+               [ft], [k_("AF%d_" % t)], 300.0, kind="r", lat=2000.0, sem=("af%d_%d" % (t, h), neng))
+            ts(bu, GT[:, 0::16], 16.0, None, ALU.add, None, [k_("GT")], [k_("bu")], CA)
+            tt(sm, s_, nfb, ALU.min, [k_("s"), k_("GT")], [k_("sm")], CA)
+            if last:
+                tt(YT[:, 0::16], GT[:, 1::16], sm, ALU.max, [k_("GT"), k_("sm"), k_("YT")], [k_("Y0")], CA)
+            else:
+                tt(s_, GT[:, 1::16], sm, ALU.max, [k_("GT"), k_("sm")], [k_("s")], CA)
+                cp(su, s_, [k_("s")], [k_("su")], CA)
+            oc = slice(256 * t + h * LH, 256 * t + (h + 1) * LH)
+            ot = k_("O%d_" % t)
+            ac(T1[:], T.TT[:, 0:16 + NC_].indirect(bu), AF.Identity, 0.0, 1.0, ttk + ["TTd", k_("bu")], [k_("T1")], LH, G_)
+            mm([(PS[:, LH:2 * LH], T.I1[:], T.C5[:], True, False, LH, False),
+                (PS[:, LH:2 * LH], T.I1[:], MS[:], False, False, LH, False)], ["I1", "C5", k_("MS")], [k_("B")], [bS])
+            mm([(PS[:, LH:2 * LH], T.I31[:], T1[:], False, True, LH, False)], ["I31", k_("T1")], [k_("B")], [bS])
+            tt(T.OUT[:, oc], T1[:], PS[:, LH:2 * LH], ALU.min, [k_("T1"), k_("B")], [ot], LH, 1.0, [bS])
+            land = M[:, M0 + oc.start:M0 + oc.stop]
+            op("pool", lambda land=land, oc=oc, t=t, pid=pid, rid=rid, mask=mask: g.remote_dma(
+                land, T.OUT[:, oc], T.sem["am%d_%d" % (t, h)], T.sem.left, pid, rid, mask),
+               [ot], [k_("AM%d_" % t)], 300.0, kind="r", lat=2300.0, sem=("am%d_%d" % (t, h), neng))
+            ac(T.MN[:, oc], land, AF.Relu, 0.0, 1.0, [k_("AM%d_" % t)], [k_("MN%d_" % t)], LH)
+            if last:
+                cp(YT[:, 3::16], w_, [k_("w"), k_("YT")], [k_("Y3")], CA)
+            tt(rho, p_, nfb, ALU.max, [pk, k_("GT")], [k_("rho")], CA)
+            tt(n1, n_, f_, ALU.subtract, [k_("n"), ft], [k_("n1")], CA)
+            if last:
+                tt(YT[:, 1::16], p1, nfb, ALU.min, [k_("p1"), k_("GT"), k_("YT")], [k_("Y1")], CA)
+                bcast(0, 2, [k_("rho"), k_("n1")])
+            else:
+                tt(pn, p1, nfb, ALU.min, [k_("p1"), k_("GT")], [pnk], CA)
+                lin("pneg", pneg, pn, -1.0, 0.0, [pnk], [k_("pneg")])
+                bcast(0, 3, [k_("rho"), k_("n1"), k_("pneg")])
+            tt(PZ[:, 0:LH], PZ[:, 0:LH], Q[:, 1:LH + 1], ALU.min, [k_("Z0_"), k_("Q"), k_("Qpad")], [k_("Z0_")], LH, 1.0, [bZ])
+            tt(PZ[:, LH:2 * LH], PZ[:, LH:2 * LH], T.KEY[:, oc], ALU.min, [k_("Z1_"), "KEY%d" % t], [k_("Z1_")], LH, 1.0, [bZ])
+            tt(Q[:, 0:LH], Q[:, 0:LH], PZ[:, 0:LH], ALU.max, [k_("Z0_"), k_("Q")], [k_("Q")], LH, 1.0, [bZ])
+            tt(Q[:, 0:LH], Q[:, 0:LH], PZ[:, LH:2 * LH], ALU.max, [k_("Z1_"), k_("Q")], [k_("Q")], LH, 1.0, [bZ])
+            if not last:
+                select()
+            tt(nu, n1, a_, ALU.add, [k_("n1"), k_("AF%d_" % t)], [k_("nu")], CA)
+            if not last:
+                ts(n_, nu, 16.0, None, ALU.min, None, [k_("nu")], [k_("n")], CA)
+                ready(pn, pnk)
+
+        ts(pneg, nu, -1.0, 1.0, ALU.mult, ALU.add, [k_("nu")], [k_("pneg")], CA)
+        ts(YT[:, 2::16], nu, 16.0, None, ALU.min, None, [k_("nu"), k_("YT")], [k_("Y2")], CA)
+        bcast(2, 3, [k_("pneg")])
+        cp(QJ[:], Q[:, 0:LH], [k_("Q")], [k_("QJ")], LH)
+        ts(QJ[:], QJ[:], 4095, None, ALU.bitwise_and, None, [k_("QJ")], [k_("QJ")], LH)
+        op("dve", [(lambda a=a: V.transpose(A3[:, a, :], YT[:, 32 * a:32 * a + 32])) for a in range(NB)],
+           [k_("Y0"), k_("Y1"), k_("Y2"), k_("Y3")], [k_("A3")], NB * vc(32))
+        swap_big(h, A3, 0, [k_("A3")], [k_("X0")])
+        ac(T.YS[:, lanes], PX[:, 0:NB, :], AF.Identity, 0.0, 1.0, [k_("X0")], [k_("YS")], LH, banks=[bX])
+        tt(XS[:], QJ[:], PZ[:, 2 * LH:3 * LH], ALU.min, [k_("QJ"), k_("Z2_")], [k_("XS")], LH, 1.0, [bZ])
+        op("dve", [(lambda a=a: V.transpose(B3[:, a, :], XS[:, 32 * a:32 * a + 32])) for a in range(NB)],
+           [k_("XS")], [k_("B3")], NB * vc(32))
+        swap_big(h, B3, NB, [k_("B3")], [k_("X1")])
+        ac(T.YQ[:, lanes], PX[:, NB:2 * NB, :], AF.Relu, -16.0, 1.0, [k_("X1")], [k_("YQ")], LH, banks=[bX])
+        dma("act" if h else "sp", T.yq[:, lanes], T.YQ[:, lanes], [k_("YQ")], [k_("yq")], 65536)
+
+    runs = [half(h) for h in range(H)]
+    for _ in range(STEPS + 1):
+        for h, r in enumerate(runs):
+            n0 = len(ops)
+            next(r, None)
+            for o in ops[n0:]:
+                o["half"] = h
+    e4 = 256 * (STEPS - 1) + LH
+    names = ["MN%d_%d" % (t, h) for t in range(STEPS) for h in range(H)]
+    dma("sp", T.mn[:, 0:e4], T.MN[:, 0:e4], names[:-1], ["mn0"], 262144)
+    dma("act", T.mn[:, e4:256 * STEPS], T.MN[:, e4:256 * STEPS], names[-1:], ["mn1"], 32768)
+    for x in range(4):
+        dma("act" if x % 2 else "sp", T.ys[:, 256 * x:256 * (x + 1)], T.YS[x::16, :], ["YS%d" % h for h in range(H)], ["ys%d" % x], 8192)
+    return ops
+
+
+def link(ops):
+    lastw, readers, bank = {}, {}, {}
+    for i, o in enumerate(ops):
+        hard, soft = set(), set()
+        for r in o["r"]:
+            if r in lastw:
+                hard.add(lastw[r])
+        for w in o["w"]:
+            if w in lastw:
+                (soft if w == "pool_order" else hard).add(lastw[w])
+            hard.update(readers.get(w, []))
+        for bk in o["banks"]:
+            for e, j in bank.get(bk, {}).items():
+                (soft if e == o["eng"] else hard).add(j)
+        if o["eng"] == "pe":
+            own = set(j for j in hard if ops[j]["eng"] == "pe")
+            hard -= own
+            soft |= own
+        hard.discard(i)
+        soft.discard(i)
+        o["hard"], o["soft"] = hard, soft - hard
+        for r in o["r"]:
+            readers.setdefault(r, []).append(i)
+        for w in o["w"]:
+            lastw[w] = i
+            readers[w] = []
+        for bk in o["banks"]:
+            bank.setdefault(bk, {})[o["eng"]] = i
+
+
+def schedule(eng, cost, succ, npred, rdy0, tail, prio):
+    n = len(eng)
+    left = list(npred)
+    rdy = list(rdy0)
+    free = [0.0] * 5
+    pend = [[] for _ in range(5)]
+    for i in range(n):
+        if left[i] == 0:
+            pend[eng[i]].append(i)
+    out, start, end = [], [0.0] * n, 0.0
+    for _ in range(n):
+        t0, e = 1e18, 0
+        for q in range(5):
+            if pend[q]:
+                t = min([rdy[i] for i in pend[q]])
+                if t < free[q]:
+                    t = free[q]
+                if t < t0:
+                    t0, e = t, q
+        i, bp = -1, -1e18
+        for j in pend[e]:
+            if rdy[j] <= t0 and prio[j] > bp:
+                i, bp = j, prio[j]
+        pend[e].remove(i)
+        fin = t0 + cost[i]
+        start[i] = t0
+        free[e] = fin
+        if fin + tail[i] > end:
+            end = fin + tail[i]
+        out.append(i)
+        for j, d in succ[i]:
+            if fin + d > rdy[j]:
+                rdy[j] = fin + d
+            left[j] -= 1
+            if left[j] == 0:
+                pend[eng[j]].append(j)
+    return out, start, end
+
+
+def order(ops):
+    n = len(ops)
+    names = ["pe", "dve", "act", "pool", "sp"]
+    eng = [names.index(o["eng"]) for o in ops]
+    cost = [o["cost"] for o in ops]
+    lat = [o["lat"] for o in ops]
+    succ, pred = [[] for _ in range(n)], [[] for _ in range(n)]
+    for i, o in enumerate(ops):
+        for j in sorted(o["hard"]):
+            succ[j].append((i, lat[j] + HOP))
+            pred[i].append((j, lat[j] + HOP))
+        for j in sorted(o["soft"]):
+            succ[j].append((i, 0.0))
+            pred[i].append((j, 0.0))
+    np_, ns_, zero = [len(p) for p in pred], [len(s) for s in succ], [0.0] * n
+    fwd = lambda pr: schedule(eng, cost, succ, np_, zero, lat, pr)
+    bwd = lambda pr: schedule(eng, cost, pred, ns_, lat, zero, pr)
+    prio = [0.0] * n
+    for i in range(n - 1, -1, -1):
+        prio[i] = cost[i] + max([prio[j] + d for j, d in succ[i]] + [lat[i]])
+    rng = np.random.default_rng(CFG["seed"])
+    best = fwd([prio[i] - CFG["bias"] * ops[i]["half"] for i in range(n)])
+    cur = best
+    for k in range(CFG["tries"]):
+        noise = (rng.normal(0.0, CFG["noise"], n) * (rng.random(n) < CFG["share"])).tolist()
+        back = bwd([cur[1][i] + cost[i] + noise[i] for i in range(n)])
+        got = fwd([back[1][i] + cost[i] for i in range(n)])
+        if got[2] <= cur[2] + CFG["temp"] * (1.0 - k / CFG["tries"]) * rng.exponential():
+            cur = got
+            if got[2] < best[2]:
+                best = got
+    return best
+
+
+ORDER = {}
+
+
+def rank_program(g, core, T, topo):
+    rank = T.rank_of(core)
+    if rank is None:
+        return
+    ops = plan_ops(g, T, topo, core, rank)
+    link(ops)
+    if "seq" not in ORDER:
+        ORDER["seq"] = order(ops)[0]
+    queue = {"pe": g.tensor, "dve": g.vector, "act": g.scalar, "pool": g, "sp": g.sync}
+    count = {"pe": 0, "dve": 0, "act": 0, "pool": 0}
+    seen = dict((e, {}) for e in queue)
+    dmas = []
+    left = 0
+    for i in ORDER["seq"]:
+        o = ops[i]
+        e = o["eng"]
+        need = {}
+        for j in o["hard"]:
+            s, v = ops[j]["done"]
+            need[s] = max(need.get(s, 0), v)
+        for s in sorted(need):
+            if seen[e].get(s, 0) < need[s]:
+                queue[e].wait_ge(T.sem[s], need[s])
+                seen[e][s] = need[s]
+        if o["kind"] == "c":
+            for c in o["calls"]:
+                c().then_inc(T.sem[e], 1)
+                count[e] += 1
+            o["done"] = (e, count[e])
+        elif o["kind"] == "d":
+            s = "d%d" % len(dmas)
+            o["calls"][0]().then_inc(T.sem[s], 16)
+            dmas.append(s)
+            o["done"] = (s, 16)
+        else:
+            o["calls"][0]()
+            o["done"] = o["sem"]
+            left += o["sem"][1]
+    g.wait_ge(T.sem.left, left)
+    for e in count:
+        g.sync.wait_ge(T.sem[e], count[e])
+    for s in dmas:
+        if not any(seen[e].get(s, 0) for e in seen):
+            g.sync.wait_ge(T.sem[s], 16)

@@ -13,14 +13,15 @@ NC_, NS, NF = 3072, 2560, 1536
 M0 = 16 + NF
 GBW = 6152
 TCH = 4
-CFG = {"f": "act", "pneg": "act", "gg": "act", "bias": 2000.0, "tries": 2500, "seed": 1, "t0dve": 2, "ech": 1, "ovh": 15.0,
-       "temp": 200.0, "noise": 1500.0, "share": 0.03}
+CFG = {"fc": "act", "nch": "dve", "ins": "dve", "f": "dve", "pneg": "dve", "gg": "act", "bias": 2000.0, "tries": 6000, "seed": 1, "t0dve": 2, "ech": 2, "ovh": 3.0,
+       "temp": 150.0, "noise": 1000.0, "share": 0.05}
 
 SCRATCH = {
     "CL": ("sbuf", [128, NS], "int32"),
     "PT": ("sbuf", [128, NC_], "bfloat16"),
     "TT": ("sbuf", [128, 16 + NC_], "bfloat16"),
     "I1": ("sbuf", [128, 128], "bfloat16"),
+    "SWB": ("sbuf", [128, 320], "bfloat16"),
     "I13": ("sbuf", [128, 128], "bfloat16"),
     "I31": ("sbuf", [128, 128], "bfloat16"),
     "C5": ("sbuf", [128, LH], "bfloat16"),
@@ -28,7 +29,6 @@ SCRATCH = {
     "M": ("sbuf", [128, M0 + STEPS * 256], "bfloat16"),
     "BG": ("sbuf", [128, 384], "int32"),
     "BF": ("sbuf", [128, 384], "float32"),
-    "BD": ("dram", [16, NC_], "float32"),
     "QI": ("sbuf", [128, 256], "int32"),
     "SR": ("sbuf", [128, 256], "int32"),
     "PI": ("sbuf", [128, 8], "int32"),
@@ -46,7 +46,12 @@ SCRATCH = {
     "RK": ("sbuf", [128, LH], "float32"),
     "KI": ("sbuf", [128, STEPS * 256], "float32"),
     "KEY": ("sbuf", [128, STEPS * 256], "float32"),
-    "MN": ("sbuf", [128, STEPS * 256], "bfloat16"),
+    "GO": ("sbuf", [128, 256], "bfloat16"),
+    "GM": ("sbuf", [128, 2048], "bfloat16"),
+    "DG": ("sbuf", [128, 128], "bfloat16"),
+    "RM": ("sbuf", [128, 16], "float32"),
+    "YN": ("sbuf", [128, 256], "float32"),
+    "N40": ("sbuf", [128, 128], "bfloat16"),
     "OUT": ("sbuf", [128, STEPS * 256], "bfloat16"),
     "FS": ("sbuf", [128, STEPS * H * CA], "bfloat16"),
     "FR": ("sbuf", [128, STEPS * H * CA], "bfloat16"),
@@ -56,7 +61,7 @@ SCRATCH = {
 for _h in range(H):
     for _n, _w, _d in (
         ("T", 16 * LH, "bfloat16"), ("E", 16 * LH, "bfloat16"),
-        ("C16", LH, "uint16"), ("KF", LH, "float32"), ("MS", LH, "bfloat16"), ("T1", LH, "bfloat16"),
+        ("C16", LH, "uint16"), ("KF", LH, "float32"), ("MS", LH, "bfloat16"), ("T1", LH, "bfloat16"), ("U", LH, "bfloat16"),
         ("TR", LH, "float32"), ("SC", LH, "float32"), ("GG", LH, "float32"), ("GT", LH, "float32"),
         ("Q", LH + 8, "float32"), ("XS", LH, "float32"), ("QJ", LH, "int32"), ("YT", LH, "float32"),
         ("RH", 3 * CA, "bfloat16"), ("SB", 10 * CA, "bfloat16"), ("SF", 10 * CA, "float32"),
@@ -76,13 +81,20 @@ SEMAPHORES = (["pe", "dve", "act", "pool", "left"] + ["d%d" % i for i in range(N
               + ["af%d_%d" % (t, h) for t in range(STEPS) for h in range(H)])
 
 G_ = 1.55
-CY = 0.95
-PC = 0.5
-HOP = 90.0
-BW_ = 200.0
+CY = 0.88
+PC = 0.46
+HOP = 120.0
+BW_ = 260.0
+FIRST = 3000.0
 
 
-def plan_ops(g, T, topo, core, rank):
+RL = 1.0
+PLANS = ((G_, CY, PC, HOP, BW_, FIRST, RL), (1.15, 0.9, 0.46, 100.0, 300.0, 2000.0, 0.9), (2.0, 1.1, 0.56, 150.0, 230.0, 4000.0, 1.25),
+         (1.55, 1.2, 0.62, 150.0, 230.0, 3000.0, 1.1))
+
+
+def plan_ops(g, T, topo, core, rank, plan=0):
+    G_, CY, PC, _, BW_, FIRST, RL = PLANS[plan]
     ops = []
     N = len(T.cores)
 
@@ -147,14 +159,13 @@ def plan_ops(g, T, topo, core, rank):
     for x, src in enumerate((T.s0, T.p0, T.n0, T.w0)):
         dma("act" if x % 2 else "sp", T.SR[x::16, :], src[:], ["SR"], ["SR%d" % x], 8192, True)
     dma("sp", T.QI[:], T.q0[:], [], ["QI"], 131072, True)
-    for x, src in enumerate((T.bo, T.gs)):
-        dma("act" if x else "sp", T.BG[:, 192 * x:192 * (x + 1)], src[:], [], ["BG%d" % x], 98304, True)
     for k in range(2):
         dma("act" if k else "sp", T.CL[:, k * 1280:(k + 1) * 1280], T.cl[:, k * 1280:(k + 1) * 1280], [], ["CL%d" % k], 655360, True)
     dma("act", T.M[:, 16:M0], T.m0[:], [], ["Mi"], 393216, True)
-    cp(T.BF[:], T.BG[:], ["BG0", "BG1"], ["BF"], 384)
-    for x in range(2):
-        dma("sp", T.BD[8 * x:8 * x + 8, :], T.BF[:, 192 * x:192 * (x + 1)], ["BF"], ["BD%d" % x], 98304)
+    for x, src in enumerate((T.bo, T.gs)):
+        for ga in range(2):
+            dma("sp", T.BG[64 * ga:64 * ga + 64, 192 * x:192 * (x + 1)], src[ga::2, :], [], ["BG%d%d" % (x, ga)], 49152, True)
+    cp(T.BF[:], T.BG[:], ["BG00", "BG01", "BG10", "BG11"], ["BF"], 384)
 
     PI, PF = T.PI, T.PF
     io(PI[:, 0:1], [[0, 1]], 0, 1, ["pi"], 1, flt=False)
@@ -163,9 +174,9 @@ def plan_ops(g, T, topo, core, rank):
     io(T.ZC[:, 2 * LH:3 * LH], [[0, CA], [2, 16]], -1, 0, ["ZC1"], LH)
     io(T.ZC[:, 0:2 * LH], [[0, 2 * CA], [-2, 16]], -1, 0, ["ZC0"], 2 * LH)
     io(T.KI[:], [[16, STEPS * 16], [0, 16]], M0, 1, ["KI"], STEPS * 256)
-    io(T.GB[:, 1028:GBW], [[0, GBW - 1028]], 0, 0, ["GBa"], GBW - 1028)
-    ms(T.GB[:, 4:1028], 0.0, ["GBb"], 1024)
-    ms(T.M[:, 0:16], -2.0 ** 64, ["Md"], 8)
+    io(T.GB[:, 2052:GBW], [[0, GBW - 2052]], 0, 0, ["GBa"], GBW - 2052)
+    ms(T.GB[:, 4:2052], 0.0, ["GBb"], 2048)
+    ms(T.M[:, 0:16], 2.0 ** 64, ["Md"], 8)
     ts(PI[:, 1:2], PI[:, 0:1], 15, None, ALU.bitwise_and, None, ["pi"], ["pb"], 1)
     ts(PI[:, 2:3], PI[:, 0:1], 4, 1, ALU.arith_shift_right, ALU.bitwise_and, ["pi"], ["pg"], 1)
     cp(PF[:, 0:3], PI[:, 0:3], ["pi", "pb", "pg"], ["pf"], 3)
@@ -186,10 +197,21 @@ def plan_ops(g, T, topo, core, rank):
     ms(T.SEG[:, 0::16], 0.0, ["SEG"], CA)
     for t in range(STEPS):
         ac(T.KEY[:, 256 * t:256 * (t + 1)], T.KI[:, 256 * t:256 * (t + 1)], AF.Identity, PF[:, 3:4], 1.0, ["KI", "ng"], ["KEY%d" % t], 256)
-    ms(T.TT[:, 0:16], -1.0, ["TTd"], 16)
+    ms(T.TT[:, 0:16], 0.0, ["TTd"], 16)
+    ts(T.N40[:], T.IB[:], 2.0 ** -58, None, ALU.mult, None, ["IB"], ["N40"], 64)
     ms(T.C5[:], 512.0, ["C5"], 64)
     ts(PF[:, 9:10], PF[:, 1:2], 2.0, 4112.0, ALU.is_ge, ALU.mult, ["pf"], ["dum"], 1)
     ts(T.GB[:, 0:4], T.IU[:, 0:4], -16.0, PF[:, 9:10], ALU.min, ALU.add, ["IU", "dum"], ["GBd"], 4)
+    cp(T.SWB[:, 0:160], T.SW0[:], ["SW0"], ["SWB0"], 160)
+    cp(T.SWB[:, 160:320], T.SW1[:], ["SW1"], ["SWB1"], 160)
+    ts(T.GO[:, 0:128], T.IU[:, 0:128], PF[:, 3:4], 0.0, ALU.add, ALU.is_ge, ["IU", "ng"], ["GO0"], 128)
+    ts(T.GO[:, 128:256], T.IU[:, 0:128], PF[:, 4:5], None, ALU.is_le, None, ["IU", "g15"], ["GO1"], 128)
+    tt(T.GO[:, 0:128], T.GO[:, 0:128], T.GO[:, 128:256], ALU.mult, ["GO0", "GO1"], ["GO0"], 128)
+    ts(T.RM[:], T.IU[:, 0:16], PF[:, 1:2], 8192.0, ALU.is_equal, ALU.mult, ["IU", "pf"], ["RM"], 16)
+    ts(PF[:, 10:11], PF[:, 1:2], -16.0, -8.0, ALU.mult, ALU.add, ["pf"], ["dg"], 1)
+    ts(T.DG[:], T.IU[:, 0:128], PF[:, 0:1], PF[:, 10:11], ALU.is_equal, ALU.mult, ["IU", "pf", "dg"], ["DG"], 128)
+    for j in range(16):
+        ac(T.GM[:, 128 * j:128 * (j + 1)], T.GO[:, 0:128], AF.Identity, 0.0, T.RM[:, j:j + 1], ["GO0", "RM"], ["GM%d" % j], 128)
     ts(T.I13[:], T.IB[:], 2.0 ** -5, None, ALU.mult, None, ["IB"], ["I13"], 64)
     ts(T.I1[:], T.IB[:], -2.0 ** -18, None, ALU.mult, None, ["IB"], ["I1"], 64)
     ts(T.I31[:], T.IB[:], 2.0 ** -49, None, ALU.mult, None, ["IB"], ["I31"], 64)
@@ -208,8 +230,8 @@ def plan_ops(g, T, topo, core, rank):
             for x in range(2):
                 tok = "GB%d%d%d" % (al, ga, x)
                 gbt.append(tok)
-                dma("sp", T.GB[16 * al + x::32, 4 + ga * NC_:4 + (ga + 1) * NC_], T.BD[8 * x + ga:8 * x + 8:2, :],
-                    ["GBa", "GBb", "BD%d" % x], [tok], 200000)
+                dma("sp", T.GB[16 * al + x::32, 4 + ga * NC_:4 + (ga + 1) * NC_], T.BF[64 * ga:64 * ga + 64, 192 * x:192 * (x + 1)],
+                    ["GBa", "GBb", "BF"], [tok], 200000)
 
     def swap_big(h, src3, lo, r, w):
         PX = T["PX%d" % h]
@@ -232,8 +254,14 @@ def plan_ops(g, T, topo, core, rank):
         col = lambda buf, i: buf[:, i * CA:(i + 1) * CA]
         k_ = lambda n: n + S
         rho, n1, pneg = col(RH, 0), col(RH, 1), col(RH, 2)
-        pA, pB, n_, wz, act, p1, nr, dd, nu = [col(SB, i) for i in range(9)]
-        sA, sm = [col(SF, i) for i in range(2)]
+        n_, wz, act, nr, dd, nu, fw = [col(SB, i) for i in range(7)]
+        fwv = [SB[:, 6 * CA + ga:7 * CA:2] for ga in range(2)]
+        both = SF[:, 0:2 * CA]
+        p1, sA = SF[:, 0:2 * CA:2], SF[:, 1:2 * CA:2]
+        kept = [SF[:, 2 * CA * u:2 * CA * (u + 1)] for u in (1, 2)]
+        pA, pB = SF[:, 2 * CA:4 * CA:2], SF[:, 4 * CA:6 * CA:2]
+        sms = [SF[:, 2 * CA + 1:4 * CA:2], SF[:, 4 * CA + 1:6 * CA:2]]
+        U = b("U")
         ci, ix, w_, xk, xi = [col(SI, i) for i in range(5)]
         nfb = GT[:, 2::16]
         su, iu, bu, xu = [col(SU, i) for i in range(4)]
@@ -298,8 +326,10 @@ def plan_ops(g, T, topo, core, rank):
             pn, pnk = pp[(t + 1) % 2]
             dst = T.cores[(rank + 1 + t % (N - 1)) % N]
             rid, pid, _ = topo.addr(dst)
-            mask = topo.mask(core, dst)
-            neng = len(topo.engines(core, dst))
+            engs = topo.engines(core, dst)
+            mask = sum(1 << e for e in engs)
+            neng = len(engs)
+            first = FIRST if t == 0 and h == 0 else 0.0
             cp(C16[:], T.CL[:, 0:NS].indirect(su), ["CL0", "CL1", k_("su")], [k_("C16")], LH + 40, G_)
             lc = LH // TCH
             tk = [k_("T%d_" % c) for c in range(TCH)]
@@ -325,7 +355,7 @@ def plan_ops(g, T, topo, core, rank):
                     mm([(PS[:, lo:hi_], T.BW[:, 15 - k:143 - k], Tg[:, 16 * lo + k:16 * hi_:16], False, False, le, False)
                         for k in range(4 * c, 4 * c + 4)], tke + ["BW"], [k_("S")], [bS])
                 if e == 0:
-                    mm([(PS[:, 0:LH], T.I40[:], MS[:], False, False, LH, False)], [k_("MS"), "I40"], [k_("S")], [bS])
+                    mm([(PS[:, 0:LH], T.N40[:], MS[:], False, False, LH, False)], [k_("MS"), "N40"], [k_("S")], [bS])
                 for c in range(16 // per):
                     ks = range(per * c, per * (c + 1))
                     et = k_("E%d_%d_" % (e, c))
@@ -352,23 +382,33 @@ def plan_ops(g, T, topo, core, rank):
                     off = 16 - 16 * (ga - al)
                     lst.append((PX[:, 0, al:CA:2], SW[:, off:off + 128], SC[:, 15 + 16 * ga::32], False, al + ga == 2, NB, True))
             so = PX[:, 0, 0:CA]
+            fc = slice((t * H + h) * CA, (t * H + h + 1) * CA)
+            f_, a_ = T.FS[:, fc], T.FR[:, fc]
+            ft = k_("f%d_" % t)
+            if CFG["f"] == "act":
+                ac(fw, SC[:, 15::16], AF.Sign, 0.0, 1.0, [k_("SC")], [k_("fw")], CA)
+            else:
+                ts(fw, SC[:, 15::16], 0.5, None, ALU.is_gt, None, [k_("SC")], [k_("fw")], CA)
+            mm([(PX[:, 1, al:CA:2], T.SWB[:, 160 * al + 16 - 16 * (ga - al):160 * al + 144 - 16 * (ga - al)], fwv[ga],
+                 ga == 0, ga == 1, NB, False) for al in range(2) for ga in range(2)], [k_("fw"), "SWB0", "SWB1"], [k_("Xf")], [bX])
+            if CFG["fc"] == "act":
+                ac(f_, PX[:, 1, 0:CA], AF.Identity, 0.0, 1.0, [k_("Xf")], [ft], CA, banks=[bX])
+            else:
+                cp(f_, PX[:, 1, 0:CA], [k_("Xf")], [ft], CA, banks=[bX])
             mm([(so, T.I13[:], wz, True, False, CA, False), (so, T.IH[:], act, False, False, CA, False)],
                [k_("wz"), k_("act"), "I13", "IH"], [k_("X0")], [bX])
             mm(lst, [k_("SC"), "SW0", "SW1"], [k_("X0")], [bX])
             ts(w_, so, -2.0 ** -13, 0.375, ALU.mult, ALU.add, [k_("X0")], [k_("w")], CA, banks=[bX])
-            fc = slice((t * H + h) * CA, (t * H + h + 1) * CA)
-            f_, a_ = T.FS[:, fc], T.FR[:, fc]
-            ft = k_("f%d_" % t)
-            lin("f", f_, nfb, -2.0 ** -12, 1.0, [k_("GT")], [ft])
             op("pool", lambda f_=f_, a_=a_, t=t, pid=pid, rid=rid, mask=mask: g.remote_dma(
                 a_, f_, T.sem["af%d_%d" % (t, h)], T.sem.left, pid, rid, mask),
-               [ft], [k_("AF%d_" % t)], 300.0, kind="r", lat=2000.0, sem=("af%d_%d" % (t, h), neng))
+               [ft], [k_("AF%d_" % t)], 300.0 + first, kind="r", lat=2000.0 * RL, sem=("af%d_%d" % (t, h), neng))
             ts(bu, GT[:, 0::16], 16.0, None, ALU.add, None, [k_("GT")], [k_("bu")], CA)
-            tt(sm, s_, nfb, ALU.min, [k_("s"), k_("GT")], [k_("sm")], CA)
+            sm = sms[(t + 1) % 2]
+            tt(kept[(t + 1) % 2], both, GT[:, 4::8], ALU.min, [k_("s"), k_("p1"), k_("GT")], [pnk], 2 * CA)
             if last:
-                tt(YT[:, 0::16], GT[:, 1::16], sm, ALU.max, [k_("GT"), k_("sm"), k_("YT")], [k_("Y0")], CA)
+                tt(YT[:, 0::16], GT[:, 1::16], sm, ALU.max, [k_("GT"), pnk, k_("YT")], [k_("Y0")], CA)
             else:
-                tt(s_, GT[:, 1::16], sm, ALU.max, [k_("GT"), k_("sm")], [k_("s")], CA)
+                tt(s_, GT[:, 1::16], sm, ALU.max, [k_("GT"), pnk], [k_("s")], CA)
                 cp(su, s_, [k_("s")], [k_("su")], CA)
             oc = slice(256 * t + h * LH, 256 * t + (h + 1) * LH)
             ot = k_("O%d_" % t)
@@ -380,44 +420,64 @@ def plan_ops(g, T, topo, core, rank):
             land = M[:, M0 + oc.start:M0 + oc.stop]
             op("pool", lambda land=land, oc=oc, t=t, pid=pid, rid=rid, mask=mask: g.remote_dma(
                 land, T.OUT[:, oc], T.sem["am%d_%d" % (t, h)], T.sem.left, pid, rid, mask),
-               [ot], [k_("AM%d_" % t)], 300.0, kind="r", lat=2300.0, sem=("am%d_%d" % (t, h), neng))
-            ac(T.MN[:, oc], land, AF.Relu, 0.0, 1.0, [k_("AM%d_" % t)], [k_("MN%d_" % t)], LH)
+               [ot], [k_("AM%d_" % t)], 300.0, kind="r", lat=2300.0 * RL, sem=("am%d_%d" % (t, h), neng))
             if last:
                 cp(YT[:, 3::16], w_, [k_("w"), k_("YT")], [k_("Y3")], CA)
             tt(rho, p_, nfb, ALU.max, [pk, k_("GT")], [k_("rho")], CA)
-            tt(n1, n_, f_, ALU.subtract, [k_("n"), ft], [k_("n1")], CA)
+            pe_n = CFG["nch"] == "pe" and not last
+            sn = PX[:, 1, 0:CA]
+            if pe_n:
+                mm([(sn, T.IB[:], n_, True, False, CA, False), (sn, T.IP[:], f_, False, True, CA, False)],
+                   [k_("n"), ft, "IB", "IP"], [k_("Xn")], [bX])
+                ac(n1, sn, AF.Identity, 0.0, -2.0 ** -18, [k_("Xn")], [k_("n1")], CA, banks=[bX])
+            else:
+                tt(n1, n_, f_, ALU.subtract, [k_("n"), ft], [k_("n1")], CA)
             if last:
-                tt(YT[:, 1::16], p1, nfb, ALU.min, [k_("p1"), k_("GT"), k_("YT")], [k_("Y1")], CA)
+                ac(YT[:, 1::16], pn, AF.Identity, 0.0, 1.0, [pnk, k_("YT")], [k_("Y1")], CA)
                 bcast(0, 2, [k_("rho"), k_("n1")])
             else:
-                tt(pn, p1, nfb, ALU.min, [k_("p1"), k_("GT")], [pnk], CA)
                 lin("pneg", pneg, pn, -1.0, 0.0, [pnk], [k_("pneg")])
                 bcast(0, 3, [k_("rho"), k_("n1"), k_("pneg")])
             tt(PZ[:, 0:LH], PZ[:, 0:LH], Q[:, 1:LH + 1], ALU.min, [k_("Z0_"), k_("Q"), k_("Qpad")], [k_("Z0_")], LH, 1.0, [bZ])
-            tt(PZ[:, LH:2 * LH], PZ[:, LH:2 * LH], T.KEY[:, oc], ALU.min, [k_("Z1_"), "KEY%d" % t], [k_("Z1_")], LH, 1.0, [bZ])
-            tt(Q[:, 0:LH], Q[:, 0:LH], PZ[:, 0:LH], ALU.max, [k_("Z0_"), k_("Q")], [k_("Q")], LH, 1.0, [bZ])
-            tt(Q[:, 0:LH], Q[:, 0:LH], PZ[:, LH:2 * LH], ALU.max, [k_("Z1_"), k_("Q")], [k_("Q")], LH, 1.0, [bZ])
+            if CFG["ins"] == "act":
+                tt(Q[:, 0:LH], Q[:, 0:LH], PZ[:, 0:LH], ALU.max, [k_("Z0_"), k_("Q")], [k_("Q")], LH, 1.0, [bZ])
+                ac(U[:], PZ[:, LH:2 * LH], AF.Relu, 0.0, -2.0 ** -18, [k_("Z1_")], [k_("U")], LH, banks=[bZ])
+                mm([(PM[:, LH:2 * LH], T.IF[:], T.KEY[:, oc], True, False, LH, True)], ["IF", "KEY%d" % t], [k_("Yk")], [bM])
+                mm([(PM[:, LH:2 * LH], T.IB[:], U[:], False, True, LH, False)], ["IB", k_("U")], [k_("Yk")], [bM])
+                tt(Q[:, 0:LH], Q[:, 0:LH], PM[:, LH:2 * LH], ALU.max, [k_("Yk"), k_("Q")], [k_("Q")], LH, 1.0, [bM])
+            else:
+                tt(PZ[:, LH:2 * LH], PZ[:, LH:2 * LH], T.KEY[:, oc], ALU.min, [k_("Z1_"), "KEY%d" % t], [k_("Z1_")], LH, 1.0, [bZ])
+                tt(Q[:, 0:LH], Q[:, 0:LH], PZ[:, 0:LH], ALU.max, [k_("Z0_"), k_("Q")], [k_("Q")], LH, 1.0, [bZ])
+                tt(Q[:, 0:LH], Q[:, 0:LH], PZ[:, LH:2 * LH], ALU.max, [k_("Z1_"), k_("Q")], [k_("Q")], LH, 1.0, [bZ])
             if not last:
                 select()
-            tt(nu, n1, a_, ALU.add, [k_("n1"), k_("AF%d_" % t)], [k_("nu")], CA)
+            if pe_n:
+                mm([(sn, T.IB[:], a_, False, True, CA, False)], [k_("AF%d_" % t), "IB"], [k_("Xn")], [bX])
+                ac(nu, sn, AF.Relu, 16.0, 2.0 ** -18, [k_("Xn")], [k_("nu")], CA, banks=[bX])
+                ac(n_, nu, AF.Identity, 16.0, -1.0, [k_("nu")], [k_("n")], CA)
+            else:
+                tt(nu, n1, a_, ALU.add, [k_("n1"), k_("AF%d_" % t)], [k_("nu")], CA)
+                if not last:
+                    ts(n_, nu, 16.0, None, ALU.min, None, [k_("nu")], [k_("n")], CA)
             if not last:
-                ts(n_, nu, 16.0, None, ALU.min, None, [k_("nu")], [k_("n")], CA)
                 ready(pn, pnk)
 
-        ts(pneg, nu, -1.0, 1.0, ALU.mult, ALU.add, [k_("nu")], [k_("pneg")], CA)
-        ts(YT[:, 2::16], nu, 16.0, None, ALU.min, None, [k_("nu"), k_("YT")], [k_("Y2")], CA)
-        bcast(2, 3, [k_("pneg")])
-        cp(QJ[:], Q[:, 0:LH], [k_("Q")], [k_("QJ")], LH)
-        ts(QJ[:], QJ[:], 4095, None, ALU.bitwise_and, None, [k_("QJ")], [k_("QJ")], LH)
+        ts(n_, nu, 16.0, None, ALU.min, None, [k_("nu")], [k_("n")], CA)
+        mm([(PM[:, 0:LH], T.DG[:], T.C5[:], True, False, LH, False)], ["DG", "C5"], [k_("PMv")], [bM])
+        mm([(PM[:, j:LH:16], T.GM[:, 128 * j:128 * (j + 1)], n_, False, j == 15, CA, False) for j in range(16)],
+           [k_("n")] + ["GM%d" % j for j in range(16)], [k_("PMv")], [bM])
         op("dve", [(lambda a=a: V.transpose(A3[:, a, :], YT[:, 32 * a:32 * a + 32])) for a in range(NB)],
-           [k_("Y0"), k_("Y1"), k_("Y2"), k_("Y3")], [k_("A3")], NB * vc(32))
+           [k_("Y0"), k_("Y1"), k_("Y3")], [k_("A3")], NB * vc(32))
         swap_big(h, A3, 0, [k_("A3")], [k_("X0")])
         ac(T.YS[:, lanes], PX[:, 0:NB, :], AF.Identity, 0.0, 1.0, [k_("X0")], [k_("YS")], LH, banks=[bX])
-        tt(XS[:], QJ[:], PZ[:, 2 * LH:3 * LH], ALU.min, [k_("QJ"), k_("Z2_")], [k_("XS")], LH, 1.0, [bZ])
-        op("dve", [(lambda a=a: V.transpose(B3[:, a, :], XS[:, 32 * a:32 * a + 32])) for a in range(NB)],
-           [k_("XS")], [k_("B3")], NB * vc(32))
+        op("dve", [(lambda a=a: V.transpose(B3[:, a, :], Q[:, 32 * a:32 * a + 32])) for a in range(NB)],
+           [k_("Q")], [k_("B3")], NB * vc(32))
         swap_big(h, B3, NB, [k_("B3")], [k_("X1")])
-        ac(T.YQ[:, lanes], PX[:, NB:2 * NB, :], AF.Relu, -16.0, 1.0, [k_("X1")], [k_("YQ")], LH, banks=[bX])
+        cp(QJ[:], PX[:, NB:2 * NB, :], [k_("X1")], [k_("QJ")], LH, banks=[bX])
+        ts(QJ[:], QJ[:], 4095, None, ALU.bitwise_and, None, [k_("QJ")], [k_("QJ")], LH)
+        ac(T.YN[:, lanes], PM[:, 0:LH], AF.Identity, 0.5, 2.0 ** -13, [k_("PMv")], [k_("YN")], LH, banks=[bM])
+        tt(XS[:], QJ[:], PM[:, 0:LH], ALU.min, [k_("QJ"), k_("PMv")], [k_("XS")], LH, 1.0, [bM])
+        ts(T.YQ[:, lanes], XS[:], -16.0, 0.0, ALU.add, ALU.max, [k_("XS")], [k_("YQ")], LH)
         dma("act" if h else "sp", T.yq[:, lanes], T.YQ[:, lanes], [k_("YQ")], [k_("yq")], 65536)
 
     runs = [half(h) for h in range(H)]
@@ -428,11 +488,14 @@ def plan_ops(g, T, topo, core, rank):
             for o in ops[n0:]:
                 o["half"] = h
     e4 = 256 * (STEPS - 1) + LH
-    names = ["MN%d_%d" % (t, h) for t in range(STEPS) for h in range(H)]
-    dma("sp", T.mn[:, 0:e4], T.MN[:, 0:e4], names[:-1], ["mn0"], 262144)
-    dma("act", T.mn[:, e4:256 * STEPS], T.MN[:, e4:256 * STEPS], names[-1:], ["mn1"], 32768)
+    names = ["AM%d_%d" % (t, h) for t in range(STEPS) for h in range(H)]
+    e3 = e4 - LH
+    dma("sp", T.mn[:, 0:e3], T.M[:, M0:M0 + e3], names[:-2], ["mn0"], 262144)
+    dma("sp", T.mn[:, e3:256 * STEPS], T.M[:, M0 + e3:M0 + 256 * STEPS], names[-2:], ["mn1"], 65536)
     for x in range(4):
-        dma("act" if x % 2 else "sp", T.ys[:, 256 * x:256 * (x + 1)], T.YS[x::16, :], ["YS%d" % h for h in range(H)], ["ys%d" % x], 8192)
+        src = T.YN[0::16, :] if x == 2 else T.YS[x::16, :]
+        dma("act" if x % 2 else "sp", T.ys[:, 256 * x:256 * (x + 1)], src,
+            [("YN%d" if x == 2 else "YS%d") % h for h in range(H)], ["ys%d" % x], 8192)
     return ops
 
 
@@ -505,33 +568,58 @@ def schedule(eng, cost, succ, npred, rdy0, tail, prio):
     return out, start, end
 
 
-def order(ops):
+def replay(seq, eng, cost, lat, pred):
+    fin, start, free, end = [0.0] * len(seq), [0.0] * len(seq), [0.0] * 5, 0.0
+    for i in seq:
+        t = free[eng[i]]
+        for j, d in pred[i]:
+            if fin[j] + d > t:
+                t = fin[j] + d
+        start[i] = t
+        t += cost[i]
+        fin[i] = t
+        free[eng[i]] = t
+        if t + lat[i] > end:
+            end = t + lat[i]
+    return start, end
+
+
+def order(ops, variants):
     n = len(ops)
     names = ["pe", "dve", "act", "pool", "sp"]
     eng = [names.index(o["eng"]) for o in ops]
-    cost = [o["cost"] for o in ops]
-    lat = [o["lat"] for o in ops]
-    succ, pred = [[] for _ in range(n)], [[] for _ in range(n)]
-    for i, o in enumerate(ops):
-        for j in sorted(o["hard"]):
-            succ[j].append((i, lat[j] + HOP))
-            pred[i].append((j, lat[j] + HOP))
-        for j in sorted(o["soft"]):
-            succ[j].append((i, 0.0))
-            pred[i].append((j, 0.0))
-    np_, ns_, zero = [len(p) for p in pred], [len(s) for s in succ], [0.0] * n
-    fwd = lambda pr: schedule(eng, cost, succ, np_, zero, lat, pr)
-    bwd = lambda pr: schedule(eng, cost, pred, ns_, lat, zero, pr)
+    sets = []
+    for v, plan in zip(variants, PLANS):
+        cost, lat = [o["cost"] for o in v], [o["lat"] for o in v]
+        succ, pred = [[] for _ in range(n)], [[] for _ in range(n)]
+        for i, o in enumerate(ops):
+            for j in sorted(o["hard"]):
+                succ[j].append((i, lat[j] + plan[3]))
+                pred[i].append((j, lat[j] + plan[3]))
+            for j in sorted(o["soft"]):
+                succ[j].append((i, 0.0))
+                pred[i].append((j, 0.0))
+        sets.append((cost, lat, succ, pred))
+    np_, ns_, zero = [len(p) for p in sets[0][3]], [len(s) for s in sets[0][2]], [0.0] * n
+    scale = [sum(s[0]) for s in sets]
+
+    def judge(seq):
+        runs = [replay(seq, eng, s[0], s[1], s[3]) for s in sets]
+        return seq, runs, sum(r[1] * scale[0] / c for r, c in zip(runs, scale)) / len(sets)
+
+    cost, lat, succ, pred = sets[0]
     prio = [0.0] * n
     for i in range(n - 1, -1, -1):
         prio[i] = cost[i] + max([prio[j] + d for j, d in succ[i]] + [lat[i]])
     rng = np.random.default_rng(CFG["seed"])
-    best = fwd([prio[i] - CFG["bias"] * ops[i]["half"] for i in range(n)])
+    best = judge(schedule(eng, cost, succ, np_, zero, lat, [prio[i] - CFG["bias"] * ops[i]["half"] for i in range(n)])[0])
     cur = best
     for k in range(CFG["tries"]):
+        m = k % len(sets)
+        cost, lat, succ, pred = sets[m]
         noise = (rng.normal(0.0, CFG["noise"], n) * (rng.random(n) < CFG["share"])).tolist()
-        back = bwd([cur[1][i] + cost[i] + noise[i] for i in range(n)])
-        got = fwd([back[1][i] + cost[i] for i in range(n)])
+        back = schedule(eng, cost, pred, ns_, lat, zero, [cur[1][m][0][i] + cost[i] + noise[i] for i in range(n)])
+        got = judge(schedule(eng, cost, succ, np_, zero, lat, [back[1][i] + cost[i] for i in range(n)])[0])
         if got[2] <= cur[2] + CFG["temp"] * (1.0 - k / CFG["tries"]) * rng.exponential():
             cur = got
             if got[2] < best[2]:
@@ -549,7 +637,7 @@ def rank_program(g, core, T, topo):
     ops = plan_ops(g, T, topo, core, rank)
     link(ops)
     if "seq" not in ORDER:
-        ORDER["seq"] = order(ops)[0]
+        ORDER["seq"] = order(ops, [plan_ops(g, T, topo, core, rank, m) for m in range(len(PLANS))])[0]
     queue = {"pe": g.tensor, "dve": g.vector, "act": g.scalar, "pool": g, "sp": g.sync}
     count = {"pe": 0, "dve": 0, "act": 0, "pool": 0}
     seen = dict((e, {}) for e in queue)

@@ -10,49 +10,59 @@ CA = LH // 16
 NB = LH // 32
 STEPS = 5
 NC_, NS, NF = 3072, 2560, 1536
-M0 = 16 + NF
-GBW = 6152
-TCH = 4
-CFG = {"fc": "act", "nch": "dve", "ins": "dve", "f": "dve", "pneg": "dve", "gg": "act", "bias": 2000.0, "tries": 6000, "seed": 1, "t0dve": 2, "ech": 2, "ovh": 3.0,
-       "temp": 150.0, "noise": 1000.0, "share": 0.05}
+Z0 = 16 + NC_
+ZW = Z0 + 256
+TOP, ULP = 2.0 ** 20, 2.0 ** 13
+SIG = 2.0 ** 23
+MID = 1536.0
+TCH = NB
+TB = 6
+CFG = {"nv": "act", "hi": "act", "xh": "act", "yn": "pe", "ync": "act", "nu": "pe", "gs": "act",
+       "om": "vvvvv", "fg": 1.0, "tt": "aaaaav", "bt": "avavav", "c2": "vaavaa", "tdve": [1, 1, 0, 0, 0, 0, 0, 0, 0, 0],
+       "bias": 2000.0, "tries": 1500, "seed": 1, "ovh": 3.0,
+       "temp": 150.0, "noise": 1000.0, "share": 0.05, "wait": 0.5, "gap": 0.0, "polish": 14000, "reach": 8, "heat": 25.0}
+IDS = {"one": 1.0, "neg": -1.0, "hi": -0.25 / ULP, "sig": SIG,
+       "p512": 512.0, "n512": -512.0, "n496": -496.0, "n32": -32.0, "p256": 256.0, "p16k": 16384.0}
 
 SCRATCH = {
-    "CL": ("sbuf", [128, NS], "int32"),
+    "CL": ("sbuf", [128, ZW], "int32"),
     "PT": ("sbuf", [128, NC_], "bfloat16"),
-    "TT": ("sbuf", [128, 16 + NC_], "bfloat16"),
-    "I1": ("sbuf", [128, 128], "bfloat16"),
-    "SWB": ("sbuf", [128, 320], "bfloat16"),
-    "I13": ("sbuf", [128, 128], "bfloat16"),
-    "I31": ("sbuf", [128, 128], "bfloat16"),
-    "C5": ("sbuf", [128, LH], "bfloat16"),
-    "GB": ("sbuf", [128, GBW], "float32"),
-    "M": ("sbuf", [128, M0 + STEPS * 256], "bfloat16"),
+    "TT": ("sbuf", [128, Z0], "bfloat16"),
+    "BT": ("sbuf", [128, Z0], "bfloat16"),
+    "C2": ("sbuf", [128, ZW], "float32"),
+    "M": ("sbuf", [128, NF + STEPS * 256], "bfloat16"),
     "BG": ("sbuf", [128, 384], "int32"),
-    "BF": ("sbuf", [128, 384], "float32"),
+    "BF": ("sbuf", [128, 12, 32], "float32"),
+    "BY": ("sbuf", [128, 24, 16], "float32"),
+    "BL": ("sbuf", [128, 2, 192], "uint16"),
     "QI": ("sbuf", [128, 256], "int32"),
     "SR": ("sbuf", [128, 256], "int32"),
     "PI": ("sbuf", [128, 8], "int32"),
     "PF": ("sbuf", [128, 16], "float32"),
     "IU": ("sbuf", [128, 160], "float32"),
-    "BW": ("sbuf", [128, 144], "bfloat16"),
-    "I40": ("sbuf", [128, 128], "bfloat16"),
-    "IB": ("sbuf", [128, 128], "bfloat16"),
-    "IH": ("sbuf", [128, 128], "bfloat16"),
+    "ID": ("sbuf", [128, 128 * len(IDS)], "bfloat16"),
     "IF": ("sbuf", [128, 128], "float32"),
+    "BW": ("sbuf", [128, 288], "bfloat16"),
     "SW0": ("sbuf", [128, 160], "float32"),
     "SW1": ("sbuf", [128, 160], "float32"),
-    "ZC": ("sbuf", [128, 3 * LH], "bfloat16"),
+    "SH": ("sbuf", [128, 320], "float16"),
+    "C5": ("sbuf", [128, LH], "bfloat16"),
+    "CW": ("sbuf", [128, 6 * CA], "bfloat16"),
+    "LS": ("sbuf", [128, 2], "uint16"),
+    "CN": ("sbuf", [128, LH], "bfloat16"),
+    "L2": ("sbuf", [128, 128], "bfloat16"),
     "SEG": ("sbuf", [128, LH], "float32"),
+    "ZI": ("sbuf", [128, 3 * LH], "float32"),
+    "ZC": ("sbuf", [128, 3 * LH], "bfloat16"),
     "RK": ("sbuf", [128, LH], "float32"),
-    "KI": ("sbuf", [128, STEPS * 256], "float32"),
     "KEY": ("sbuf", [128, STEPS * 256], "float32"),
-    "GO": ("sbuf", [128, 256], "bfloat16"),
+    "G8": ("sbuf", [128, 512], "bfloat16"),
     "GM": ("sbuf", [128, 2048], "bfloat16"),
     "DG": ("sbuf", [128, 128], "bfloat16"),
-    "RM": ("sbuf", [128, 16], "float32"),
     "YN": ("sbuf", [128, 256], "float32"),
-    "N40": ("sbuf", [128, 128], "bfloat16"),
+    "YG": ("sbuf", [128, 256], "float32"),
     "OUT": ("sbuf", [128, STEPS * 256], "bfloat16"),
+    "MN": ("sbuf", [128, (STEPS - 1) * 256], "bfloat16"),
     "FS": ("sbuf", [128, STEPS * H * CA], "bfloat16"),
     "FR": ("sbuf", [128, STEPS * H * CA], "bfloat16"),
     "YQ": ("sbuf", [128, 256], "float32"),
@@ -60,16 +70,20 @@ SCRATCH = {
 }
 for _h in range(H):
     for _n, _w, _d in (
-        ("T", 16 * LH, "bfloat16"), ("E", 16 * LH, "bfloat16"),
-        ("C16", LH, "uint16"), ("KF", LH, "float32"), ("MS", LH, "bfloat16"), ("T1", LH, "bfloat16"), ("U", LH, "bfloat16"),
-        ("TR", LH, "float32"), ("SC", LH, "float32"), ("GG", LH, "float32"), ("GT", LH, "float32"),
-        ("Q", LH + 8, "float32"), ("XS", LH, "float32"), ("QJ", LH, "int32"), ("YT", LH, "float32"),
-        ("RH", 3 * CA, "bfloat16"), ("SB", 10 * CA, "bfloat16"), ("SF", 10 * CA, "float32"),
-        ("SI", 8 * CA, "int32"), ("SU", 4 * CA, "uint16"),
+        ("C16", LH, "uint16"), ("SC", LH, "float32"), ("MS", LH, "bfloat16"), ("T1", LH, "bfloat16"),
+        ("TR", LH, "float32"), ("GT", LH, "float32"),
+        ("Q", LH + 8, "float32"), ("XS", LH, "float32"), ("QJ", LH, "int32"), ("YT", LH, "float16"),
+        ("RH", 3 * CA, "bfloat16"), ("SB", 10 * CA, "bfloat16"), ("SF", 6 * CA, "float32"), ("SU", 4 * CA, "uint16"),
+        ("SI", 4 * CA, "int32"),
     ):
         SCRATCH["%s%d" % (_n, _h)] = ("sbuf", [128, _w], _d)
+    SCRATCH["T%d" % _h] = ("sbuf", [128, TCH, 16 * LH // TCH], "bfloat16")
+    SCRATCH["E%d" % _h] = ("sbuf", [128, LH, 16], "bfloat16")
+    SCRATCH["KF%d" % _h] = ("sbuf", [128, NB, 32], "float16")
+    SCRATCH["KT%d" % _h] = ("sbuf", [128, NB, 32], "float16")
+    SCRATCH["K2%d" % _h] = ("sbuf", [128, NB, 32], "float16")
     SCRATCH["A3%d" % _h] = ("sbuf", [128, NB, 32], "float32")
-    SCRATCH["B3%d" % _h] = ("sbuf", [128, NB, 32], "float32")
+    SCRATCH["B3%d" % _h] = ("sbuf", [128, NB, 32], "float16")
     SCRATCH["PS%d" % _h] = ("psum", [128, 512], "float32")
     SCRATCH["PM%d" % _h] = ("psum", [128, 512], "float32")
     SCRATCH["PZ%d" % _h] = ("psum", [128, 512], "float32")
@@ -80,17 +94,8 @@ SEMAPHORES = (["pe", "dve", "act", "pool", "left"] + ["d%d" % i for i in range(N
               + ["am%d_%d" % (t, h) for t in range(STEPS) for h in range(H)]
               + ["af%d_%d" % (t, h) for t in range(STEPS) for h in range(H)])
 
-G_ = 1.55
-CY = 0.88
-PC = 0.46
-HOP = 120.0
-BW_ = 260.0
-FIRST = 3000.0
-
-
-RL = 1.0
-PLANS = ((G_, CY, PC, HOP, BW_, FIRST, RL), (1.15, 0.9, 0.46, 100.0, 300.0, 2000.0, 0.9), (2.0, 1.1, 0.56, 150.0, 230.0, 4000.0, 1.25),
-         (1.55, 1.2, 0.62, 150.0, 230.0, 3000.0, 1.1))
+PLANS = ((1.55, 0.88, 0.46, 120.0, 260.0, 3000.0, 1.0), (1.15, 0.9, 0.46, 100.0, 300.0, 2000.0, 0.9),
+         (2.05, 1.15, 0.6, 140.0, 250.0, 3000.0, 1.1), (1.5, 1.15, 0.6, 140.0, 240.0, 3000.0, 1.1))
 
 
 def plan_ops(g, T, topo, core, rank, plan=0):
@@ -128,6 +133,14 @@ def plan_ops(g, T, topo, core, rank, plan=0):
     def ac(out, a, func, bias, scale, r, w, n, c=1.0, banks=()):
         op("act", lambda: A.activation(out, a, func, bias=bias, scale=scale), r, w, vc(n, c) + (60 if c > 1 else 0), banks)
 
+    def mv(who, out, a, r, w, n, c=1.0, banks=(), bias=0.0):
+        if who[0] == "a":
+            ac(out, a, AF.Identity, bias, 1.0, r, w, n, c, banks)
+        elif bias:
+            ts(out, a, bias, None, ALU.add, None, r, w, n + (40 if c > 1 else 0), c, banks)
+        else:
+            cp(out, a, r, w, n + (40 if c > 1 else 0), c, banks)
+
     def mm(lst, r, w, banks):
         calls = []
         cost = 0.0
@@ -152,31 +165,38 @@ def plan_ops(g, T, topo, core, rank, plan=0):
             nbytes = loaded[0]
         op(q, lambda: e.dma_start(out, in_), r, w, 60.0, ["loads_" + q] if load else [], kind="d", lat=1800 + nbytes / BW_)
 
+    names = list(IDS)
+    I_ = dict((n, T.ID[:, 128 * i:128 * (i + 1)]) for i, n in enumerate(names))
+
     hc = NC_ // 2
     ms(T.SR[:], 0, ["SR"], 256)
+    for x, src in enumerate((T.bo, T.gs)):
+        dma("act" if x else "sp", T.BG[:, 192 * x:192 * (x + 1)], src[:], [], ["BG%d" % x], 98304, True)
     for k in range(2):
         dma("act" if k else "sp", T.PT[:, k * hc:(k + 1) * hc], T.pt[:, k * hc:(k + 1) * hc], [], ["PT%d" % k], 393216, True)
     for x, src in enumerate((T.s0, T.p0, T.n0, T.w0)):
         dma("act" if x % 2 else "sp", T.SR[x::16, :], src[:], ["SR"], ["SR%d" % x], 8192, True)
-    dma("sp", T.QI[:], T.q0[:], [], ["QI"], 131072, True)
     for k in range(2):
         dma("act" if k else "sp", T.CL[:, k * 1280:(k + 1) * 1280], T.cl[:, k * 1280:(k + 1) * 1280], [], ["CL%d" % k], 655360, True)
-    dma("act", T.M[:, 16:M0], T.m0[:], [], ["Mi"], 393216, True)
-    for x, src in enumerate((T.bo, T.gs)):
-        for ga in range(2):
-            dma("sp", T.BG[64 * ga:64 * ga + 64, 192 * x:192 * (x + 1)], src[ga::2, :], [], ["BG%d%d" % (x, ga)], 49152, True)
-    cp(T.BF[:], T.BG[:], ["BG00", "BG01", "BG10", "BG11"], ["BF"], 384)
+    dma("sp", T.QI[:], T.q0[:], [], ["QI"], 131072, True)
+    dma("act", T.M[:, 0:NF], T.m0[:], [], ["Mi"], 393216, True)
 
     PI, PF = T.PI, T.PF
     io(PI[:, 0:1], [[0, 1]], 0, 1, ["pi"], 1, flt=False)
     io(T.IU[:], [[1, 160]], 0, 0, ["IU"], 160)
-    io(T.RK[:], [[0, CA], [4096, 16]], 16 - 65536, 0, ["RK"], LH)
-    io(T.ZC[:, 2 * LH:3 * LH], [[0, CA], [2, 16]], -1, 0, ["ZC1"], LH)
-    io(T.ZC[:, 0:2 * LH], [[0, 2 * CA], [-2, 16]], -1, 0, ["ZC0"], 2 * LH)
-    io(T.KI[:], [[16, STEPS * 16], [0, 16]], M0, 1, ["KI"], STEPS * 256)
-    io(T.GB[:, 2052:GBW], [[0, GBW - 2052]], 0, 0, ["GBa"], GBW - 2052)
-    ms(T.GB[:, 4:2052], 0.0, ["GBb"], 2048)
-    ms(T.M[:, 0:16], 2.0 ** 64, ["Md"], 8)
+    io(T.CN[:], [[0, CA], [-4, 16]], 65, 0, ["CN"], LH)
+    io(T.RK[:], [[0, CA], [int(ULP), 16]], int(TOP), 0, ["RK"], LH)
+    io(T.ZI[:, 0:LH], [[0, CA], [-32, 16]], 16, 0, ["ZI0"], LH)
+    io(T.ZI[:, LH:2 * LH], [[0, CA], [2, 16]], -31, 0, ["ZI1"], LH)
+    io(T.ZI[:, 2 * LH:3 * LH], [[0, CA], [32, 16]], -2000, 0, ["ZI2"], LH)
+    io(PI[:, 4:6], [[0, 2]], 0, 1, ["pl"], 2, flt=False)
+    key0 = int(TOP + 16 * ULP) + NF
+    io(T.KEY[:], [[16, STEPS * 16], [0, 16]], key0, 1, ["KEY"], STEPS * 256)
+    io(T.CL[:, NS:ZW], [[0, ZW - NS]], 0, 0, ["CLx"], ZW - NS, flt=False)
+    ms(T.G8[:], 8192.0, ["G8"], 256)
+    for c in range(4):
+        op("pool", lambda c=c: g.affine_select(T.GM[:, 512 * c:512 * (c + 1)], T.G8[:], [[-1, 4], [-16, 8], [0, 16]], ALU.is_equal, 0.0, -4 * c, 1),
+           ["G8"], ["GM%d" % c, "pool_order"], 170 + 2 * 512 * CY)
     ts(PI[:, 1:2], PI[:, 0:1], 15, None, ALU.bitwise_and, None, ["pi"], ["pb"], 1)
     ts(PI[:, 2:3], PI[:, 0:1], 4, 1, ALU.arith_shift_right, ALU.bitwise_and, ["pi"], ["pg"], 1)
     cp(PF[:, 0:3], PI[:, 0:3], ["pi", "pb", "pg"], ["pf"], 3)
@@ -184,318 +204,321 @@ def plan_ops(g, T, topo, core, rank, plan=0):
     ts(PF[:, 4:5], PF[:, 3:4], -1.0, 15.0, ALU.mult, ALU.add, ["ng"], ["g15"], 1)
     ts(PF[:, 5:6], PF[:, 0:1], 16.0, None, ALU.add, None, ["pf"], ["p16"], 1)
     ts(PF[:, 6:7], PF[:, 2:3], -1.0, 1.0, ALU.mult, ALU.add, ["pf"], ["ev"], 1)
-    ts(PF[:, 7:8], PF[:, 1:2], -8192.0, float(15 * 8192 + 4 - 2 ** 21), ALU.mult, ALU.add, ["pf"], ["k0"], 1)
-    ts(PF[:, 8:9], PF[:, 2:3], float(NC_), PF[:, 7:8], ALU.mult, ALU.add, ["pf", "k0"], ["kcol"], 1)
     ts(T.SW0[:], T.IU[:], PF[:, 5:6], PF[:, 6:7], ALU.is_equal, ALU.mult, ["IU", "p16", "ev"], ["SW0"], 160)
     ts(T.SW1[:], T.IU[:], PF[:, 5:6], PF[:, 2:3], ALU.is_equal, ALU.mult, ["IU", "p16", "pf"], ["SW1"], 160)
-    ts(T.IB[:], T.IU[:, 0:128], PF[:, 0:1], -2.0 ** 18, ALU.is_equal, ALU.mult, ["IU", "pf"], ["IB"], 128)
-    ts(T.IH[:], T.IB[:], 0.5, None, ALU.mult, None, ["IB"], ["IH"], 64)
-    ts(T.I40[:], T.IB[:], -2.0 ** -58, None, ALU.mult, None, ["IB"], ["I40"], 64)
     ts(T.IF[:], T.IU[:, 0:128], PF[:, 0:1], None, ALU.is_equal, None, ["IU", "pf"], ["IF"], 128)
-    ts(T.BW[:], T.IU[:, 0:144], PF[:, 4:5], 2.0 ** 17, ALU.is_equal, ALU.mult, ["IU", "g15"], ["BW"], 144)
+    for n in names:
+        ac(I_[n], T.IF[:], AF.Identity, 0.0, IDS[n], ["IF"], ["I" + n], 128)
+    ts(T.BW[:, 0:144], T.IU[:, 0:144], PF[:, 4:5], TOP, ALU.is_equal, ALU.mult, ["IU", "g15"], ["BW"], 144)
+    ts(T.BW[:, 144:288], T.BW[:, 0:144], -2.0 ** -60, None, ALU.mult, None, ["BW"], ["BV"], 72)
     ms(T.SEG[:], 1.0, ["SEG"], LH)
     ms(T.SEG[:, 0::16], 0.0, ["SEG"], CA)
-    for t in range(STEPS):
-        ac(T.KEY[:, 256 * t:256 * (t + 1)], T.KI[:, 256 * t:256 * (t + 1)], AF.Identity, PF[:, 3:4], 1.0, ["KI", "ng"], ["KEY%d" % t], 256)
-    ms(T.TT[:, 0:16], 0.0, ["TTd"], 16)
-    ts(T.N40[:], T.IB[:], 2.0 ** -58, None, ALU.mult, None, ["IB"], ["N40"], 64)
+    ms(T.CN[0:32, :], -15 * TOP / ULP, ["CN"], 64)
+    ms(T.CN[64:128, :], MID / ULP / 2, ["CN"], 64)
+    for al in range(2):
+        cp(T.SH[:, 160 * al:160 * (al + 1)], T["SW%d" % al][:], ["SW%d" % al], ["SH%d" % al], 160)
+    ms(T.L2[:], ULP / 32, ["L2"], 64)
     ms(T.C5[:], 512.0, ["C5"], 64)
-    ts(PF[:, 9:10], PF[:, 1:2], 2.0, 4112.0, ALU.is_ge, ALU.mult, ["pf"], ["dum"], 1)
-    ts(T.GB[:, 0:4], T.IU[:, 0:4], -16.0, PF[:, 9:10], ALU.min, ALU.add, ["IU", "dum"], ["GBd"], 4)
-    cp(T.SWB[:, 0:160], T.SW0[:], ["SW0"], ["SWB0"], 160)
-    cp(T.SWB[:, 160:320], T.SW1[:], ["SW1"], ["SWB1"], 160)
-    ts(T.GO[:, 0:128], T.IU[:, 0:128], PF[:, 3:4], 0.0, ALU.add, ALU.is_ge, ["IU", "ng"], ["GO0"], 128)
-    ts(T.GO[:, 128:256], T.IU[:, 0:128], PF[:, 4:5], None, ALU.is_le, None, ["IU", "g15"], ["GO1"], 128)
-    tt(T.GO[:, 0:128], T.GO[:, 0:128], T.GO[:, 128:256], ALU.mult, ["GO0", "GO1"], ["GO0"], 128)
-    ts(T.RM[:], T.IU[:, 0:16], PF[:, 1:2], 8192.0, ALU.is_equal, ALU.mult, ["IU", "pf"], ["RM"], 16)
-    ts(PF[:, 10:11], PF[:, 1:2], -16.0, -8.0, ALU.mult, ALU.add, ["pf"], ["dg"], 1)
+    ms(T.CW[:], 0.0, ["CW"], 24)
+    for i, v in ((0, 49.25), (1, -8448.0), (5, 512.0)):
+        ms(T.CW[:, i * CA:(i + 1) * CA], v, ["CW"], 8)
+    ts(PI[:, 4:6], PI[:, 4:6], CA - 1, None, ALU.bitwise_and, None, ["pl"], ["pl"], 2)
+    cp(T.LS[:], PI[:, 4:6], ["pl"], ["LS"], 2)
+    ms(T.TT[:, 0:16], 0.0, ["TTd"], 16)
+    ms(T.BT[:, 0:16], 0.0, ["BTd"], 16)
+    ms(T.C2[:, 0:16], 0.0, ["C2d"], 16)
+    ms(T.C2[:, Z0:ZW], 0.0, ["C2z0", "C2z1"], 256)
+    ac(T.ZC[:], T.ZI[:], AF.Identity, 0.0, 0.5, ["ZI0", "ZI1", "ZI2"], ["ZC"], 3 * LH)
+    ts(PF[:, 7:8], PF[:, 3:4], -1.0, None, ALU.mult, None, ["ng"], ["pg16"], 1)
+    ts(PF[:, 10:11], PF[:, 1:2], -16.0, None, ALU.mult, None, ["pf"], ["dg"], 1)
     ts(T.DG[:], T.IU[:, 0:128], PF[:, 0:1], PF[:, 10:11], ALU.is_equal, ALU.mult, ["IU", "pf", "dg"], ["DG"], 128)
-    for j in range(16):
-        ac(T.GM[:, 128 * j:128 * (j + 1)], T.GO[:, 0:128], AF.Identity, 0.0, T.RM[:, j:j + 1], ["GO0", "RM"], ["GM%d" % j], 128)
-    ts(T.I13[:], T.IB[:], 2.0 ** -5, None, ALU.mult, None, ["IB"], ["I13"], 64)
-    ts(T.I1[:], T.IB[:], -2.0 ** -18, None, ALU.mult, None, ["IB"], ["I1"], 64)
-    ts(T.I31[:], T.IB[:], 2.0 ** -49, None, ALU.mult, None, ["IB"], ["I31"], 64)
-    ttk = []
+
+    def swap(PX, src3, lo, nb, r, w, bank, narrow=False):
+        lst = []
+        for al in range(2):
+            SW, c0 = (T.SH, 160 * al) if narrow else (T["SW%d" % al], 0)
+            for ga in range(2):
+                off = c0 + 16 - 16 * (ga - al)
+                lst.append((PX[:, lo:lo + nb, 16 * al:16 * al + 16], SW[:, off:off + 128],
+                            src3[:, :, 16 * ga:16 * ga + 16], ga == 0, ga == 1, 16 * nb, not narrow))
+        mm(lst, r + ["SW0", "SW1", "SH0", "SH1"], w, [bank])
+
+    cp(T.BF[:], T.BG[:], ["BG0", "BG1"], ["BF"], 384)
+    swap(T.PX0, T.BF, 0, 12, ["BF"], ["Xb"], "PX0")
+    op("dve", lambda: V.transpose(T.BY[:], T.PX0[:, 0:12, :]), ["Xb"], ["BY"], vc(384), ["PX0"])
+    blk = []
+    for a in range(12):
+        cp(T.BL[:, :, a::12], T.BY[:, a::12, :], ["BY"], ["BL%d" % a], 32)
+        blk.append("BL%d" % a)
+    ttk = ["TTd"]
     for k in range(6):
         cs = slice(512 * k, 512 * (k + 1))
         cd = slice(16 + 512 * k, 16 + 512 * (k + 1))
-        bk = ("PS0", "PM0", "PS1", "PM1")[k % 4]
+        bk = ("PZ0", "PM0", "PZ1", "PM1")[k % 4]
         src = "PT%d" % (k // 3)
-        ac(T[bk][:, 0:512], T.PT[:, cs], AF.Relu, -254.0 * 2.0 ** 40, 2.0 ** 40, [src], ["V" + bk], 512, banks=[bk])
-        tt(T.TT[:, cd], T.PT[:, cs], T[bk][:, 0:512], ALU.max, [src, "V" + bk], ["TT%d" % k], 512, 1.0, [bk])
+        ts(T.TT[:, cd], T.PT[:, cs], 255.0, -2.0 ** 60, ALU.is_ge, ALU.mult, [src], ["TT%d" % k], 512, 0.5)
+        mm([(T[bk][:, 0:512], I_["one"], T.PT[:, cs], True, False, 512, False), (T[bk][:, 0:512], I_["one"], T.TT[:, cd], False, True, 512, False)],
+           [src, "TT%d" % k, "Ione"], ["V" + bk], [bk])
+        mv(CFG["tt"][k], T.TT[:, cd], T[bk][:, 0:512], ["V" + bk], ["TT%d" % k], 512, banks=[bk])
         ttk.append("TT%d" % k)
-    gbt = ["GBb"]
-    for al in range(2):
-        for ga in range(2):
-            for x in range(2):
-                tok = "GB%d%d%d" % (al, ga, x)
-                gbt.append(tok)
-                dma("sp", T.GB[16 * al + x::32, 4 + ga * NC_:4 + (ga + 1) * NC_], T.BF[64 * ga:64 * ga + 64, 192 * x:192 * (x + 1)],
-                    ["GBa", "GBb", "BF"], [tok], 200000)
+    btk, c2k = ["BTd"], ["C2d"]
+    wc = NC_ // TB
+    for k in range(TB):
+        cd = slice(16 + wc * k, 16 + wc * (k + 1))
+        lo, hi_ = wc * k // 16, wc * (k + 1) // 16
+        body = T.TT[:, 16:Z0].indirect(T.BL[:, 0, lo:hi_])
+        if CFG["bt"][k] == "a":
+            ac(T.BT[:, cd], body, AF.Identity, 0.0, -1.0, ttk + blk, ["BT%d" % k], wc, G_)
+        else:
+            ts(T.BT[:, cd], body, -1.0, None, ALU.mult, None, ttk + blk, ["BT%d" % k], wc + 40, G_)
+        mv(CFG["c2"][k], T.C2[:, cd], T.CL[:, 0:NS].indirect(T.BL[:, 1, lo:hi_]), ["CL0", "CL1"] + blk, ["C2%d" % k], wc, G_, bias=16.0)
+        btk.append("BT%d" % k)
+        c2k.append("C2%d" % k)
+    c2k += ["C2z%d" % h for h in range(H)]
 
-    def swap_big(h, src3, lo, r, w):
-        PX = T["PX%d" % h]
-        lst = []
-        for al in range(2):
-            SW = T.SW1 if al else T.SW0
-            for ga in range(2):
-                off = 16 - 16 * (ga - al)
-                lst.append((PX[:, lo:lo + NB, 16 * al:16 * al + 16], SW[:, off:off + 128],
-                            src3[:, :, 16 * ga:16 * ga + 16], ga == 0, ga == 1, LH // 2, True))
-        mm(lst, r + ["SW0", "SW1"], w, ["PX%d" % h])
+    def states():
+        dma("sp", T.CL[0::16, 16:Z0], T.gs[:], ["CLx"], ["CL0", "CL1"], 98304)
+        dma("sp", T.CL[0::16, Z0:ZW], T.s0[:], ["CLx"], ["GSb"], 8192)
 
     def half(h):
         S = str(h)
         b = lambda n: T[n + S]
-        M, Tg, E, C16, KF, MS, T1 = T.M, b("T"), b("E"), b("C16"), b("KF"), b("MS"), b("T1")
-        TR, SC, GG, GT, Q, XS, QJ, YT = b("TR"), b("SC"), b("GG"), b("GT"), b("Q"), b("XS"), b("QJ"), b("YT")
-        RH, SB, SF, SI, SU = b("RH"), b("SB"), b("SF"), b("SI"), b("SU")
+        M, Tg, E, C16, KF, KT, MS, T1 = T.M, b("T"), b("E"), b("C16"), b("KF"), b("KT"), b("MS"), b("T1")
+        TR, SC, GT, Q, XS, QJ, YT = b("TR"), b("SC"), b("GT"), b("Q"), b("XS"), b("QJ"), b("YT")
+        RH, SB, SF, SU = b("RH"), b("SB"), b("SF"), b("SU")
         A3, B3, PS, PM, PZ, PX = b("A3"), b("B3"), b("PS"), b("PM"), b("PZ"), b("PX")
         col = lambda buf, i: buf[:, i * CA:(i + 1) * CA]
         k_ = lambda n: n + S
-        rho, n1, pneg = col(RH, 0), col(RH, 1), col(RH, 2)
-        n_, wz, act, nr, dd, nu, fw = [col(SB, i) for i in range(7)]
-        fwv = [SB[:, 6 * CA + ga:7 * CA:2] for ga in range(2)]
-        both = SF[:, 0:2 * CA]
-        p1, sA = SF[:, 0:2 * CA:2], SF[:, 1:2 * CA:2]
-        kept = [SF[:, 2 * CA * u:2 * CA * (u + 1)] for u in (1, 2)]
-        pA, pB = SF[:, 2 * CA:4 * CA:2], SF[:, 4 * CA:6 * CA:2]
-        sms = [SF[:, 2 * CA + 1:4 * CA:2], SF[:, 4 * CA + 1:6 * CA:2]]
-        U = b("U")
-        ci, ix, w_, xk, xi = [col(SI, i) for i in range(5)]
-        nfb = GT[:, 2::16]
-        su, iu, bu, xu = [col(SU, i) for i in range(4)]
-        pp = [(pA, k_("pA")), (pB, k_("pB"))]
+        p_, m1, ny = col(RH, 0), col(RH, 1), col(RH, 2)
+        act, m_, nr, wz, xh, n1, wr, hi = [col(SB, i) for i in range(8)]
+        xf, nh, none = [col(SF, i) for i in range(3)]
+        bu, zu, xu = [col(SU, i) for i in range(3)]
+        SI, K2 = b("SI"), b("K2")
+        zi = col(SI, 3)
         lanes = slice(h * LH, (h + 1) * LH)
         bS, bM, bZ, bX = k_("PS"), k_("PM"), k_("PZ"), k_("PX")
-        s_ = sA
+        strip = lambda r, lo, n=1: PX[:, r, lo * CA:(lo + n) * CA]
+        sW = strip(1, 0)
 
-        ms(Q[:, LH:LH + 8], -1.0e6, [k_("Qpad")], 8)
-        ms(YT[:], 0.0, [k_("YT")], LH)
+        def mixed(src, r, step=1):
+            buf, c0 = (GT, 0) if step > 1 else (SI, 3 * CA)
+            half_ = CA // 2
+            op("dve", [(lambda al=al: V.tensor_copy(SU[:, CA + al:2 * CA:2], buf[:, c0 + step * half_ * al:c0 + step * half_ * (al + 1):step]))
+                       for al in range(2)], [r], [k_("zu")], 2 * vc(CA))
+
+        ms(Q[:, LH:LH + 8], 0.0, [k_("Qpad")], 8)
+        ts(YT[:], T.C5[:], 0.0, None, ALU.mult, None, ["C5"], [k_("YT")], LH, 0.5)
 
         cp(A3[:], T.SR[:, lanes], ["SR", "SR0", "SR1", "SR2", "SR3"], [k_("A3")], LH)
-        swap_big(h, A3, 0, [k_("A3")], [k_("X0")])
-        op("dve", [(lambda a=a: V.transpose(GT[:, 32 * a:32 * a + 32], PX[:, a, :])) for a in range(NB)],
-           [k_("X0")], [k_("GT")], NB * vc(32), [bX])
-        cp(su, GT[:, 0::16], [k_("GT")], [k_("su")], CA)
-        cp(B3[:], T.QI[:, lanes], ["QI"], [k_("B3")], LH)
-        swap_big(h, B3, NB, [k_("B3")], [k_("X1")])
-        ac(s_, GT[:, 0::16], AF.Identity, 0.0, 1.0, [k_("GT")], [k_("s")], CA)
-        ac(pA, GT[:, 1::16], AF.Identity, 0.0, 1.0, [k_("GT")], [k_("pA")], CA)
-        ac(pneg, GT[:, 1::16], AF.Identity, 0.0, -1.0, [k_("GT")], [k_("pneg")], CA)
-        ac(n_, GT[:, 2::16], AF.Identity, 0.0, 1.0, [k_("GT")], [k_("n")], CA)
-        cp(w_, GT[:, 3::16], [k_("GT")], [k_("w")], CA)
-        op("dve", [(lambda a=a: V.transpose(TR[:, 32 * a:32 * a + 32], PX[:, NB + a, :])) for a in range(NB)],
-           [k_("X1")], [k_("TR")], NB * vc(32), [bX])
-        tt(Q[:, 0:LH], TR[:], T.RK[:], ALU.add, [k_("TR"), "RK"], [k_("Q")], LH)
-
-        def lin(who, out, a, sc, bi, r, w):
-            if CFG[who] == "act":
-                ac(out, a, AF.Identity, bi, sc, r, w, CA)
-            else:
-                ts(out, a, sc, bi, ALU.mult, ALU.add, r, w, CA)
+        swap(PX, A3, 0, NB, [k_("A3")], [k_("X0")], bX)
+        op("dve", lambda: V.transpose(GT[:], PX[:, 0:NB, :]), [k_("X0")], [k_("GT")], vc(LH), [bX])
+        mixed(GT[:, 0::16], k_("GT"), 16)
+        ts(B3[:], T.QI[:, lanes], PF[:, 7:8], None, ALU.add, None, ["QI", "pg16"], [k_("B3")], LH)
+        op("dve", lambda: V.transpose(K2[:], B3[:]), [k_("B3")], [k_("K2")], vc(LH, 0.5))
+        swap(PX, K2, NB, NB, [k_("K2")], [k_("X1")], bX, True)
+        ac(p_, GT[:, 1::16], AF.Identity, 0.0, 16.0, [k_("GT")], [k_("p")], CA)
+        ac(m1, GT[:, 2::16], AF.Identity, 16.0, -1.0, [k_("GT")], [k_("m1")], CA)
+        ts(nr, GT[:, 3::16], 32.0, None, ALU.is_lt, None, [k_("GT")], [k_("nr")], CA)
+        tt(wz, GT[:, 3::16], nr, ALU.mult, [k_("GT"), k_("nr")], [k_("wz")], CA)
+        ts(zi, T.KEY[:, h * LH:(h + 1) * LH:16], PF[:, 3:4], float(Z0 - key0), ALU.add, ALU.add, ["KEY", "ng"], [k_("zi")], CA)
+        tt(Q[:, 0:LH], T.RK[:], PX[:, NB:2 * NB, :], ALU.add, [k_("X1"), "RK"], [k_("Q")], LH, 1.0, [bX])
 
         def bcast(lo, hi_, r):
-            lst = [(PZ[:, lo * LH:hi_ * LH], T.IH[:], T.ZC[:, lo * LH:hi_ * LH], True, False, (hi_ - lo) * LH, False)]
-            mm(lst, ["IH", "ZC0", "ZC1"], [k_("Z%d_" % q) for q in range(lo, hi_)], [bZ])
-            lst = [(PZ[:, lo * LH + j:hi_ * LH:16], T.IB[:], RH[:, lo * CA:hi_ * CA], False, j == 15, CA, False) for j in range(16)]
-            mm(lst, r + ["IB"], [k_("Z%d_" % q) for q in range(lo, hi_)], [bZ])
+            zt = [k_("Z%d_" % q) for q in range(lo, hi_)]
+            mm([(PZ[:, lo * LH:hi_ * LH], I_["sig"], T.ZC[:, lo * LH:hi_ * LH], True, False, (hi_ - lo) * LH, False)],
+               ["Isig", "ZC"], zt, [bZ])
+            mm([(PZ[:, lo * LH + j:hi_ * LH:16], I_["sig"], RH[:, lo * CA:hi_ * CA], False, j == 15, CA, False) for j in range(16)],
+               r + ["Isig"], zt, [bZ])
 
         def select():
-            op("dve", lambda: V.tensor_tensor_scan(XS[:], PZ[:, 2 * LH:3 * LH], Q[:, 0:LH], 0.0, ALU.max, ALU.min),
-               [k_("Z2_"), k_("Q")], [k_("XS")], vc(LH), [bZ])
+            op("dve", lambda: V.tensor_tensor_scan(XS[:], PZ[:, 0:LH], Q[:, 0:LH], 0.0, ALU.max, ALU.min),
+               [k_("Z0_"), k_("Q")], [k_("XS")], vc(LH), [bZ])
+            mv(CFG["xh"], xh, XS[:, 15::16], [k_("XS")], [k_("xh")], CA)
+            tt(xf, XS[:, 15::16], xh, ALU.subtract, [k_("XS"), k_("xh")], [k_("xf")], CA)
+            ts(xu, xf, PF[:, 3:4], None, ALU.add, None, [k_("xf"), "ng"], [k_("xu")], CA)
 
-        def ready(p_, pk):
-            ts(nr, w_, 32.0, None, ALU.is_lt, None, [k_("w")], [k_("nr")], CA)
-            tt(dd, n_, p_, ALU.subtract, [k_("n"), pk], [k_("dd")], CA)
-            tt(act, dd, nr, ALU.min, [k_("dd"), k_("nr")], [k_("act")], CA)
-            tt(xk, XS[:, 15::16], act, ALU.mult, [k_("XS"), k_("act")], [k_("xk")], CA)
-            ts(xi, xk, 4095, None, ALU.bitwise_and, None, [k_("xk")], [k_("xi")], CA)
-            cp(xu, xi, [k_("xi")], [k_("xu")], CA)
-            tt(p1, p_, act, ALU.add, [pk, k_("act")], [k_("p1")], CA)
-            tt(wz, w_, nr, ALU.mult, [k_("w"), k_("nr")], [k_("wz")], CA)
+        def linear(terms, r, w, start, stop):
+            mm([(strip(row, lo, n), I_[f], src, start and i == 0, stop and i == len(terms) - 1, n * CA, False)
+                for i, (row, lo, n, f, src) in enumerate(terms)], r + ["I" + x[3] for x in terms], w, [bX])
 
-        bcast(2, 3, [k_("pneg")])
+        def ready(a_, at):
+            terms = [(2, 0, 2, "one", T.CW[:, CA:3 * CA]), (2, 0, 1, "n496", m1), (2, 0, 1, "n32", p_), (2, 0, 1, "p16k", nr),
+                     (2, 1, 1, "one", m1)]
+            linear(terms, ["CW", k_("m1"), k_("p"), k_("nr")], [k_("Xd")], True, a_ is None)
+            if a_ is not None:
+                linear([(2, 0, 1, "p256", a_), (2, 1, 1, "neg", a_)], [at], [k_("Xd")], False, True)
+            ts(SB[:, 0:2 * CA], strip(2, 0, 2), 16.0, 0.0, ALU.min, ALU.max, [k_("Xd")], [k_("act")], CA, banks=[bX])
+            if CFG["nv"] == "act":
+                ac(nh, act, AF.Identity, TOP + 69 * ULP, -65.0 / 16 * ULP, [k_("act")], [k_("nh")], CA)
+            else:
+                ts(nh, act, -65.0 / 16 * ULP, TOP + 69 * ULP, ALU.mult, ALU.add, [k_("act")], [k_("nh")], CA)
+            tt(none, nh, zi, ALU.add, [k_("nh"), k_("zi")], [k_("nv")], CA)
+            linear([(0, 0, 3, "one", T.CW[:, 3 * CA:6 * CA]), (0, 0, 2, "one", SB[:, 0:2 * CA]), (0, 0, 1, "one", p_),
+                    (0, 2, 1, "neg", act), (0, 2, 1, "neg", p_)], ["CW", k_("act"), k_("p")], [k_("Xy")], True, False)
+
+        bcast(0, 1, [k_("p")])
         select()
-        ready(*pp[0])
+        ready(None, None)
 
         for t in range(STEPS):
             yield
             last = t == STEPS - 1
-            p_, pk = pp[t % 2]
-            pn, pnk = pp[(t + 1) % 2]
             dst = T.cores[(rank + 1 + t % (N - 1)) % N]
             rid, pid, _ = topo.addr(dst)
             engs = topo.engines(core, dst)
             mask = sum(1 << e for e in engs)
             neng = len(engs)
             first = FIRST if t == 0 and h == 0 else 0.0
-            cp(C16[:], T.CL[:, 0:NS].indirect(su), ["CL0", "CL1", k_("su")], [k_("C16")], LH + 40, G_)
+            if t == 0:
+                mv("v", C16[:], T.CL[:, 0:NS].indirect(zu), ["CL0", "CL1", k_("zu")], [k_("C16")], LH, G_, bias=16.0)
+            else:
+                mv("v", C16[:], T.C2[:, 0:ZW].indirect(zu), c2k + [k_("zu")], [k_("C16")], LH, G_)
+            ts(KF[:], C16[:], -MID, None, ALU.add, None, [k_("C16")], [k_("KF")], LH, 0.5)
+            if t == 0:
+                own = Z0 + h * LH
+                op("dve", [(lambda al=al: V.tensor_scalar(T.C2[:, own + 64 * al:own + 64 * al + 64], KF[:, :, 16 * al:16 * al + 16],
+                                                          MID, None, ALU.add)) for al in range(2)], [k_("KF")], ["C2z" + S], 2 * vc(64))
             lc = LH // TCH
             tk = [k_("T%d_" % c) for c in range(TCH)]
             for c in range(TCH):
-                o_ = Tg[:, 16 * lc * c:16 * lc * (c + 1)]
-                i_ = T.TT[:, 16:16 + NC_].indirect(C16[:, lc * c:lc * (c + 1)])
-                if t == 0 and h == 0 and c >= TCH - CFG["t0dve"]:
-                    ts(o_, i_, 2.0 ** -40, None, ALU.mult, None, ttk + [k_("C16")], [tk[c]], 16 * lc + 40, G_)
-                else:
-                    ac(o_, i_, AF.Identity, 0.0, 2.0 ** -40, ttk + [k_("C16")], [tk[c]], 16 * lc, G_)
-            ts(KF[:], C16[:], PF[:, 8:9], None, ALU.add, None, [k_("C16"), "kcol"], [k_("KF")], LH)
-            wend = M0 if t == 0 else M0 + 256 * (t - 1) + LH * (h + 1)
-            rd = ["Md", "Mi", k_("xu")] + ["AM%d_%d" % (u, o) for u in range(t) for o in range(H) if u < t - 1 or o <= h]
-            ac(MS[:], M[:, 0:wend].indirect(xu), AF.Identity, 0.0, 1.0, rd, [k_("MS")], LH, G_)
-            mm([(PM[:, 0:LH], T.I40[:], MS[:], True, True, LH, False)], [k_("MS"), "I40"], [k_("PMv")], [bM])
-            mm([(PS[:, 0:LH], T.IF[:], KF[:], True, False, LH, True)], [k_("KF"), "IF"], [k_("S")], [bS])
-            ech = CFG["ech"]
-            le, per = LH // ech, 2 * ech
-            for e in range(ech):
-                tke = tk[e * TCH // ech:(e + 1) * TCH // ech]
-                lo, hi_ = e * le, (e + 1) * le
-                for c in range(4):
-                    mm([(PS[:, lo:hi_], T.BW[:, 15 - k:143 - k], Tg[:, 16 * lo + k:16 * hi_:16], False, False, le, False)
-                        for k in range(4 * c, 4 * c + 4)], tke + ["BW"], [k_("S")], [bS])
-                if e == 0:
-                    mm([(PS[:, 0:LH], T.N40[:], MS[:], False, False, LH, False)], [k_("MS"), "N40"], [k_("S")], [bS])
-                for c in range(16 // per):
-                    ks = range(per * c, per * (c + 1))
-                    et = k_("E%d_%d_" % (e, c))
-                    op("dve", [(lambda k=k, lo=lo, hi_=hi_: V.tensor_tensor(
-                        E[:, k * LH + lo:k * LH + hi_], Tg[:, 16 * lo + k:16 * hi_:16], PM[:, lo:hi_], ALU.is_equal)) for k in ks],
-                       tke + [k_("PMv")], [et], per * (vc(le) + CFG["ovh"]), [bM])
-                    mm([(PS[:, lo:hi_], T.BW[:, 15 - k:143 - k], E[:, k * LH + lo:k * LH + hi_], False,
-                         k == 15 and e == ech - 1, le, False) for k in ks], [et, "BW"], [k_("S")], [bS])
-            op("dve", lambda: V.transpose(TR[:], PS[:, 0:LH]), [k_("S")], [k_("TR")], vc(LH), [bS])
-            op("dve", lambda: V.tensor_tensor_scan(SC[:], T.SEG[:], TR[:], 0.0, ALU.mult, ALU.max),
-               [k_("TR"), "SEG"], [k_("SC")], vc(LH))
-            cp(ci, SC[:, 15::16], [k_("SC")], [k_("ci")], CA)
-            ts(ix, ci, 8191, None, ALU.bitwise_and, None, [k_("ci")], [k_("ix")], CA)
-            cp(iu, ix, [k_("ix")], [k_("iu")], CA)
-            if CFG["gg"] == "act":
-                ac(GG[:], T.GB[:, 0:GBW].indirect(iu), AF.Identity, 0.0, 1.0, ["GBa", "GBd", k_("iu")] + gbt, [k_("GG")], LH, G_)
-            else:
-                cp(GG[:], T.GB[:, 0:GBW].indirect(iu), ["GBa", "GBd", k_("iu")] + gbt, [k_("GG")], LH + 40, G_)
-            op("dve", lambda: V.transpose(GT[:], GG[:]), [k_("GG")], [k_("GT")], vc(LH))
-            lst = []
+                who = "v" if c >= TCH - CFG["tdve"][H * t + h] else "a"
+                mv(who, Tg[:, c, :], T.TT[:, 0:Z0].indirect(C16[:, lc * c:lc * (c + 1)]),
+                   ttk + [k_("C16")], [tk[c]], 16 * lc, G_)
+            op("dve", lambda: V.transpose(KT[:], KF[:]), [k_("KF")], [k_("KT")], vc(LH, 0.5))
+            wend = NF if t == 0 else NF + 256 * (t - 1) + LH * (h + 1)
+            rd = ["Mi", k_("xu")] + ["AM%d_%d" % (u, o) for u in range(t) for o in range(H) if u < t - 1 or o <= h]
+            ac(MS[:], M[:, 0:wend].indirect(xu), AF.Abs, 0.0, 1.0, rd, [k_("MS")], LH, G_)
+            mm([(PM[:, 0:LH], I_["one"], MS[:], True, True, LH, False)], [k_("MS"), "Ione"], [k_("PMv")], [bM])
+            mm([(PS[:, 0:LH], T.L2[:], T.CN[:], True, False, LH, False)], ["L2", "CN"], [k_("S0")], [bS])
+            parts = []
+
+            def part(lst, r):
+                parts.append(k_("Sp%d_" % len(parts)))
+                mm(lst, r + [k_("S0")], [parts[-1]], [])
+
             for al in range(2):
-                SW = T.SW1 if al else T.SW0
-                for ga in range(2):
-                    off = 16 - 16 * (ga - al)
-                    lst.append((PX[:, 0, al:CA:2], SW[:, off:off + 128], SC[:, 15 + 16 * ga::32], False, al + ga == 2, NB, True))
-            so = PX[:, 0, 0:CA]
+                part([(PS[:, 64 * al:64 * al + 64], T.SH[:, 160 * al + 16 - 16 * (ga - al):160 * al + 144 - 16 * (ga - al)],
+                       KT[:, :, 16 * ga:16 * ga + 16], False, False, LH // 2, False) for ga in range(2)], [k_("KT"), "SH0", "SH1"])
+            ech, le = 2, LH // 2
+            for e in range(ech):
+                lo, hi_ = e * le, (e + 1) * le
+                so = PS[:, lo:hi_]
+                for c in range(4):
+                    part([(so, T.BW[:, 159 - j:287 - j], Tg[:, :, 256 * e + 16 * j:256 * e + 16 * j + 16], False, False, le, False)
+                          for j in range(4 * c, 4 * c + 4)], tk + ["BV"])
+                et = []
+                for c in range(4):
+                    et.append(k_("E%d_%d_" % (e, c)))
+                    op("dve", [(lambda k=k, lo=lo, hi_=hi_, e=e: V.tensor_tensor(
+                        E[:, lo:hi_, k], Tg[:, :, 256 * e + k:256 * (e + 1):16], PM[:, lo:hi_], ALU.is_equal))
+                               for k in range(4 * c, 4 * c + 4)], tk + [k_("PMv")], [et[c]], 4 * (vc(le) + CFG["ovh"]), [bM])
+                for c in range(4):
+                    end = e == ech - 1 and c == 3
+                    lst = [(so, T.BW[:, 15 - j:143 - j], E[:, lo + j:hi_:16, :], False, end and j == 15, le, False)
+                           for j in range(4 * c, 4 * c + 4)]
+                    if end:
+                        mm(lst, et + parts + ["BW"], [k_("S")], [bS])
+                    else:
+                        part(lst, et + ["BW"])
+            op("dve", lambda: V.tensor_tensor_scan(SC[:], T.SEG[:], PS[:, 0:LH], 0.0, ALU.mult, ALU.max),
+               [k_("S"), "SEG"], [k_("SC")], vc(LH), [bS])
+            tt(col(SI, 0), SC[:, 15::16], nh, ALU.max, [k_("SC"), k_("nh")], [k_("cb")], CA)
+            tt(col(SI, 1), SC[:, 15::16], none, ALU.max, [k_("SC"), k_("nv")], [k_("cz")], CA)
+            ts(SI[:, 2 * CA:4 * CA], SI[:, 0:2 * CA], 4095, None, ALU.bitwise_and, None, [k_("cb"), k_("cz")], [k_("zi")], CA)
+            if last:
+                cp(SU[:, 0:2 * CA], SI[:, 2 * CA:4 * CA], [k_("zi")], [k_("zu"), k_("bu")], CA)
+            else:
+                cp(bu, col(SI, 2), [k_("zi")], [k_("bu")], CA)
+                mixed(zi, k_("zi"))
+            if CFG["hi"] == "act":
+                mv("a", SB[:, 7 * CA:9 * CA], SI[:, 0:CA].indirect(T.LS[:, 0:1]), [k_("cb"), "LS"], [k_("hi")], 2 * CA, G_)
+            else:
+                tt(hi, SC[:, 15::16], nh, ALU.max, [k_("SC"), k_("nh")], [k_("hi")], CA)
             fc = slice((t * H + h) * CA, (t * H + h + 1) * CA)
             f_, a_ = T.FS[:, fc], T.FR[:, fc]
             ft = k_("f%d_" % t)
-            if CFG["f"] == "act":
-                ac(fw, SC[:, 15::16], AF.Sign, 0.0, 1.0, [k_("SC")], [k_("fw")], CA)
-            else:
-                ts(fw, SC[:, 15::16], 0.5, None, ALU.is_gt, None, [k_("SC")], [k_("fw")], CA)
-            mm([(PX[:, 1, al:CA:2], T.SWB[:, 160 * al + 16 - 16 * (ga - al):160 * al + 144 - 16 * (ga - al)], fwv[ga],
-                 ga == 0, ga == 1, NB, False) for al in range(2) for ga in range(2)], [k_("fw"), "SWB0", "SWB1"], [k_("Xf")], [bX])
-            if CFG["fc"] == "act":
-                ac(f_, PX[:, 1, 0:CA], AF.Identity, 0.0, 1.0, [k_("Xf")], [ft], CA, banks=[bX])
-            else:
-                cp(f_, PX[:, 1, 0:CA], [k_("Xf")], [ft], CA, banks=[bX])
-            mm([(so, T.I13[:], wz, True, False, CA, False), (so, T.IH[:], act, False, False, CA, False)],
-               [k_("wz"), k_("act"), "I13", "IH"], [k_("X0")], [bX])
-            mm(lst, [k_("SC"), "SW0", "SW1"], [k_("X0")], [bX])
-            ts(w_, so, -2.0 ** -13, 0.375, ALU.mult, ALU.add, [k_("X0")], [k_("w")], CA, banks=[bX])
+            tt(f_, SC[:, 15::16], nh, ALU.is_gt, [k_("SC"), k_("nh")], [ft], CA)
             op("pool", lambda f_=f_, a_=a_, t=t, pid=pid, rid=rid, mask=mask: g.remote_dma(
                 a_, f_, T.sem["af%d_%d" % (t, h)], T.sem.left, pid, rid, mask),
                [ft], [k_("AF%d_" % t)], 300.0 + first, kind="r", lat=2000.0 * RL, sem=("af%d_%d" % (t, h), neng))
-            ts(bu, GT[:, 0::16], 16.0, None, ALU.add, None, [k_("GT")], [k_("bu")], CA)
-            sm = sms[(t + 1) % 2]
-            tt(kept[(t + 1) % 2], both, GT[:, 4::8], ALU.min, [k_("s"), k_("p1"), k_("GT")], [pnk], 2 * CA)
-            if last:
-                tt(YT[:, 0::16], GT[:, 1::16], sm, ALU.max, [k_("GT"), pnk, k_("YT")], [k_("Y0")], CA)
-            else:
-                tt(s_, GT[:, 1::16], sm, ALU.max, [k_("GT"), pnk], [k_("s")], CA)
-                cp(su, s_, [k_("s")], [k_("su")], CA)
             oc = slice(256 * t + h * LH, 256 * t + (h + 1) * LH)
             ot = k_("O%d_" % t)
-            ac(T1[:], T.TT[:, 0:16 + NC_].indirect(bu), AF.Identity, 0.0, 1.0, ttk + ["TTd", k_("bu")], [k_("T1")], LH, G_)
-            mm([(PS[:, LH:2 * LH], T.I1[:], T.C5[:], True, False, LH, False),
-                (PS[:, LH:2 * LH], T.I1[:], MS[:], False, False, LH, False)], ["I1", "C5", k_("MS")], [k_("B")], [bS])
-            mm([(PS[:, LH:2 * LH], T.I31[:], T1[:], False, True, LH, False)], ["I31", k_("T1")], [k_("B")], [bS])
-            tt(T.OUT[:, oc], T1[:], PS[:, LH:2 * LH], ALU.min, [k_("T1"), k_("B")], [ot], LH, 1.0, [bS])
-            land = M[:, M0 + oc.start:M0 + oc.stop]
+            sent, st = (T1[:], k_("T1")) if last else (T.OUT[:, oc], ot)
+            if CFG["om"][t] == "v":
+                tt(sent, T.BT[:, 0:Z0].indirect(bu), MS[:], ALU.min, btk + [k_("bu"), k_("MS")], [st], LH + 40, max(G_, CFG["fg"]))
+            else:
+                mv("a", TR[:], T.BT[:, 0:Z0].indirect(bu), btk + [k_("bu")], [k_("TR")], LH, G_)
+                tt(sent, TR[:], PM[:, 0:LH], ALU.min, [k_("TR"), k_("PMv")], [st], LH, 1.0, [bM])
+            if last:
+                ac(T.OUT[:, oc], sent, AF.Abs, 0.0, 1.0, [st], [ot], LH)
+            land = M[:, NF + oc.start:NF + oc.stop]
             op("pool", lambda land=land, oc=oc, t=t, pid=pid, rid=rid, mask=mask: g.remote_dma(
                 land, T.OUT[:, oc], T.sem["am%d_%d" % (t, h)], T.sem.left, pid, rid, mask),
                [ot], [k_("AM%d_" % t)], 300.0, kind="r", lat=2300.0 * RL, sem=("am%d_%d" % (t, h), neng))
-            if last:
-                cp(YT[:, 3::16], w_, [k_("w"), k_("YT")], [k_("Y3")], CA)
-            tt(rho, p_, nfb, ALU.max, [pk, k_("GT")], [k_("rho")], CA)
-            pe_n = CFG["nch"] == "pe" and not last
-            sn = PX[:, 1, 0:CA]
-            if pe_n:
-                mm([(sn, T.IB[:], n_, True, False, CA, False), (sn, T.IP[:], f_, False, True, CA, False)],
-                   [k_("n"), ft, "IB", "IP"], [k_("Xn")], [bX])
-                ac(n1, sn, AF.Identity, 0.0, -2.0 ** -18, [k_("Xn")], [k_("n1")], CA, banks=[bX])
+            linear([(0, 0, 1, "n512", f_), (0, 1, 1, "one", f_), (0, 2, 1, "p512", f_)], [ft], [k_("Xy")], False, True)
+            if CFG["ync"] == "act":
+                ac(RH[:], strip(0, 0, 3), AF.Relu, 0.0, 1.0, [k_("Xy")], [k_("p"), k_("m1"), k_("ny")], CA, banks=[bX])
             else:
-                tt(n1, n_, f_, ALU.subtract, [k_("n"), ft], [k_("n1")], CA)
-            if last:
-                ac(YT[:, 1::16], pn, AF.Identity, 0.0, 1.0, [pnk, k_("YT")], [k_("Y1")], CA)
-                bcast(0, 2, [k_("rho"), k_("n1")])
-            else:
-                lin("pneg", pneg, pn, -1.0, 0.0, [pnk], [k_("pneg")])
-                bcast(0, 3, [k_("rho"), k_("n1"), k_("pneg")])
-            tt(PZ[:, 0:LH], PZ[:, 0:LH], Q[:, 1:LH + 1], ALU.min, [k_("Z0_"), k_("Q"), k_("Qpad")], [k_("Z0_")], LH, 1.0, [bZ])
-            if CFG["ins"] == "act":
-                tt(Q[:, 0:LH], Q[:, 0:LH], PZ[:, 0:LH], ALU.max, [k_("Z0_"), k_("Q")], [k_("Q")], LH, 1.0, [bZ])
-                ac(U[:], PZ[:, LH:2 * LH], AF.Relu, 0.0, -2.0 ** -18, [k_("Z1_")], [k_("U")], LH, banks=[bZ])
-                mm([(PM[:, LH:2 * LH], T.IF[:], T.KEY[:, oc], True, False, LH, True)], ["IF", "KEY%d" % t], [k_("Yk")], [bM])
-                mm([(PM[:, LH:2 * LH], T.IB[:], U[:], False, True, LH, False)], ["IB", k_("U")], [k_("Yk")], [bM])
-                tt(Q[:, 0:LH], Q[:, 0:LH], PM[:, LH:2 * LH], ALU.max, [k_("Yk"), k_("Q")], [k_("Q")], LH, 1.0, [bM])
-            else:
-                tt(PZ[:, LH:2 * LH], PZ[:, LH:2 * LH], T.KEY[:, oc], ALU.min, [k_("Z1_"), "KEY%d" % t], [k_("Z1_")], LH, 1.0, [bZ])
-                tt(Q[:, 0:LH], Q[:, 0:LH], PZ[:, 0:LH], ALU.max, [k_("Z0_"), k_("Q")], [k_("Q")], LH, 1.0, [bZ])
-                tt(Q[:, 0:LH], Q[:, 0:LH], PZ[:, LH:2 * LH], ALU.max, [k_("Z1_"), k_("Q")], [k_("Q")], LH, 1.0, [bZ])
+                ts(RH[:], strip(0, 0, 3), 0.0, None, ALU.max, None, [k_("Xy")], [k_("p"), k_("m1"), k_("ny")], CA, banks=[bX])
+            bcast(1 if last else 0, 3, [k_("p"), k_("m1"), k_("ny")])
+            z2 = PZ[:, 2 * LH:3 * LH]
+            tt(z2, z2, Q[:, 1:LH + 1], ALU.min, [k_("Z2_"), k_("Q"), k_("Qpad")], [k_("Z2_")], LH, 1.0, [bZ])
+            tt(PZ[:, LH:2 * LH], PZ[:, LH:2 * LH], T.KEY[:, oc], ALU.min, [k_("Z1_"), "KEY"], [k_("Z1_")], LH, 1.0, [bZ])
+            tt(Q[:, 0:LH], Q[:, 0:LH], z2, ALU.max, [k_("Z2_"), k_("Q")], [k_("Q")], LH, 1.0, [bZ])
+            tt(Q[:, 0:LH], Q[:, 0:LH], PZ[:, LH:2 * LH], ALU.max, [k_("Z1_"), k_("Q")], [k_("Q")], LH, 1.0, [bZ])
             if not last:
                 select()
-            if pe_n:
-                mm([(sn, T.IB[:], a_, False, True, CA, False)], [k_("AF%d_" % t), "IB"], [k_("Xn")], [bX])
-                ac(nu, sn, AF.Relu, 16.0, 2.0 ** -18, [k_("Xn")], [k_("nu")], CA, banks=[bX])
-                ac(n_, nu, AF.Identity, 16.0, -1.0, [k_("nu")], [k_("n")], CA)
+            linear([(1, 0, 1, "one", T.CW[:, 0:CA]), (1, 0, 1, "one", wz), (1, 0, 1, "hi", hi)], ["CW", k_("wz"), k_("hi")], [k_("Xw")], True, True)
+            if last:
+                ac(wr, sW, AF.Identity, 127.75, 1.0, [k_("Xw")], [k_("wr")], CA, banks=[bX])
+                ts(YT[:, 3::16], wr, -128.0, None, ALU.add, None, [k_("wr"), k_("YT")], [k_("Y3")], CA)
+                ts(YT[:, 1::16], p_, 1.0 / 16, None, ALU.mult, None, [k_("p"), k_("YT")], [k_("Y1")], CA)
+                ac(n1, m1, AF.Identity, 16.0, -1.0, [k_("m1")], [k_("n1")], CA)
+                mv(CFG["gs"], T.YG[:, lanes], T.CL[:, 0:ZW].indirect(zu), ["CL0", "CL1", "GSb", k_("zu")], [k_("YG")], LH, G_)
             else:
-                tt(nu, n1, a_, ALU.add, [k_("n1"), k_("AF%d_" % t)], [k_("nu")], CA)
-                if not last:
-                    ts(n_, nu, 16.0, None, ALU.min, None, [k_("nu")], [k_("n")], CA)
-            if not last:
-                ready(pn, pnk)
+                ts(nr, sW, 32.0, None, ALU.is_lt, None, [k_("Xw")], [k_("nr")], CA, banks=[bX])
+                tt(wz, nr, sW, ALU.mult, [k_("Xw"), k_("nr")], [k_("wz")], CA, 1.0, [bX])
+                ready(a_, k_("AF%d_" % t))
 
-        ts(n_, nu, 16.0, None, ALU.min, None, [k_("nu")], [k_("n")], CA)
-        mm([(PM[:, 0:LH], T.DG[:], T.C5[:], True, False, LH, False)], ["DG", "C5"], [k_("PMv")], [bM])
-        mm([(PM[:, j:LH:16], T.GM[:, 128 * j:128 * (j + 1)], n_, False, j == 15, CA, False) for j in range(16)],
-           [k_("n")] + ["GM%d" % j for j in range(16)], [k_("PMv")], [bM])
-        op("dve", [(lambda a=a: V.transpose(A3[:, a, :], YT[:, 32 * a:32 * a + 32])) for a in range(NB)],
-           [k_("Y0"), k_("Y1"), k_("Y3")], [k_("A3")], NB * vc(32))
-        swap_big(h, A3, 0, [k_("A3")], [k_("X0")])
+        gm = ["GM%d" % j for j in range(4)]
+        mm([(PS[:, 0:LH], T.DG[:], T.C5[:], True, False, LH, False)], ["DG", "C5"], [k_("S0")], [bS])
+        mm([(PS[:, j:LH:16], T.GM[:, 128 * j:128 * (j + 1)], n1, False, False, CA, False) for j in range(16)],
+           [k_("n1"), k_("S0")] + gm, [k_("S1")], [bS])
+        mm([(PS[:, j:LH:16], T.GM[:, 128 * j:128 * (j + 1)], a_, False, j == 15, CA, False) for j in range(16)],
+           [k_("AF%d_" % t), k_("S1")] + gm, [k_("S")], [bS])
+        op("dve", lambda: V.transpose(KT[:], YT[:]), [k_("Y1"), k_("Y3")], [k_("KT")], vc(LH, 0.5))
+        swap(PX, KT, 0, NB, [k_("KT")], [k_("X0")], bX, True)
         ac(T.YS[:, lanes], PX[:, 0:NB, :], AF.Identity, 0.0, 1.0, [k_("X0")], [k_("YS")], LH, banks=[bX])
-        op("dve", [(lambda a=a: V.transpose(B3[:, a, :], Q[:, 32 * a:32 * a + 32])) for a in range(NB)],
-           [k_("Q")], [k_("B3")], NB * vc(32))
-        swap_big(h, B3, NB, [k_("B3")], [k_("X1")])
-        cp(QJ[:], PX[:, NB:2 * NB, :], [k_("X1")], [k_("QJ")], LH, banks=[bX])
+        cp(QJ[:], Q[:, 0:LH], [k_("Q")], [k_("QJ")], LH)
         ts(QJ[:], QJ[:], 4095, None, ALU.bitwise_and, None, [k_("QJ")], [k_("QJ")], LH)
-        ac(T.YN[:, lanes], PM[:, 0:LH], AF.Identity, 0.5, 2.0 ** -13, [k_("PMv")], [k_("YN")], LH, banks=[bM])
-        tt(XS[:], QJ[:], PM[:, 0:LH], ALU.min, [k_("QJ"), k_("PMv")], [k_("XS")], LH, 1.0, [bM])
-        ts(T.YQ[:, lanes], XS[:], -16.0, 0.0, ALU.add, ALU.max, [k_("XS")], [k_("YQ")], LH)
+        ts(KF[:], QJ[:], PF[:, 3:4], -MID, ALU.add, ALU.add, [k_("QJ"), "ng"], [k_("KF")], LH)
+        op("dve", lambda: V.transpose(K2[:], KF[:]), [k_("KF")], [k_("K2")], vc(LH, 0.5))
+        swap(PX, K2, NB, NB, [k_("K2")], [k_("X1")], bX, True)
+        ac(TR[:], PX[:, NB:2 * NB, :], AF.Identity, MID, 1.0, [k_("X1")], [k_("TR")], LH, banks=[bX])
+        tt(XS[:], TR[:], PS[:, 0:LH], ALU.min, [k_("TR"), k_("S")], [k_("XS")], LH, 1.0, [bS])
+        ts(T.YQ[:, lanes], XS[:], 0.0, None, ALU.max, None, [k_("XS")], [k_("YQ")], LH)
+        ts(T.YN[:, lanes], PS[:, 0:LH], 2.0 ** -13, 16.0, ALU.mult, ALU.min, [k_("S")], [k_("YN")], LH, banks=[bS])
         dma("act" if h else "sp", T.yq[:, lanes], T.YQ[:, lanes], [k_("YQ")], [k_("yq")], 65536)
 
     runs = [half(h) for h in range(H)]
-    for _ in range(STEPS + 1):
+    for turn in range(STEPS + 1):
+        if turn == 2:
+            states()
         for h, r in enumerate(runs):
             n0 = len(ops)
             next(r, None)
             for o in ops[n0:]:
                 o["half"] = h
-    e4 = 256 * (STEPS - 1) + LH
-    names = ["AM%d_%d" % (t, h) for t in range(STEPS) for h in range(H)]
-    e3 = e4 - LH
-    dma("sp", T.mn[:, 0:e3], T.M[:, M0:M0 + e3], names[:-2], ["mn0"], 262144)
-    dma("sp", T.mn[:, e3:256 * STEPS], T.M[:, M0 + e3:M0 + 256 * STEPS], names[-2:], ["mn1"], 65536)
-    for x in range(4):
-        src = T.YN[0::16, :] if x == 2 else T.YS[x::16, :]
-        dma("act" if x % 2 else "sp", T.ys[:, 256 * x:256 * (x + 1)], src,
-            [("YN%d" if x == 2 else "YS%d") % h for h in range(H)], ["ys%d" % x], 8192)
+    arr = ["AM%d_%d" % (t, h) for t in range(STEPS) for h in range(H)]
+    e3 = 256 * (STEPS - 1)
+    for t in range(STEPS - 1):
+        ac(T.MN[:, 256 * t:256 * (t + 1)], T.M[:, NF + 256 * t:NF + 256 * (t + 1)], AF.Abs, 0.0, 1.0, arr[H * t:H * (t + 1)], ["MN%d" % t], 256)
+    dma("sp", T.mn[:, 0:e3], T.MN[:], ["MN%d" % t for t in range(STEPS - 1)], ["mn"], 262144)
+    for h in range(H):
+        dma("sp", T.mn[:, e3 + h * LH:e3 + (h + 1) * LH], T.M[:, NF + e3 + h * LH:NF + e3 + (h + 1) * LH], [arr[h - H]], ["mn%d" % h], 32768)
+    for x, n in enumerate(("YG", "YS", "YN", "YS")):
+        dma("act" if x % 2 else "sp", T.ys[:, 256 * x:256 * (x + 1)], T[n][(x if n == "YS" else 0)::16, :],
+            [n + str(h) for h in range(H)], ["ys%d" % x], 8192)
     return ops
 
 
@@ -531,6 +554,7 @@ def link(ops):
 
 def schedule(eng, cost, succ, npred, rdy0, tail, prio):
     n = len(eng)
+    wait, gap = CFG["wait"], CFG["gap"]
     left = list(npred)
     rdy = list(rdy0)
     free = [0.0] * 5
@@ -552,6 +576,13 @@ def schedule(eng, cost, succ, npred, rdy0, tail, prio):
         for j in pend[e]:
             if rdy[j] <= t0 and prio[j] > bp:
                 i, bp = j, prio[j]
+        soon = t0 + wait * cost[i]
+        bp += gap
+        for j in pend[e]:
+            if rdy[j] < soon and prio[j] > bp:
+                i, bp = j, prio[j]
+        if rdy[i] > t0:
+            t0 = rdy[i]
         pend[e].remove(i)
         fin = t0 + cost[i]
         start[i] = t0
@@ -624,7 +655,89 @@ def order(ops, variants):
             cur = got
             if got[2] < best[2]:
                 best = got
-    return best
+    return judge(polish(best[0], eng, sets, [scale[0] / c / len(sets) for c in scale], rng))
+
+
+def polish(seq, eng, sets, weight, rng):
+    n = len(seq)
+    need = [set(j for j, _ in p) for p in sets[0][3]]
+
+    def run(seq, lo, fins):
+        out, total = [], 0.0
+        for (cost, lat, _, pred), fin0, w in zip(sets, fins, weight):
+            fin = list(fin0)
+            free, end = [0.0] * 5, 0.0
+            for i in seq[:lo]:
+                free[eng[i]] = fin[i]
+            for i in seq[lo:]:
+                t = free[eng[i]]
+                for j, d in pred[i]:
+                    if fin[j] + d > t:
+                        t = fin[j] + d
+                t += cost[i]
+                fin[i] = t
+                free[eng[i]] = t
+            for i in ends:
+                if fin[i] + lat[i] > end:
+                    end = fin[i] + lat[i]
+            out.append(fin)
+            total += w * end
+        return out, total
+
+    ends = [i for i in range(n) if not sets[0][2][i]]
+    fins, cur = run(seq, 0, [[0.0] * n for _ in sets])
+    best, bseq = cur, seq
+    steps = CFG["polish"]
+    pick = rng.random((steps, 4)).tolist()
+    arcs = None
+    for k in range(steps):
+        r = pick[k]
+        if arcs is None:
+            pos, before, last = [0] * n, [-1] * n, [-1] * 5
+            for p, i in enumerate(seq):
+                pos[i] = p
+                before[i] = last[eng[i]]
+                last[eng[i]] = i
+            arcs = []
+            for (cost, lat, _, pred), fin in zip(sets, fins):
+                i = max(ends, key=lambda i: fin[i] + lat[i])
+                while i >= 0:
+                    t, nxt = fin[i] - cost[i] - 1e-6, -1
+                    for j, d in pred[i]:
+                        if fin[j] + d >= t:
+                            nxt = j
+                    if nxt < 0 and before[i] >= 0 and fin[before[i]] >= t:
+                        nxt = before[i]
+                        arcs.append(i)
+                    i = nxt
+            if not arcs:
+                break
+        v = arcs[int(r[0] * len(arcs))]
+        u = before[v]
+        for _ in range(int(r[1] ** 3 * CFG["reach"])):
+            if before[u] >= 0:
+                u = before[u]
+        lo, hi = pos[u], pos[v]
+        ahead, want, seen, ok = [], set(need[v]), set(), True
+        for p in range(hi - 1, lo - 1, -1):
+            i = seq[p]
+            if i in want or eng[i] in seen:
+                if i == u:
+                    ok = False
+                    break
+                ahead.append(i)
+                want |= need[i]
+                seen.add(eng[i])
+        if not ok:
+            continue
+        moved = set(ahead)
+        new = seq[:lo] + ahead[::-1] + [v] + [i for i in seq[lo:hi] if i not in moved] + seq[hi + 1:]
+        nf, val = run(new, lo, fins)
+        if val <= cur - CFG["heat"] * (1.0 - k / steps) * np.log(r[2] + 1e-12):
+            seq, fins, cur, arcs = new, nf, val, None
+            if cur < best:
+                best, bseq = cur, seq
+    return bseq
 
 
 ORDER = {}

import numpy as np
from concourse.bass import DstId, RemoteDMATransfer
from concourse.mybir import dt, AluOpType, AxisListType, ActivationFunctionType

ALU = AluOpType
AF = ActivationFunctionType
H = 2
LH = 256 // H
CA = LH // 16
NB = LH // 32
STEPS = 5
NC_, NS, NF = 3072, 2560, 1536
Z0 = 16 + NC_
ZW = Z0 + 256
TOP, ULP = 2.0 ** 20, 2.0 ** 13
SIG = 2.0 ** 23
MID = 1536.0
TCH = NB
TB = 6
CFG = {"nv": "act", "hi": "act", "xh": "act", "yn": "pe", "ync": "act", "nu": "pe", "gs": "act",
       "om": "vvvvv", "fg": 1.0, "tt": "aaaaav", "bt": "avavav", "c2": "vaavaa", "tdve": [1, 1, 0, 0, 0, 0, 0, 0, 0, 0],
       "bias": 2000.0, "tries": 1500, "seed": 1, "ovh": 3.0,
       "temp": 150.0, "noise": 1000.0, "share": 0.05, "wait": 0.5, "gap": 0.0, "polish": 14000, "reach": 8, "heat": 25.0}
IDS = {"one": 1.0, "neg": -1.0, "hi": -0.25 / ULP, "sig": SIG,
       "p512": 512.0, "n512": -512.0, "n496": -496.0, "n32": -32.0, "p256": 256.0, "p16k": 16384.0}

SCRATCH = {
    "CL": ("sbuf", [128, ZW], "int32"),
    "PT": ("sbuf", [128, NC_], "bfloat16"),
    "TT": ("sbuf", [128, Z0], "bfloat16"),
    "BT": ("sbuf", [128, Z0], "bfloat16"),
    "C2": ("sbuf", [128, ZW], "float32"),
    "M": ("sbuf", [128, NF + STEPS * 256], "bfloat16"),
    "BG": ("sbuf", [128, 384], "int32"),
    "BF": ("sbuf", [128, 12, 32], "float32"),
    "BY": ("sbuf", [128, 24, 16], "float32"),
    "BL": ("sbuf", [128, 2, 192], "uint16"),
    "QI": ("sbuf", [128, 256], "int32"),
    "SR": ("sbuf", [128, 256], "int32"),
    "PI": ("sbuf", [128, 8], "int32"),
    "PF": ("sbuf", [128, 16], "float32"),
    "IU": ("sbuf", [128, 160], "float32"),
    "ID": ("sbuf", [128, 128 * len(IDS)], "bfloat16"),
    "IF": ("sbuf", [128, 128], "float32"),
    "BW": ("sbuf", [128, 288], "bfloat16"),
    "SW0": ("sbuf", [128, 160], "float32"),
    "SW1": ("sbuf", [128, 160], "float32"),
    "SH": ("sbuf", [128, 320], "float16"),
    "C5": ("sbuf", [128, LH], "bfloat16"),
    "CW": ("sbuf", [128, 6 * CA], "bfloat16"),
    "LS": ("sbuf", [128, 2], "uint16"),
    "CN": ("sbuf", [128, LH], "bfloat16"),
    "L2": ("sbuf", [128, 128], "bfloat16"),
    "SEG": ("sbuf", [128, LH], "float32"),
    "ZI": ("sbuf", [128, 3 * LH], "float32"),
    "ZC": ("sbuf", [128, 3 * LH], "bfloat16"),
    "RK": ("sbuf", [128, LH], "float32"),
    "KEY": ("sbuf", [128, STEPS * 256], "float32"),
    "G8": ("sbuf", [128, 512], "bfloat16"),
    "GM": ("sbuf", [128, 2048], "bfloat16"),
    "DG": ("sbuf", [128, 128], "bfloat16"),
    "YN": ("sbuf", [128, 256], "float32"),
    "YG": ("sbuf", [128, 256], "float32"),
    "OUT": ("sbuf", [128, STEPS * 256], "bfloat16"),
    "MN": ("sbuf", [128, (STEPS - 1) * 256], "bfloat16"),
    "FS": ("sbuf", [128, STEPS * H * CA], "bfloat16"),
    "FR": ("sbuf", [128, STEPS * H * CA], "bfloat16"),
    "YQ": ("sbuf", [128, 256], "float32"),
    "YS": ("sbuf", [128, 256], "float32"),
}
for _h in range(H):
    for _n, _w, _d in (
        ("C16", LH, "uint16"), ("SC", LH, "float32"), ("MS", LH, "bfloat16"), ("T1", LH, "bfloat16"),
        ("TR", LH, "float32"), ("GT", LH, "float32"),
        ("Q", LH + 8, "float32"), ("XS", LH, "float32"), ("QJ", LH, "int32"), ("YT", LH, "float16"),
        ("RH", 3 * CA, "bfloat16"), ("SB", 10 * CA, "bfloat16"), ("SF", 6 * CA, "float32"), ("SU", 4 * CA, "uint16"),
        ("SI", 4 * CA, "int32"),
    ):
        SCRATCH["%s%d" % (_n, _h)] = ("sbuf", [128, _w], _d)
    SCRATCH["T%d" % _h] = ("sbuf", [128, TCH, 16 * LH // TCH], "bfloat16")
    SCRATCH["E%d" % _h] = ("sbuf", [128, LH, 16], "bfloat16")
    SCRATCH["KF%d" % _h] = ("sbuf", [128, NB, 32], "float16")
    SCRATCH["KT%d" % _h] = ("sbuf", [128, NB, 32], "float16")
    SCRATCH["K2%d" % _h] = ("sbuf", [128, NB, 32], "float16")
    SCRATCH["A3%d" % _h] = ("sbuf", [128, NB, 32], "float32")
    SCRATCH["B3%d" % _h] = ("sbuf", [128, NB, 32], "float16")
    SCRATCH["PS%d" % _h] = ("psum", [128, 512], "float32")
    SCRATCH["PM%d" % _h] = ("psum", [128, 512], "float32")
    SCRATCH["PZ%d" % _h] = ("psum", [128, 512], "float32")
    SCRATCH["PX%d" % _h] = ("psum", [128, 16, 32], "float32")

NDMA = 40
SEMAPHORES = (["pe", "dve", "act", "pool", "left"] + ["d%d" % i for i in range(NDMA)]
              + ["am%d_%d" % (t, h) for t in range(STEPS) for h in range(H)]
              + ["af%d_%d" % (t, h) for t in range(STEPS) for h in range(H)])

PLANS = ((1.55, 0.88, 0.46, 120.0, 260.0, 3000.0, 1.0), (1.15, 0.9, 0.46, 100.0, 300.0, 2000.0, 0.9),
         (2.05, 1.15, 0.6, 140.0, 250.0, 3000.0, 1.1), (1.5, 1.15, 0.6, 140.0, 240.0, 3000.0, 1.1))


def plan_ops(g, T, topo, core, rank, plan=0):
    G_, CY, PC, _, BW_, FIRST, RL = PLANS[plan]
    ops = []
    N = len(T.cores)

    def op(eng, calls, reads, writes, cost, banks=(), kind="c", lat=0.0, sem=None):
        if not isinstance(calls, list):
            calls = [calls]
        ops.append({"eng": eng, "calls": calls, "r": list(reads), "w": list(writes), "cost": cost,
                    "banks": list(banks), "kind": kind, "lat": lat, "sem": sem, "half": 0})

    V, A, P = g.vector, g.scalar, g.tensor

    def vc(n, c=1.0):
        return max(64.0, n * c) * CY

    def ts(out, in0, s1, s2, o0, o1, r, w, n, c=1.0, banks=()):
        if o1 is None:
            f = lambda: V.tensor_scalar(out, in0, s1, None, o0)
        else:
            f = lambda: V.tensor_scalar(out, in0, s1, s2, o0, o1)
        op("dve", f, r, w, vc(n, c), banks)

    def tt(out, a, b, o, r, w, n, c=2.0, banks=()):
        op("dve", lambda: V.tensor_tensor(out, a, b, o), r, w, vc(n, c), banks)

    def cp(out, a, r, w, n, c=1.0, banks=()):
        op("dve", lambda: V.tensor_copy(out, a), r, w, vc(n, c), banks)

    def ms(ap, v, w, n):
        op("dve", lambda: V.memset(ap, v), [], w, vc(n))

    def ac(out, a, func, bias, scale, r, w, n, c=1.0, banks=()):
        op("act", lambda: A.activation(out, a, func, bias=bias, scale=scale), r, w, vc(n, c) + (60 if c > 1 else 0), banks)

    def mv(who, out, a, r, w, n, c=1.0, banks=(), bias=0.0):
        if who[0] == "a":
            ac(out, a, AF.Identity, bias, 1.0, r, w, n, c, banks)
        elif bias:
            ts(out, a, bias, None, ALU.add, None, r, w, n + (40 if c > 1 else 0), c, banks)
        else:
            cp(out, a, r, w, n + (40 if c > 1 else 0), c, banks)

    def mm(lst, r, w, banks):
        calls = []
        cost = 0.0
        for (o, l, rh, st, sp, n, f4) in lst:
            calls.append(lambda o=o, l=l, rh=rh, st=st, sp=sp: P.matmul(o, l, rh, st, sp))
            cost += max(64, n) * (4 if f4 else 1) * PC
        op("pe", calls, r, w, cost, banks)

    def io(out, pat, base, cm, w, n, flt=True):
        if flt:
            f = lambda: g.iota(out, pat, base, cm, allow_small_or_imprecise_dtypes=True)
        else:
            f = lambda: g.iota(out, pat, base, cm)
        op("pool", f, [], w + ["pool_order"], 130 + 2 * n * CY)

    loaded = [0.0]

    def dma(q, out, in_, r, w, nbytes, load=False):
        e = g.sync if q == "sp" else g.scalar
        if load:
            loaded[0] += nbytes
            nbytes = loaded[0]
        op(q, lambda: e.dma_start(out, in_), r, w, 60.0, ["loads_" + q] if load else [], kind="d", lat=1800 + nbytes / BW_)

    names = list(IDS)
    I_ = dict((n, T.ID[:, 128 * i:128 * (i + 1)]) for i, n in enumerate(names))

    hc = NC_ // 2
    ms(T.SR[:], 0, ["SR"], 256)
    for x, src in enumerate((T.bo, T.gs)):
        dma("act" if x else "sp", T.BG[:, 192 * x:192 * (x + 1)], src[:], [], ["BG%d" % x], 98304, True)
    for k in range(2):
        dma("act" if k else "sp", T.PT[:, k * hc:(k + 1) * hc], T.pt[:, k * hc:(k + 1) * hc], [], ["PT%d" % k], 393216, True)
    for x, src in enumerate((T.s0, T.p0, T.n0, T.w0)):
        dma("act" if x % 2 else "sp", T.SR[x::16, :], src[:], ["SR"], ["SR%d" % x], 8192, True)
    for k in range(2):
        dma("act" if k else "sp", T.CL[:, k * 1280:(k + 1) * 1280], T.cl[:, k * 1280:(k + 1) * 1280], [], ["CL%d" % k], 655360, True)
    dma("sp", T.QI[:], T.q0[:], [], ["QI"], 131072, True)
    dma("act", T.M[:, 0:NF], T.m0[:], [], ["Mi"], 393216, True)

    PI, PF = T.PI, T.PF
    io(PI[:, 0:1], [[0, 1]], 0, 1, ["pi"], 1, flt=False)
    io(T.IU[:], [[1, 160]], 0, 0, ["IU"], 160)
    io(T.CN[:], [[0, CA], [-4, 16]], 65, 0, ["CN"], LH)
    io(T.RK[:], [[0, CA], [int(ULP), 16]], int(TOP), 0, ["RK"], LH)
    io(T.ZI[:, 0:LH], [[0, CA], [-32, 16]], 16, 0, ["ZI0"], LH)
    io(T.ZI[:, LH:2 * LH], [[0, CA], [2, 16]], -31, 0, ["ZI1"], LH)
    io(T.ZI[:, 2 * LH:3 * LH], [[0, CA], [32, 16]], -2000, 0, ["ZI2"], LH)
    io(PI[:, 4:6], [[0, 2]], 0, 1, ["pl"], 2, flt=False)
    key0 = int(TOP + 16 * ULP) + NF
    io(T.KEY[:], [[16, STEPS * 16], [0, 16]], key0, 1, ["KEY"], STEPS * 256)
    io(T.CL[:, NS:ZW], [[0, ZW - NS]], 0, 0, ["CLx"], ZW - NS, flt=False)
    ms(T.G8[:], 8192.0, ["G8"], 256)
    for c in range(4):
        op("pool", lambda c=c: g.affine_select(T.GM[:, 512 * c:512 * (c + 1)], T.G8[:], [[-1, 4], [-16, 8], [0, 16]], ALU.is_equal, 0.0, -4 * c, 1),
           ["G8"], ["GM%d" % c, "pool_order"], 170 + 2 * 512 * CY)
    ts(PI[:, 1:2], PI[:, 0:1], 15, None, ALU.bitwise_and, None, ["pi"], ["pb"], 1)
    ts(PI[:, 2:3], PI[:, 0:1], 4, 1, ALU.arith_shift_right, ALU.bitwise_and, ["pi"], ["pg"], 1)
    cp(PF[:, 0:3], PI[:, 0:3], ["pi", "pb", "pg"], ["pf"], 3)
    tt(PF[:, 3:4], PF[:, 1:2], PF[:, 0:1], ALU.subtract, ["pf"], ["ng"], 1)
    ts(PF[:, 4:5], PF[:, 3:4], -1.0, 15.0, ALU.mult, ALU.add, ["ng"], ["g15"], 1)
    ts(PF[:, 5:6], PF[:, 0:1], 16.0, None, ALU.add, None, ["pf"], ["p16"], 1)
    ts(PF[:, 6:7], PF[:, 2:3], -1.0, 1.0, ALU.mult, ALU.add, ["pf"], ["ev"], 1)
    ts(T.SW0[:], T.IU[:], PF[:, 5:6], PF[:, 6:7], ALU.is_equal, ALU.mult, ["IU", "p16", "ev"], ["SW0"], 160)
    ts(T.SW1[:], T.IU[:], PF[:, 5:6], PF[:, 2:3], ALU.is_equal, ALU.mult, ["IU", "p16", "pf"], ["SW1"], 160)
    ts(T.IF[:], T.IU[:, 0:128], PF[:, 0:1], None, ALU.is_equal, None, ["IU", "pf"], ["IF"], 128)
    for n in names:
        ac(I_[n], T.IF[:], AF.Identity, 0.0, IDS[n], ["IF"], ["I" + n], 128)
    ts(T.BW[:, 0:144], T.IU[:, 0:144], PF[:, 4:5], TOP, ALU.is_equal, ALU.mult, ["IU", "g15"], ["BW"], 144)
    ts(T.BW[:, 144:288], T.BW[:, 0:144], -2.0 ** -60, None, ALU.mult, None, ["BW"], ["BV"], 72)
    ms(T.SEG[:], 1.0, ["SEG"], LH)
    ms(T.SEG[:, 0::16], 0.0, ["SEG"], CA)
    ms(T.CN[0:32, :], -15 * TOP / ULP, ["CN"], 64)
    ms(T.CN[64:128, :], MID / ULP / 2, ["CN"], 64)
    for al in range(2):
        cp(T.SH[:, 160 * al:160 * (al + 1)], T["SW%d" % al][:], ["SW%d" % al], ["SH%d" % al], 160)
    ms(T.L2[:], ULP / 32, ["L2"], 64)
    ms(T.C5[:], 512.0, ["C5"], 64)
    ms(T.CW[:], 0.0, ["CW"], 24)
    for i, v in ((0, 49.25), (1, -8448.0), (5, 512.0)):
        ms(T.CW[:, i * CA:(i + 1) * CA], v, ["CW"], 8)
    ts(PI[:, 4:6], PI[:, 4:6], CA - 1, None, ALU.bitwise_and, None, ["pl"], ["pl"], 2)
    cp(T.LS[:], PI[:, 4:6], ["pl"], ["LS"], 2)
    ms(T.TT[:, 0:16], 0.0, ["TTd"], 16)
    ms(T.BT[:, 0:16], 0.0, ["BTd"], 16)
    ms(T.C2[:, 0:16], 0.0, ["C2d"], 16)
    ms(T.C2[:, Z0:ZW], 0.0, ["C2z0", "C2z1"], 256)
    ac(T.ZC[:], T.ZI[:], AF.Identity, 0.0, 0.5, ["ZI0", "ZI1", "ZI2"], ["ZC"], 3 * LH)
    ts(PF[:, 7:8], PF[:, 3:4], -1.0, None, ALU.mult, None, ["ng"], ["pg16"], 1)
    ts(PF[:, 10:11], PF[:, 1:2], -16.0, None, ALU.mult, None, ["pf"], ["dg"], 1)
    ts(T.DG[:], T.IU[:, 0:128], PF[:, 0:1], PF[:, 10:11], ALU.is_equal, ALU.mult, ["IU", "pf", "dg"], ["DG"], 128)

    def swap(PX, src3, lo, nb, r, w, bank, narrow=False):
        lst = []
        for al in range(2):
            SW, c0 = (T.SH, 160 * al) if narrow else (T["SW%d" % al], 0)
            for ga in range(2):
                off = c0 + 16 - 16 * (ga - al)
                lst.append((PX[:, lo:lo + nb, 16 * al:16 * al + 16], SW[:, off:off + 128],
                            src3[:, :, 16 * ga:16 * ga + 16], ga == 0, ga == 1, 16 * nb, not narrow))
        mm(lst, r + ["SW0", "SW1", "SH0", "SH1"], w, [bank])

    cp(T.BF[:], T.BG[:], ["BG0", "BG1"], ["BF"], 384)
    swap(T.PX0, T.BF, 0, 12, ["BF"], ["Xb"], "PX0")
    op("dve", lambda: V.transpose(T.BY[:], T.PX0[:, 0:12, :]), ["Xb"], ["BY"], vc(384), ["PX0"])
    blk = []
    for a in range(12):
        cp(T.BL[:, :, a::12], T.BY[:, a::12, :], ["BY"], ["BL%d" % a], 32)
        blk.append("BL%d" % a)
    ttk = ["TTd"]
    for k in range(6):
        cs = slice(512 * k, 512 * (k + 1))
        cd = slice(16 + 512 * k, 16 + 512 * (k + 1))
        bk = ("PZ0", "PM0", "PZ1", "PM1")[k % 4]
        src = "PT%d" % (k // 3)
        ts(T.TT[:, cd], T.PT[:, cs], 255.0, -2.0 ** 60, ALU.is_ge, ALU.mult, [src], ["TT%d" % k], 512, 0.5)
        mm([(T[bk][:, 0:512], I_["one"], T.PT[:, cs], True, False, 512, False), (T[bk][:, 0:512], I_["one"], T.TT[:, cd], False, True, 512, False)],
           [src, "TT%d" % k, "Ione"], ["V" + bk], [bk])
        mv(CFG["tt"][k], T.TT[:, cd], T[bk][:, 0:512], ["V" + bk], ["TT%d" % k], 512, banks=[bk])
        ttk.append("TT%d" % k)
    btk, c2k = ["BTd"], ["C2d"]
    wc = NC_ // TB
    for k in range(TB):
        cd = slice(16 + wc * k, 16 + wc * (k + 1))
        lo, hi_ = wc * k // 16, wc * (k + 1) // 16
        body = T.TT[:, 16:Z0].indirect(T.BL[:, 0, lo:hi_])
        if CFG["bt"][k] == "a":
            ac(T.BT[:, cd], body, AF.Identity, 0.0, -1.0, ttk + blk, ["BT%d" % k], wc, G_)
        else:
            ts(T.BT[:, cd], body, -1.0, None, ALU.mult, None, ttk + blk, ["BT%d" % k], wc + 40, G_)
        mv(CFG["c2"][k], T.C2[:, cd], T.CL[:, 0:NS].indirect(T.BL[:, 1, lo:hi_]), ["CL0", "CL1"] + blk, ["C2%d" % k], wc, G_, bias=16.0)
        btk.append("BT%d" % k)
        c2k.append("C2%d" % k)
    c2k += ["C2z%d" % h for h in range(H)]

    def states():
        dma("sp", T.CL[0::16, 16:Z0], T.gs[:], ["CLx"], ["CL0", "CL1"], 98304)
        dma("sp", T.CL[0::16, Z0:ZW], T.s0[:], ["CLx"], ["GSb"], 8192)

    def half(h):
        S = str(h)
        b = lambda n: T[n + S]
        M, Tg, E, C16, KF, KT, MS, T1 = T.M, b("T"), b("E"), b("C16"), b("KF"), b("KT"), b("MS"), b("T1")
        TR, SC, GT, Q, XS, QJ, YT = b("TR"), b("SC"), b("GT"), b("Q"), b("XS"), b("QJ"), b("YT")
        RH, SB, SF, SU = b("RH"), b("SB"), b("SF"), b("SU")
        A3, B3, PS, PM, PZ, PX = b("A3"), b("B3"), b("PS"), b("PM"), b("PZ"), b("PX")
        col = lambda buf, i: buf[:, i * CA:(i + 1) * CA]
        k_ = lambda n: n + S
        p_, m1, ny = col(RH, 0), col(RH, 1), col(RH, 2)
        act, m_, nr, wz, xh, n1, wr, hi = [col(SB, i) for i in range(8)]
        xf, nh, none = [col(SF, i) for i in range(3)]
        bu, zu, xu = [col(SU, i) for i in range(3)]
        SI, K2 = b("SI"), b("K2")
        zi = col(SI, 3)
        lanes = slice(h * LH, (h + 1) * LH)
        bS, bM, bZ, bX = k_("PS"), k_("PM"), k_("PZ"), k_("PX")
        strip = lambda r, lo, n=1: PX[:, r, lo * CA:(lo + n) * CA]
        sW = strip(1, 0)

        def mixed(src, r, step=1):
            buf, c0 = (GT, 0) if step > 1 else (SI, 3 * CA)
            half_ = CA // 2
            op("dve", [(lambda al=al: V.tensor_copy(SU[:, CA + al:2 * CA:2], buf[:, c0 + step * half_ * al:c0 + step * half_ * (al + 1):step]))
                       for al in range(2)], [r], [k_("zu")], 2 * vc(CA))

        ms(Q[:, LH:LH + 8], 0.0, [k_("Qpad")], 8)
        ts(YT[:], T.C5[:], 0.0, None, ALU.mult, None, ["C5"], [k_("YT")], LH, 0.5)

        cp(A3[:], T.SR[:, lanes], ["SR", "SR0", "SR1", "SR2", "SR3"], [k_("A3")], LH)
        swap(PX, A3, 0, NB, [k_("A3")], [k_("X0")], bX)
        op("dve", lambda: V.transpose(GT[:], PX[:, 0:NB, :]), [k_("X0")], [k_("GT")], vc(LH), [bX])
        mixed(GT[:, 0::16], k_("GT"), 16)
        ts(B3[:], T.QI[:, lanes], PF[:, 7:8], None, ALU.add, None, ["QI", "pg16"], [k_("B3")], LH)
        op("dve", lambda: V.transpose(K2[:], B3[:]), [k_("B3")], [k_("K2")], vc(LH, 0.5))
        swap(PX, K2, NB, NB, [k_("K2")], [k_("X1")], bX, True)
        ac(p_, GT[:, 1::16], AF.Identity, 0.0, 16.0, [k_("GT")], [k_("p")], CA)
        ac(m1, GT[:, 2::16], AF.Identity, 16.0, -1.0, [k_("GT")], [k_("m1")], CA)
        ts(nr, GT[:, 3::16], 32.0, None, ALU.is_lt, None, [k_("GT")], [k_("nr")], CA)
        tt(wz, GT[:, 3::16], nr, ALU.mult, [k_("GT"), k_("nr")], [k_("wz")], CA)
        ts(zi, T.KEY[:, h * LH:(h + 1) * LH:16], PF[:, 3:4], float(Z0 - key0), ALU.add, ALU.add, ["KEY", "ng"], [k_("zi")], CA)
        tt(Q[:, 0:LH], T.RK[:], PX[:, NB:2 * NB, :], ALU.add, [k_("X1"), "RK"], [k_("Q")], LH, 1.0, [bX])

        def bcast(lo, hi_, r):
            zt = [k_("Z%d_" % q) for q in range(lo, hi_)]
            mm([(PZ[:, lo * LH:hi_ * LH], I_["sig"], T.ZC[:, lo * LH:hi_ * LH], True, False, (hi_ - lo) * LH, False)],
               ["Isig", "ZC"], zt, [bZ])
            mm([(PZ[:, lo * LH + j:hi_ * LH:16], I_["sig"], RH[:, lo * CA:hi_ * CA], False, j == 15, CA, False) for j in range(16)],
               r + ["Isig"], zt, [bZ])

        def select():
            op("dve", lambda: V.tensor_tensor_scan(XS[:], PZ[:, 0:LH], Q[:, 0:LH], 0.0, ALU.max, ALU.min),
               [k_("Z0_"), k_("Q")], [k_("XS")], vc(LH), [bZ])
            mv(CFG["xh"], xh, XS[:, 15::16], [k_("XS")], [k_("xh")], CA)
            tt(xf, XS[:, 15::16], xh, ALU.subtract, [k_("XS"), k_("xh")], [k_("xf")], CA)
            ts(xu, xf, PF[:, 3:4], None, ALU.add, None, [k_("xf"), "ng"], [k_("xu")], CA)

        def linear(terms, r, w, start, stop):
            mm([(strip(row, lo, n), I_[f], src, start and i == 0, stop and i == len(terms) - 1, n * CA, False)
                for i, (row, lo, n, f, src) in enumerate(terms)], r + ["I" + x[3] for x in terms], w, [bX])

        def ready(a_, at):
            terms = [(2, 0, 2, "one", T.CW[:, CA:3 * CA]), (2, 0, 1, "n496", m1), (2, 0, 1, "n32", p_), (2, 0, 1, "p16k", nr),
                     (2, 1, 1, "one", m1)]
            linear(terms, ["CW", k_("m1"), k_("p"), k_("nr")], [k_("Xd")], True, a_ is None)
            if a_ is not None:
                linear([(2, 0, 1, "p256", a_), (2, 1, 1, "neg", a_)], [at], [k_("Xd")], False, True)
            ts(SB[:, 0:2 * CA], strip(2, 0, 2), 16.0, 0.0, ALU.min, ALU.max, [k_("Xd")], [k_("act")], CA, banks=[bX])
            if CFG["nv"] == "act":
                ac(nh, act, AF.Identity, TOP + 69 * ULP, -65.0 / 16 * ULP, [k_("act")], [k_("nh")], CA)
            else:
                ts(nh, act, -65.0 / 16 * ULP, TOP + 69 * ULP, ALU.mult, ALU.add, [k_("act")], [k_("nh")], CA)
            tt(none, nh, zi, ALU.add, [k_("nh"), k_("zi")], [k_("nv")], CA)
            linear([(0, 0, 3, "one", T.CW[:, 3 * CA:6 * CA]), (0, 0, 2, "one", SB[:, 0:2 * CA]), (0, 0, 1, "one", p_),
                    (0, 2, 1, "neg", act), (0, 2, 1, "neg", p_)], ["CW", k_("act"), k_("p")], [k_("Xy")], True, False)

        bcast(0, 1, [k_("p")])
        select()
        ready(None, None)

        for t in range(STEPS):
            yield
            last = t == STEPS - 1
            dst = T.cores[(rank + 1 + t % (N - 1)) % N]
            rid, pid, _ = topo.addr(dst)
            engs = topo.engines(core, dst)
            mask = sum(1 << e for e in engs)
            neng = len(engs)
            first = FIRST if t == 0 and h == 0 else 0.0
            if t == 0:
                mv("v", C16[:], T.CL[:, 0:NS].indirect(zu), ["CL0", "CL1", k_("zu")], [k_("C16")], LH, G_, bias=16.0)
            else:
                mv("v", C16[:], T.C2[:, 0:ZW].indirect(zu), c2k + [k_("zu")], [k_("C16")], LH, G_)
            ts(KF[:], C16[:], -MID, None, ALU.add, None, [k_("C16")], [k_("KF")], LH, 0.5)
            if t == 0:
                own = Z0 + h * LH
                op("dve", [(lambda al=al: V.tensor_scalar(T.C2[:, own + 64 * al:own + 64 * al + 64], KF[:, :, 16 * al:16 * al + 16],
                                                          MID, None, ALU.add)) for al in range(2)], [k_("KF")], ["C2z" + S], 2 * vc(64))
            lc = LH // TCH
            tk = [k_("T%d_" % c) for c in range(TCH)]
            for c in range(TCH):
                who = "v" if c >= TCH - CFG["tdve"][H * t + h] else "a"
                mv(who, Tg[:, c, :], T.TT[:, 0:Z0].indirect(C16[:, lc * c:lc * (c + 1)]),
                   ttk + [k_("C16")], [tk[c]], 16 * lc, G_)
            op("dve", lambda: V.transpose(KT[:], KF[:]), [k_("KF")], [k_("KT")], vc(LH, 0.5))
            wend = NF if t == 0 else NF + 256 * (t - 1) + LH * (h + 1)
            rd = ["Mi", k_("xu")] + ["AM%d_%d" % (u, o) for u in range(t) for o in range(H) if u < t - 1 or o <= h]
            ac(MS[:], M[:, 0:wend].indirect(xu), AF.Abs, 0.0, 1.0, rd, [k_("MS")], LH, G_)
            mm([(PM[:, 0:LH], I_["one"], MS[:], True, True, LH, False)], [k_("MS"), "Ione"], [k_("PMv")], [bM])
            mm([(PS[:, 0:LH], T.L2[:], T.CN[:], True, False, LH, False)], ["L2", "CN"], [k_("S0")], [bS])
            parts = []

            def part(lst, r):
                parts.append(k_("Sp%d_" % len(parts)))
                mm(lst, r + [k_("S0")], [parts[-1]], [])

            for al in range(2):
                part([(PS[:, 64 * al:64 * al + 64], T.SH[:, 160 * al + 16 - 16 * (ga - al):160 * al + 144 - 16 * (ga - al)],
                       KT[:, :, 16 * ga:16 * ga + 16], False, False, LH // 2, False) for ga in range(2)], [k_("KT"), "SH0", "SH1"])
            ech, le = 2, LH // 2
            for e in range(ech):
                lo, hi_ = e * le, (e + 1) * le
                so = PS[:, lo:hi_]
                for c in range(4):
                    part([(so, T.BW[:, 159 - j:287 - j], Tg[:, :, 256 * e + 16 * j:256 * e + 16 * j + 16], False, False, le, False)
                          for j in range(4 * c, 4 * c + 4)], tk + ["BV"])
                et = []
                for c in range(4):
                    et.append(k_("E%d_%d_" % (e, c)))
                    op("dve", [(lambda k=k, lo=lo, hi_=hi_, e=e: V.tensor_tensor(
                        E[:, lo:hi_, k], Tg[:, :, 256 * e + k:256 * (e + 1):16], PM[:, lo:hi_], ALU.is_equal))
                               for k in range(4 * c, 4 * c + 4)], tk + [k_("PMv")], [et[c]], 4 * (vc(le) + CFG["ovh"]), [bM])
                for c in range(4):
                    end = e == ech - 1 and c == 3
                    lst = [(so, T.BW[:, 15 - j:143 - j], E[:, lo + j:hi_:16, :], False, end and j == 15, le, False)
                           for j in range(4 * c, 4 * c + 4)]
                    if end:
                        mm(lst, et + parts + ["BW"], [k_("S")], [bS])
                    else:
                        part(lst, et + ["BW"])
            op("dve", lambda: V.tensor_tensor_scan(SC[:], T.SEG[:], PS[:, 0:LH], 0.0, ALU.mult, ALU.max),
               [k_("S"), "SEG"], [k_("SC")], vc(LH), [bS])
            tt(col(SI, 0), SC[:, 15::16], nh, ALU.max, [k_("SC"), k_("nh")], [k_("cb")], CA)
            tt(col(SI, 1), SC[:, 15::16], none, ALU.max, [k_("SC"), k_("nv")], [k_("cz")], CA)
            ts(SI[:, 2 * CA:4 * CA], SI[:, 0:2 * CA], 4095, None, ALU.bitwise_and, None, [k_("cb"), k_("cz")], [k_("zi")], CA)
            if last:
                cp(SU[:, 0:2 * CA], SI[:, 2 * CA:4 * CA], [k_("zi")], [k_("zu"), k_("bu")], CA)
            else:
                cp(bu, col(SI, 2), [k_("zi")], [k_("bu")], CA)
                mixed(zi, k_("zi"))
            if CFG["hi"] == "act":
                mv("a", SB[:, 7 * CA:9 * CA], SI[:, 0:CA].indirect(T.LS[:, 0:1]), [k_("cb"), "LS"], [k_("hi")], 2 * CA, G_)
            else:
                tt(hi, SC[:, 15::16], nh, ALU.max, [k_("SC"), k_("nh")], [k_("hi")], CA)
            fc = slice((t * H + h) * CA, (t * H + h + 1) * CA)
            f_, a_ = T.FS[:, fc], T.FR[:, fc]
            ft = k_("f%d_" % t)
            tt(f_, SC[:, 15::16], nh, ALU.is_gt, [k_("SC"), k_("nh")], [ft], CA)
            op("pool", lambda f_=f_, a_=a_, t=t, pid=pid, rid=rid, mask=mask: g.remote_dma(
                a_, f_, T.sem["af%d_%d" % (t, h)], T.sem.left, pid, rid, mask),
               [ft], [k_("AF%d_" % t)], 300.0 + first, kind="r", lat=2000.0 * RL, sem=("af%d_%d" % (t, h), neng))
            oc = slice(256 * t + h * LH, 256 * t + (h + 1) * LH)
            ot = k_("O%d_" % t)
            sent, st = (T1[:], k_("T1")) if last else (T.OUT[:, oc], ot)
            if CFG["om"][t] == "v":
                tt(sent, T.BT[:, 0:Z0].indirect(bu), MS[:], ALU.min, btk + [k_("bu"), k_("MS")], [st], LH + 40, max(G_, CFG["fg"]))
            else:
                mv("a", TR[:], T.BT[:, 0:Z0].indirect(bu), btk + [k_("bu")], [k_("TR")], LH, G_)
                tt(sent, TR[:], PM[:, 0:LH], ALU.min, [k_("TR"), k_("PMv")], [st], LH, 1.0, [bM])
            if last:
                ac(T.OUT[:, oc], sent, AF.Abs, 0.0, 1.0, [st], [ot], LH)
            land = M[:, NF + oc.start:NF + oc.stop]
            op("pool", lambda land=land, oc=oc, t=t, pid=pid, rid=rid, mask=mask: g.remote_dma(
                land, T.OUT[:, oc], T.sem["am%d_%d" % (t, h)], T.sem.left, pid, rid, mask),
               [ot], [k_("AM%d_" % t)], 300.0, kind="r", lat=2300.0 * RL, sem=("am%d_%d" % (t, h), neng))
            linear([(0, 0, 1, "n512", f_), (0, 1, 1, "one", f_), (0, 2, 1, "p512", f_)], [ft], [k_("Xy")], False, True)
            if CFG["ync"] == "act":
                ac(RH[:], strip(0, 0, 3), AF.Relu, 0.0, 1.0, [k_("Xy")], [k_("p"), k_("m1"), k_("ny")], CA, banks=[bX])
            else:
                ts(RH[:], strip(0, 0, 3), 0.0, None, ALU.max, None, [k_("Xy")], [k_("p"), k_("m1"), k_("ny")], CA, banks=[bX])
            bcast(1 if last else 0, 3, [k_("p"), k_("m1"), k_("ny")])
            z2 = PZ[:, 2 * LH:3 * LH]
            tt(z2, z2, Q[:, 1:LH + 1], ALU.min, [k_("Z2_"), k_("Q"), k_("Qpad")], [k_("Z2_")], LH, 1.0, [bZ])
            tt(PZ[:, LH:2 * LH], PZ[:, LH:2 * LH], T.KEY[:, oc], ALU.min, [k_("Z1_"), "KEY"], [k_("Z1_")], LH, 1.0, [bZ])
            tt(Q[:, 0:LH], Q[:, 0:LH], z2, ALU.max, [k_("Z2_"), k_("Q")], [k_("Q")], LH, 1.0, [bZ])
            tt(Q[:, 0:LH], Q[:, 0:LH], PZ[:, LH:2 * LH], ALU.max, [k_("Z1_"), k_("Q")], [k_("Q")], LH, 1.0, [bZ])
            if not last:
                select()
            linear([(1, 0, 1, "one", T.CW[:, 0:CA]), (1, 0, 1, "one", wz), (1, 0, 1, "hi", hi)], ["CW", k_("wz"), k_("hi")], [k_("Xw")], True, True)
            if last:
                ac(wr, sW, AF.Identity, 127.75, 1.0, [k_("Xw")], [k_("wr")], CA, banks=[bX])
                ts(YT[:, 3::16], wr, -128.0, None, ALU.add, None, [k_("wr"), k_("YT")], [k_("Y3")], CA)
                ts(YT[:, 1::16], p_, 1.0 / 16, None, ALU.mult, None, [k_("p"), k_("YT")], [k_("Y1")], CA)
                ac(n1, m1, AF.Identity, 16.0, -1.0, [k_("m1")], [k_("n1")], CA)
                mv(CFG["gs"], T.YG[:, lanes], T.CL[:, 0:ZW].indirect(zu), ["CL0", "CL1", "GSb", k_("zu")], [k_("YG")], LH, G_)
            else:
                ts(nr, sW, 32.0, None, ALU.is_lt, None, [k_("Xw")], [k_("nr")], CA, banks=[bX])
                tt(wz, nr, sW, ALU.mult, [k_("Xw"), k_("nr")], [k_("wz")], CA, 1.0, [bX])
                ready(a_, k_("AF%d_" % t))

        gm = ["GM%d" % j for j in range(4)]
        mm([(PS[:, 0:LH], T.DG[:], T.C5[:], True, False, LH, False)], ["DG", "C5"], [k_("S0")], [bS])
        mm([(PS[:, j:LH:16], T.GM[:, 128 * j:128 * (j + 1)], n1, False, False, CA, False) for j in range(16)],
           [k_("n1"), k_("S0")] + gm, [k_("S1")], [bS])
        mm([(PS[:, j:LH:16], T.GM[:, 128 * j:128 * (j + 1)], a_, False, j == 15, CA, False) for j in range(16)],
           [k_("AF%d_" % t), k_("S1")] + gm, [k_("S")], [bS])
        op("dve", lambda: V.transpose(KT[:], YT[:]), [k_("Y1"), k_("Y3")], [k_("KT")], vc(LH, 0.5))
        swap(PX, KT, 0, NB, [k_("KT")], [k_("X0")], bX, True)
        ac(T.YS[:, lanes], PX[:, 0:NB, :], AF.Identity, 0.0, 1.0, [k_("X0")], [k_("YS")], LH, banks=[bX])
        cp(QJ[:], Q[:, 0:LH], [k_("Q")], [k_("QJ")], LH)
        ts(QJ[:], QJ[:], 4095, None, ALU.bitwise_and, None, [k_("QJ")], [k_("QJ")], LH)
        ts(KF[:], QJ[:], PF[:, 3:4], -MID, ALU.add, ALU.add, [k_("QJ"), "ng"], [k_("KF")], LH)
        op("dve", lambda: V.transpose(K2[:], KF[:]), [k_("KF")], [k_("K2")], vc(LH, 0.5))
        swap(PX, K2, NB, NB, [k_("K2")], [k_("X1")], bX, True)
        ac(TR[:], PX[:, NB:2 * NB, :], AF.Identity, MID, 1.0, [k_("X1")], [k_("TR")], LH, banks=[bX])
        tt(XS[:], TR[:], PS[:, 0:LH], ALU.min, [k_("TR"), k_("S")], [k_("XS")], LH, 1.0, [bS])
        ts(T.YQ[:, lanes], XS[:], 0.0, None, ALU.max, None, [k_("XS")], [k_("YQ")], LH)
        ts(T.YN[:, lanes], PS[:, 0:LH], 2.0 ** -13, 16.0, ALU.mult, ALU.min, [k_("S")], [k_("YN")], LH, banks=[bS])
        dma("act" if h else "sp", T.yq[:, lanes], T.YQ[:, lanes], [k_("YQ")], [k_("yq")], 65536)

    runs = [half(h) for h in range(H)]
    for turn in range(STEPS + 1):
        if turn == 2:
            states()
        for h, r in enumerate(runs):
            n0 = len(ops)
            next(r, None)
            for o in ops[n0:]:
                o["half"] = h
    arr = ["AM%d_%d" % (t, h) for t in range(STEPS) for h in range(H)]
    e3 = 256 * (STEPS - 1)
    for t in range(STEPS - 1):
        ac(T.MN[:, 256 * t:256 * (t + 1)], T.M[:, NF + 256 * t:NF + 256 * (t + 1)], AF.Abs, 0.0, 1.0, arr[H * t:H * (t + 1)], ["MN%d" % t], 256)
    dma("sp", T.mn[:, 0:e3], T.MN[:], ["MN%d" % t for t in range(STEPS - 1)], ["mn"], 262144)
    for h in range(H):
        dma("sp", T.mn[:, e3 + h * LH:e3 + (h + 1) * LH], T.M[:, NF + e3 + h * LH:NF + e3 + (h + 1) * LH], [arr[h - H]], ["mn%d" % h], 32768)
    for x, n in enumerate(("YG", "YS", "YN", "YS")):
        dma("act" if x % 2 else "sp", T.ys[:, 256 * x:256 * (x + 1)], T[n][(x if n == "YS" else 0)::16, :],
            [n + str(h) for h in range(H)], ["ys%d" % x], 8192)
    return ops


def link(ops):
    lastw, readers, bank = {}, {}, {}
    for i, o in enumerate(ops):
        hard, soft = set(), set()
        for r in o["r"]:
            if r in lastw:
                hard.add(lastw[r])
        for w in o["w"]:
            if w in lastw:
                (soft if w == "pool_order" else hard).add(lastw[w])
            hard.update(readers.get(w, []))
        for bk in o["banks"]:
            for e, j in bank.get(bk, {}).items():
                (soft if e == o["eng"] else hard).add(j)
        if o["eng"] == "pe":
            own = set(j for j in hard if ops[j]["eng"] == "pe")
            hard -= own
            soft |= own
        hard.discard(i)
        soft.discard(i)
        o["hard"], o["soft"] = hard, soft - hard
        for r in o["r"]:
            readers.setdefault(r, []).append(i)
        for w in o["w"]:
            lastw[w] = i
            readers[w] = []
        for bk in o["banks"]:
            bank.setdefault(bk, {})[o["eng"]] = i


def schedule(eng, cost, succ, npred, rdy0, tail, prio):
    n = len(eng)
    wait, gap = CFG["wait"], CFG["gap"]
    left = list(npred)
    rdy = list(rdy0)
    free = [0.0] * 5
    pend = [[] for _ in range(5)]
    for i in range(n):
        if left[i] == 0:
            pend[eng[i]].append(i)
    out, start, end = [], [0.0] * n, 0.0
    for _ in range(n):
        t0, e = 1e18, 0
        for q in range(5):
            if pend[q]:
                t = min([rdy[i] for i in pend[q]])
                if t < free[q]:
                    t = free[q]
                if t < t0:
                    t0, e = t, q
        i, bp = -1, -1e18
        for j in pend[e]:
            if rdy[j] <= t0 and prio[j] > bp:
                i, bp = j, prio[j]
        soon = t0 + wait * cost[i]
        bp += gap
        for j in pend[e]:
            if rdy[j] < soon and prio[j] > bp:
                i, bp = j, prio[j]
        if rdy[i] > t0:
            t0 = rdy[i]
        pend[e].remove(i)
        fin = t0 + cost[i]
        start[i] = t0
        free[e] = fin
        if fin + tail[i] > end:
            end = fin + tail[i]
        out.append(i)
        for j, d in succ[i]:
            if fin + d > rdy[j]:
                rdy[j] = fin + d
            left[j] -= 1
            if left[j] == 0:
                pend[eng[j]].append(j)
    return out, start, end


def replay(seq, eng, cost, lat, pred):
    fin, start, free, end = [0.0] * len(seq), [0.0] * len(seq), [0.0] * 5, 0.0
    for i in seq:
        t = free[eng[i]]
        for j, d in pred[i]:
            if fin[j] + d > t:
                t = fin[j] + d
        start[i] = t
        t += cost[i]
        fin[i] = t
        free[eng[i]] = t
        if t + lat[i] > end:
            end = t + lat[i]
    return start, end


def order(ops, variants):
    n = len(ops)
    names = ["pe", "dve", "act", "pool", "sp"]
    eng = [names.index(o["eng"]) for o in ops]
    sets = []
    for v, plan in zip(variants, PLANS):
        cost, lat = [o["cost"] for o in v], [o["lat"] for o in v]
        succ, pred = [[] for _ in range(n)], [[] for _ in range(n)]
        for i, o in enumerate(ops):
            for j in sorted(o["hard"]):
                succ[j].append((i, lat[j] + plan[3]))
                pred[i].append((j, lat[j] + plan[3]))
            for j in sorted(o["soft"]):
                succ[j].append((i, 0.0))
                pred[i].append((j, 0.0))
        sets.append((cost, lat, succ, pred))
    np_, ns_, zero = [len(p) for p in sets[0][3]], [len(s) for s in sets[0][2]], [0.0] * n
    scale = [sum(s[0]) for s in sets]

    def judge(seq):
        runs = [replay(seq, eng, s[0], s[1], s[3]) for s in sets]
        return seq, runs, sum(r[1] * scale[0] / c for r, c in zip(runs, scale)) / len(sets)

    cost, lat, succ, pred = sets[0]
    prio = [0.0] * n
    for i in range(n - 1, -1, -1):
        prio[i] = cost[i] + max([prio[j] + d for j, d in succ[i]] + [lat[i]])
    rng = np.random.default_rng(CFG["seed"])
    best = judge(schedule(eng, cost, succ, np_, zero, lat, [prio[i] - CFG["bias"] * ops[i]["half"] for i in range(n)])[0])
    cur = best
    for k in range(CFG["tries"]):
        m = k % len(sets)
        cost, lat, succ, pred = sets[m]
        noise = (rng.normal(0.0, CFG["noise"], n) * (rng.random(n) < CFG["share"])).tolist()
        back = schedule(eng, cost, pred, ns_, lat, zero, [cur[1][m][0][i] + cost[i] + noise[i] for i in range(n)])
        got = judge(schedule(eng, cost, succ, np_, zero, lat, [back[1][i] + cost[i] for i in range(n)])[0])
        if got[2] <= cur[2] + CFG["temp"] * (1.0 - k / CFG["tries"]) * rng.exponential():
            cur = got
            if got[2] < best[2]:
                best = got
    return judge(polish(best[0], eng, sets, [scale[0] / c / len(sets) for c in scale], rng))


def polish(seq, eng, sets, weight, rng):
    n = len(seq)
    need = [set(j for j, _ in p) for p in sets[0][3]]

    def run(seq, lo, fins):
        out, total = [], 0.0
        for (cost, lat, _, pred), fin0, w in zip(sets, fins, weight):
            fin = list(fin0)
            free, end = [0.0] * 5, 0.0
            for i in seq[:lo]:
                free[eng[i]] = fin[i]
            for i in seq[lo:]:
                t = free[eng[i]]
                for j, d in pred[i]:
                    if fin[j] + d > t:
                        t = fin[j] + d
                t += cost[i]
                fin[i] = t
                free[eng[i]] = t
            for i in ends:
                if fin[i] + lat[i] > end:
                    end = fin[i] + lat[i]
            out.append(fin)
            total += w * end
        return out, total

    ends = [i for i in range(n) if not sets[0][2][i]]
    fins, cur = run(seq, 0, [[0.0] * n for _ in sets])
    best, bseq = cur, seq
    steps = CFG["polish"]
    pick = rng.random((steps, 4)).tolist()
    arcs = None
    for k in range(steps):
        r = pick[k]
        if arcs is None:
            pos, before, last = [0] * n, [-1] * n, [-1] * 5
            for p, i in enumerate(seq):
                pos[i] = p
                before[i] = last[eng[i]]
                last[eng[i]] = i
            arcs = []
            for (cost, lat, _, pred), fin in zip(sets, fins):
                i = max(ends, key=lambda i: fin[i] + lat[i])
                while i >= 0:
                    t, nxt = fin[i] - cost[i] - 1e-6, -1
                    for j, d in pred[i]:
                        if fin[j] + d >= t:
                            nxt = j
                    if nxt < 0 and before[i] >= 0 and fin[before[i]] >= t:
                        nxt = before[i]
                        arcs.append(i)
                    i = nxt
            if not arcs:
                break
        v = arcs[int(r[0] * len(arcs))]
        u = before[v]
        for _ in range(int(r[1] ** 3 * CFG["reach"])):
            if before[u] >= 0:
                u = before[u]
        lo, hi = pos[u], pos[v]
        ahead, want, seen, ok = [], set(need[v]), set(), True
        for p in range(hi - 1, lo - 1, -1):
            i = seq[p]
            if i in want or eng[i] in seen:
                if i == u:
                    ok = False
                    break
                ahead.append(i)
                want |= need[i]
                seen.add(eng[i])
        if not ok:
            continue
        moved = set(ahead)
        new = seq[:lo] + ahead[::-1] + [v] + [i for i in seq[lo:hi] if i not in moved] + seq[hi + 1:]
        nf, val = run(new, lo, fins)
        if val <= cur - CFG["heat"] * (1.0 - k / steps) * np.log(r[2] + 1e-12):
            seq, fins, cur, arcs = new, nf, val, None
            if cur < best:
                best, bseq = cur, seq
    return bseq


ORDER = {}


def rank_program(g, core, T, topo):
    rank = T.rank_of(core)
    if rank is None:
        return
    ops = plan_ops(g, T, topo, core, rank)
    link(ops)
    if "seq" not in ORDER:
        ORDER["seq"] = order(ops, [plan_ops(g, T, topo, core, rank, m) for m in range(len(PLANS))])[0]
    queue = {"pe": g.tensor, "dve": g.vector, "act": g.scalar, "pool": g, "sp": g.sync}
    count = {"pe": 0, "dve": 0, "act": 0, "pool": 0}
    seen = dict((e, {}) for e in queue)
    dmas = []
    left = 0
    for i in ORDER["seq"]:
        o = ops[i]
        e = o["eng"]
        need = {}
        for j in o["hard"]:
            s, v = ops[j]["done"]
            need[s] = max(need.get(s, 0), v)
        for s in sorted(need):
            if seen[e].get(s, 0) < need[s]:
                queue[e].wait_ge(T.sem[s], need[s])
                seen[e][s] = need[s]
        if o["kind"] == "c":
            for c in o["calls"]:
                c().then_inc(T.sem[e], 1)
                count[e] += 1
            o["done"] = (e, count[e])
        elif o["kind"] == "d":
            s = "d%d" % len(dmas)
            o["calls"][0]().then_inc(T.sem[s], 16)
            dmas.append(s)
            o["done"] = (s, 16)
        else:
            o["calls"][0]()
            o["done"] = o["sem"]
            left += o["sem"][1]
    g.wait_ge(T.sem.left, left)
    for e in count:
        g.sync.wait_ge(T.sem[e], count[e])
    for s in dmas:
        if not any(seen[e].get(s, 0) for e in seen):
            g.sync.wait_ge(T.sem[s], 16)
